import numpy as np
import ml_dtypes


def mxq(x, axis, fmt="e4m3"):
    dtype, down = {"e4m3": (ml_dtypes.float8_e4m3fn, 7), "e5m2": (ml_dtypes.float8_e5m2, 14)}[fmt]
    v = np.moveaxis(np.asarray(x, np.float32).astype(ml_dtypes.bfloat16).astype(np.float64), axis, -1)
    blocks = v.reshape(v.shape[:-1] + (-1, 32))
    amax = np.abs(blocks).max(-1, keepdims=True)
    byte = np.maximum(np.where(amax > 0, np.frexp(amax)[1] - 1 + 127, 0) - down, 1)
    scale = np.exp2(byte - 127.0)
    codes = (blocks / scale).astype(np.float32).astype(dtype).astype(np.float64)
    return np.moveaxis((codes * scale).reshape(v.shape), -1, axis)


WIDE = False


def mx_kscale(k):
    if not WIDE:
        return np.ones(k)
    levels = np.array([10, -10, 5, -5, 0])
    if k % 512:
        return np.exp2(np.random.permutation(np.resize(levels, k // 32))).repeat(32)
    a = np.empty((k // 512, 16))
    for p in range(k // 512):
        a[p, :8] = np.random.permutation(np.resize(levels, 8))
        for g in range(8):
            far = levels[np.abs(levels - a[p, g]) >= 10]
            a[p, g + 8] = far[np.random.randint(len(far))]
    return np.exp2(a.ravel()).repeat(32)


BF16 = ml_dtypes.bfloat16


def bf(x):
    return np.asarray(x, np.float32).astype(BF16)


def f64(x):
    return np.asarray(x).astype(np.float64)


N1, N2, J1, J2 = 1024, 2048, 1024, 512


def draw0():
    s, t = mx_kscale(J2), mx_kscale(J1)
    k1 = np.random.standard_normal((N1, J1)) / np.sqrt(J1) / t
    dist = np.random.standard_normal((J1, J2)) * s
    k2 = np.random.standard_normal((N2, J2)) / np.sqrt(J2) / s
    pol = np.random.uniform(0.5, 1.0, J1) * t
    data = np.random.standard_normal((N1, N2))
    wt = np.random.uniform(0.5, 1.5, N2)
    return {"k1": bf(k1), "dist": bf(dist), "k2": bf(k2),
            "pol": bf(pol), "data": bf(data), "wt": bf(wt)}


def core(k1, dist, k2, pol, data, wt):
    fq = mxq(f64(dist), 1, "e4m3")
    k2q = mxq(f64(k2), 1, "e4m3")
    g = fq @ k2q.T
    h = g * f64(pol)[:, None]
    k1q = mxq(f64(k1), 1, "e4m3")
    hq = mxq(h, 0, "e4m3")
    signal = k1q @ hq
    return (signal - f64(data)) * f64(wt)[None, :]


def e4m3fn_bytes(y):
    return np.clip(np.asarray(y, np.float64), -448.0, 448.0).astype(np.float32).astype(ml_dtypes.float8_e4m3fn).view(np.uint8)


def e4m3fn_values(b):
    return np.asarray(b, np.uint8).view(ml_dtypes.float8_e4m3fn).astype(np.float64)


def setup_inputs():
    d = draw0()
    x0 = np.asarray(d['k2']).astype(np.float64)
    s = (np.max(np.abs(x0), axis=(0,), keepdims=True) / 448.0).astype(np.float32)
    out = {}
    for k, v in d.items():
        if k == 'k2':
            out['k2_bytes'] = e4m3fn_bytes(x0 / s.astype(np.float64))
            out['k2_scale'] = s
        else:
            out[k] = v
    return out


def reference(k1, dist, k2_bytes, k2_scale, pol, data, wt):
    return core(k1, dist, e4m3fn_values(k2_bytes) * k2_scale.astype(np.float64), pol, data, wt)

@@ -1,0 +1,300 @@
+from contextlib import ExitStack
+
+import concourse.mybir as mybir
+from concourse.masks import make_identity
+
+N1, N2, J1, J2 = 1024, 2048, 1024, 512
+FLOPS = 2 * J1 * N2 * J2 + 2 * N1 * N2 * J1
+
+F32 = mybir.dt.float32
+BF16 = mybir.dt.bfloat16
+U32 = mybir.dt.uint32
+U8 = mybir.dt.uint8
+FP8 = mybir.dt.float8_e4m3fn
+FP8X4 = mybir.dt.float8_e4m3fn_x4
+MULT = mybir.AluOpType.mult
+SUB = mybir.AluOpType.subtract
+COPY = mybir.ActivationFunctionType.Copy
+
+P = 128
+NB = 512
+BLOCKS = N2 // NB
+ITILES = N1 // P
+GROUPS = J1 // 512
+
+
+def tile_nmr_relaxometry_residual_s7_kernel(tc, k1, dist, k2_bytes, k2_scale, pol, data, wt, out):
+    nc = tc.nc
+    with ExitStack() as ctx:
+        keep = ctx.enter_context(tc.tile_pool(name="keep", bufs=1))
+        wide = ctx.enter_context(tc.tile_pool(name="wide", bufs=2))
+        hpool = ctx.enter_context(tc.tile_pool(name="hpool", bufs=3))
+        hcpool = ctx.enter_context(tc.tile_pool(name="hcpool", bufs=4))
+        opool = ctx.enter_context(tc.tile_pool(name="opool", bufs=8))
+        ps_tr = ctx.enter_context(tc.psum_pool(name="ps_tr", bufs=2))
+        ps_g = ctx.enter_context(tc.psum_pool(name="ps_g", bufs=3))
+        ps_s = ctx.enter_context(tc.psum_pool(name="ps_s", bufs=3))
+
+        ident = keep.tile([P, P], F32, name="ident")
+        make_identity(nc, ident[:])
+
+        ks = keep.tile([P, 4], F32, name="ks")
+        nc.sync.dma_start(out=ks[:], in_=k2_scale.rearrange("o (p c) -> p (o c)", c=4))
+        kbytes, dsb, k1sb, dat = {}, {}, {}, {}
+        wt_bc = keep.tile([P, N2], BF16, name="wt_bc")
+        polb = keep.tile([P, 8], BF16, name="polb")
+        polf = keep.tile([P, 8], F32, name="polf")
+
+        def load_k2(b):
+            kbytes[b] = keep.tile([P, 4, J2], U8, name="kbytes%d" % b)
+            nc.sync.dma_start(out=kbytes[b][:], in_=k2_bytes[b * NB : (b + 1) * NB, :].rearrange("(r p) l -> p r l", p=P))
+
+        def load_dist(g):
+            dsb[g] = keep.tile([P, 4 * J2], BF16, name="dsb%d" % g)
+            nc.sync.dma_start(out=dsb[g][:], in_=dist[g * 512 : (g + 1) * 512, :].rearrange("(p t) l -> p (t l)", t=4))
+
+        def load_k1(i):
+            k1sb[i] = keep.tile([P, J1], BF16, name="k1sb%d" % i)
+            nc.sync.dma_start(out=k1sb[i][:], in_=k1[i * P : (i + 1) * P, :])
+
+        def load_data(b, h):
+            dat[b, h] = keep.tile([P, 4, NB], BF16, name="dat%d_%d" % (b, h))
+            nc.sync.dma_start(
+                out=dat[b, h][:],
+                in_=data[h * 512 : (h + 1) * 512, b * NB : (b + 1) * NB].rearrange("(i p) m -> p i m", p=P),
+            )
+
+        def load_wt(b):
+            nc.sync.dma_start(out=wt_bc[:, b * NB : (b + 1) * NB], in_=wt[b * NB : (b + 1) * NB].partition_broadcast(P))
+
+        load_k2(0)
+        load_dist(0)
+        load_dist(1)
+        nc.sync.dma_start(out=polb[:].rearrange("p (g t) -> p g t", t=4), in_=pol.rearrange("(g p t) -> p g t", p=P, t=4))
+        load_k2(1)
+        load_k1(0)
+        load_k1(1)
+        load_k2(2)
+        load_k1(2)
+        load_k1(3)
+        load_data(0, 0)
+        load_wt(0)
+        load_k1(4)
+        load_k1(5)
+        load_data(0, 1)
+        load_k1(6)
+        load_k1(7)
+        load_k2(3)
+        for b in range(1, BLOCKS):
+            load_wt(b)
+            load_data(b, 0)
+            load_data(b, 1)
+
+        psum, k2w, kg, kcodes, kscales = {}, {}, {}, {}, {}
+        dg, dcodes, dscales, k1g, k1codes, k1scales = {}, {}, {}, {}, {}, {}
+        hp, hi, hcodes, hscales, res = {}, {}, {}, {}, {}
+        scale_bc = keep.tile([P, J2], F32, name="scale_bc")
+
+        def evict_words(eng, dst, src):
+            if eng == "S":
+                nc.scalar.copy(out=dst, in_=src)
+            else:
+                nc.vector.tensor_copy(out=dst, in_=src)
+
+        def scale_bcast():
+            ps = ps_tr.tile([P, 4, P], F32, name="tr")
+            for c in range(4):
+                nc.tensor.transpose(ps[:, c, :], ks[:, c : c + 1].to_broadcast([P, P]), ident[:])
+            nc.vector.tensor_copy(out=scale_bc[:].rearrange("p (n c) -> p n c", c=4), in_=ps[:].rearrange("p c n -> p n c"))
+
+        def widen(b, r):
+            if r == 0:
+                k2w[b] = wide.tile([P, 4, J2], BF16, name="k2w")
+            nc.vector.tensor_tensor(out=k2w[b][:, r, :], in0=kbytes[b][:, r, :].bitcast(FP8), in1=scale_bc[:], op=MULT)
+
+        def widen_sg(b):
+            raw = wide.tile([P, 4, J2], BF16, name="k2raw")
+            nc.scalar.copy(out=raw[:].rearrange("p r l -> p (r l)"), in_=kbytes[b][:].rearrange("p r l -> p (r l)").bitcast(FP8))
+            k2w[b] = wide.tile([P, 4, J2], BF16, name="k2w")
+            for r in range(4):
+                nc.gpsimd.tensor_tensor(out=k2w[b][:, r, :], in0=raw[:, r, :], in1=scale_bc[:], op=MULT)
+
+        def pair_transposes(key, words, offs):
+            ps = ps_tr.tile([P, 2, 2, P], F32, name="tr")
+            psum[key] = ps
+            for a, off in enumerate(offs):
+                for u in (0, 1):
+                    nc.tensor.transpose(ps[:, a, u, :], words[:, off + u : off + 256 : 2], ident[:])
+
+        def tr_k2(b, h):
+            words = k2w[b][:].rearrange("p r l -> p (r l)").bitcast(F32)
+            pair_transposes(("k2", b, h), words, (512 * h, 512 * h + 256))
+
+        def ev_k2(b, h, eng):
+            if h == 0:
+                kg[b] = wide.tile([P, 4, P, 4], BF16, name="kg", align_bytes=64)
+            dst = kg[b][:].rearrange("p r m e -> p (r m e)").bitcast(F32).rearrange("p (r m u) -> p r m u", r=4, u=2)
+            evict_words(eng, dst[:, 2 * h : 2 * h + 2], psum["k2", b, h][:].rearrange("p a u r -> p a r u"))
+
+        def q_k2(b):
+            kcodes[b] = wide.tile([P, NB], U32, name="kcodes", align_bytes=64)
+            kscales[b] = wide.tile([P, NB], U8, name="kscales", align_bytes=64)
+            nc.vector.quantize_mx(out=kcodes[b][:].bitcast(FP8X4), scales=kscales[b][:], in_=kg[b][:].rearrange("p r m e -> p (r m e)"))
+
+        def tr_d(g, h):
+            pair_transposes(("d", g, h), dsb[g][:].bitcast(F32), (512 * h, 512 * h + 256))
+
+        def ev_d(g, h, eng):
+            if h == 0:
+                dg[g] = keep.tile([P, 4, P, 4], BF16, name="dg%d" % g, align_bytes=64)
+            dst = dg[g][:].rearrange("p r m e -> p (r m e)").bitcast(F32).rearrange("p (r m u) -> p r m u", r=4, u=2)
+            evict_words(eng, dst[:, 2 * h : 2 * h + 2], psum["d", g, h][:].rearrange("p a u r -> p a r u"))
+
+        def q_d(g):
+            dcodes[g] = keep.tile([P, 512], U32, name="dcodes%d" % g, align_bytes=64)
+            dscales[g] = keep.tile([P, 512], U8, name="dscales%d" % g, align_bytes=64)
+            nc.vector.quantize_mx(out=dcodes[g][:].bitcast(FP8X4), scales=dscales[g][:], in_=dg[g][:].rearrange("p r m e -> p (r m e)"))
+
+        def tr_k1(i):
+            pair_transposes(("k1", i), k1sb[i][:].bitcast(F32), (0, 256))
+
+        def ev_k1(i, eng):
+            k1g[i] = keep.tile([P, 2, P, 4], BF16, name="k1g%d" % i, align_bytes=64)
+            dst = k1g[i][:].rearrange("p g m e -> p (g m e)").bitcast(F32).rearrange("p (g m u) -> p g m u", g=2, u=2)
+            evict_words(eng, dst, psum["k1", i][:].rearrange("p g u r -> p g r u"))
+
+        def q_k1(i):
+            k1codes[i] = keep.tile([P, 256], U32, name="k1codes%d" % i, align_bytes=64)
+            k1scales[i] = keep.tile([P, 256], U8, name="k1scales%d" % i, align_bytes=64)
+            nc.vector.quantize_mx(out=k1codes[i][:].bitcast(FP8X4), scales=k1scales[i][:], in_=k1g[i][:].rearrange("p g m e -> p (g m e)"))
+
+        def mm1(b, g, t):
+            ps = ps_g.tile([P, NB], F32, name="g_ps")
+            psum["g", b, g, t] = ps
+            cols = slice(t * P, (t + 1) * P)
+            nc.tensor.matmul_mx(
+                out=ps[:],
+                lhsT=dcodes[g][:, cols].bitcast(FP8X4),
+                lhsT_scale=dscales[g][:, cols],
+                rhs=kcodes[b][:].bitcast(FP8X4),
+                rhs_scale=kscales[b][:],
+                start=True,
+                stop=True,
+            )
+
+        def ev_g(b, g, t, eng):
+            if t == 0:
+                hp[b, g] = hpool.tile([P, 4, NB], BF16, name="hp", align_bytes=64)
+            dst = hp[b, g][:, t, :]
+            src = psum["g", b, g, t][:]
+            col = polf[:, 4 * g + t : 4 * g + t + 1]
+            if eng == "S":
+                nc.scalar.activation(out=dst, in_=src, func=COPY, scale=col)
+            else:
+                nc.vector.tensor_scalar(out=dst, in0=src, scalar1=col, scalar2=None, op0=MULT)
+
+        def inter(b, g, half, eng):
+            if half == 0:
+                hi[b, g] = hpool.tile([P, NB, 4], BF16, name="hi", align_bytes=64)
+            cols = slice(half * 256, half * 256 + 256)
+            dst = hi[b, g][:, cols, :].rearrange("p (c i) t -> p c t i", i=4)
+            src = hp[b, g][:, :, cols].rearrange("p t (c i) -> p c t i", i=4)
+            evict_words(eng, dst, src)
+
+        def q_h(b, g):
+            hcodes[b, g] = hcpool.tile([P, NB], U32, name="hcodes", align_bytes=64)
+            hscales[b, g] = hcpool.tile([P, NB], U8, name="hscales", align_bytes=64)
+            nc.vector.quantize_mx(
+                out=hcodes[b, g][:].bitcast(FP8X4), scales=hscales[b, g][:], in_=hi[b, g][:].rearrange("p n t -> p (n t)")
+            )
+
+        def mm2(b, i):
+            ps = ps_s.tile([P, NB], F32, name="s_ps")
+            psum["s", b, i] = ps
+            for g in range(GROUPS):
+                cols = slice(g * P, (g + 1) * P)
+                nc.tensor.matmul_mx(
+                    out=ps[:],
+                    lhsT=k1codes[i][:, cols].bitcast(FP8X4),
+                    lhsT_scale=k1scales[i][:, cols],
+                    rhs=hcodes[b, g][:].bitcast(FP8X4),
+                    rhs_scale=hscales[b, g][:],
+                    start=(g == 0),
+                    stop=(g == GROUPS - 1),
+                )
+
+        def sub(b, i):
+            res[b, i] = opool.tile([P, NB], F32, name="res")
+            nc.vector.tensor_tensor(out=res[b, i][:], in0=psum["s", b, i][:], in1=dat[b, i // 4][:, i % 4, :], op=SUB)
+
+        def mul_store(b, i, eng):
+            if eng == "V":
+                nc.vector.tensor_tensor(out=res[b, i][:], in0=res[b, i][:], in1=wt_bc[:, b * NB : (b + 1) * NB], op=MULT)
+            else:
+                for h in (0, 1):
+                    c = slice(h * 256, h * 256 + 256)
+                    nc.gpsimd.tensor_tensor(out=res[b, i][:, c], in0=res[b, i][:, c], in1=wt_bc[:, b * NB + h * 256 : b * NB + h * 256 + 256], op=MULT)
+            nc.sync.dma_start(out=out[i * P : (i + 1) * P, b * NB : (b + 1) * NB], in_=res[b, i][:])
+
+        def k2_prep(b, engs):
+            tr_k2(b, 0)
+            ev_k2(b, 0, engs[0])
+            tr_k2(b, 1)
+            ev_k2(b, 1, engs[1])
+            q_k2(b)
+
+        scale_bcast()
+        nc.scalar.activation(out=polf[:], in_=polb[:], func=COPY)
+        for r in range(4):
+            widen(0, r)
+        tr_k2(0, 0)
+        ev_k2(0, 0, "S")
+        tr_d(0, 0)
+        ev_d(0, 0, "S")
+        tr_k2(0, 1)
+        ev_k2(0, 1, "S")
+        tr_d(0, 1)
+        ev_d(0, 1, "S")
+        q_k2(0)
+        q_d(0)
+        tr_d(1, 0)
+        ev_d(1, 0, "S")
+        tr_d(1, 1)
+        ev_d(1, 1, "S")
+        q_d(1)
+
+        def h_chain(b, g, evs, ints):
+            for t in range(4):
+                mm1(b, g, t)
+                ev_g(b, g, t, evs[t])
+            inter(b, g, 0, ints[0])
+            inter(b, g, 1, ints[1])
+            q_h(b, g)
+
+        h_chain(0, 0, "SVSV", "VV")
+        h_chain(0, 1, "SVSV", "VS")
+        for i in range(2):
+            tr_k1(i)
+            ev_k1(i, "S")
+            q_k1(i)
+        for r in range(4):
+            widen(1, r)
+        k2_prep(1, "SS")
+        INT = {(b, g): "SS" if g == 0 else "SV" for b in range(1, BLOCKS) for g in range(GROUPS)}
+        for b in range(BLOCKS):
+            nxt = b + 1 if b + 1 < BLOCKS else None
+            nn = b + 2 if b + 2 < BLOCKS else None
+            for i in range(ITILES):
+                mm2(b, i)
+                sub(b, i)
+                if b == 0 and i + 2 < ITILES:
+                    tr_k1(i + 2)
+                    ev_k1(i + 2, "S")
+                    q_k1(i + 2)
+                if nxt is not None and i in (0, 2):
+                    h_chain(nxt, i // 2, "SSSS", INT[nxt, i // 2])
+                if nn is not None and i < 4:
+                    widen(nn, i)
+                if nn is not None and i == 5:
+                    k2_prep(nn, "SS")
+                mul_store(b, i, "V" if i % 3 == 2 or (b == 3 and i > 5) else "G")

@@ -8,11 +8,13 @@ FLOPS = 2 * J1 * N2 * J2 + 2 * N1 * N2 * J1
 
 F32 = mybir.dt.float32
 BF16 = mybir.dt.bfloat16
+I32 = mybir.dt.int32
 U32 = mybir.dt.uint32
 U8 = mybir.dt.uint8
 FP8 = mybir.dt.float8_e4m3fn
 FP8X4 = mybir.dt.float8_e4m3fn_x4
 MULT = mybir.AluOpType.mult
+ADD = mybir.AluOpType.add
 SUB = mybir.AluOpType.subtract
 COPY = mybir.ActivationFunctionType.Copy
 
@@ -22,36 +24,48 @@ BLOCKS = N2 // NB
 ITILES = N1 // P
 GROUPS = J1 // 512
 
+V_BANKS = 4
+A_BANKS = 3
+RES_BUFS = 16
+V_AHEAD = 3
+S_FROM = (0, 2, 0, 0, 0, 0)
+
 
 def tile_nmr_relaxometry_residual_s7_kernel(tc, k1, dist, k2_bytes, k2_scale, pol, data, wt, out):
     nc = tc.nc
     with ExitStack() as ctx:
         keep = ctx.enter_context(tc.tile_pool(name="keep", bufs=1))
         wide = ctx.enter_context(tc.tile_pool(name="wide", bufs=2))
-        hpool = ctx.enter_context(tc.tile_pool(name="hpool", bufs=3))
-        hcpool = ctx.enter_context(tc.tile_pool(name="hcpool", bufs=4))
-        opool = ctx.enter_context(tc.tile_pool(name="opool", bufs=8))
-        ps_tr = ctx.enter_context(tc.psum_pool(name="ps_tr", bufs=2))
-        ps_g = ctx.enter_context(tc.psum_pool(name="ps_g", bufs=3))
-        ps_s = ctx.enter_context(tc.psum_pool(name="ps_s", bufs=3))
+        opool = ctx.enter_context(tc.tile_pool(name="opool", bufs=RES_BUFS))
+        ps_v = ctx.enter_context(tc.psum_pool(name="ps_v", bufs=V_BANKS))
+        ps_a = ctx.enter_context(tc.psum_pool(name="ps_a", bufs=A_BANKS))
+        ps_w = ctx.enter_context(tc.psum_pool(name="ps_w", bufs=1))
+        ctx.enter_context(tc.manual_schedule())
+        banks = {"v": ps_v, "a": ps_a, "w": ps_w}
 
         ident = keep.tile([P, P], F32, name="ident")
-        make_identity(nc, ident[:])
-
-        ks = keep.tile([P, 4], F32, name="ks")
-        nc.sync.dma_start(out=ks[:], in_=k2_scale.rearrange("o (p c) -> p (o c)", c=4))
-        kbytes, dsb, k1sb, dat = {}, {}, {}, {}
+        identb = keep.tile([P, BLOCKS], BF16, name="identb")
+        wt_rows = keep.tile([P, NB], BF16, name="wt_rows")
         wt_bc = keep.tile([P, N2], BF16, name="wt_bc")
+        ks = keep.tile([P, 4], F32, name="ks")
         polb = keep.tile([P, 8], BF16, name="polb")
         polf = keep.tile([P, 8], F32, name="polf")
+        kbytes, dsb, k1sb, dat = {}, {}, {}, {}
+        psum, k2w, kg, kcodes, kscales = {}, {}, {}, {}, {}
+        dg, dcodes, dscales = {}, {}, {}
+        k1g = keep.tile([P, 2 * ITILES, P, 4], BF16, name="k1g", align_bytes=64)
+        k1codes = keep.tile([P, 2 * ITILES * P], U32, name="k1codes", align_bytes=64)
+        k1scales = keep.tile([P, 2 * ITILES * P], U8, name="k1scales", align_bytes=64)
+        hp, hi, hcodes, hscales, res, wt_ps = {}, {}, {}, {}, {}, {}
 
         def load_k2(b):
             kbytes[b] = keep.tile([P, 4, J2], U8, name="kbytes%d" % b)
             nc.sync.dma_start(out=kbytes[b][:], in_=k2_bytes[b * NB : (b + 1) * NB, :].rearrange("(r p) l -> p r l", p=P))
 
-        def load_dist(g):
-            dsb[g] = keep.tile([P, 4 * J2], BF16, name="dsb%d" % g)
-            nc.sync.dma_start(out=dsb[g][:], in_=dist[g * 512 : (g + 1) * 512, :].rearrange("(p t) l -> p (t l)", t=4))
+        def load_dist(g, h):
+            dsb[g, h] = keep.tile([P, 2 * J2], BF16, name="dsb%d_%d" % (g, h))
+            rows = dist[g * 512 : (g + 1) * 512, :].rearrange("(p t) l -> p (t l)", t=4)
+            nc.sync.dma_start(out=dsb[g, h][:], in_=rows[:, h * 2 * J2 : (h + 1) * 2 * J2])
 
         def load_k1(i):
             k1sb[i] = keep.tile([P, J1], BF16, name="k1sb%d" % i)
@@ -64,12 +78,167 @@ def tile_nmr_relaxometry_residual_s7_kernel(tc, k1, dist, k2_bytes, k2_scale, po
                 in_=data[h * 512 : (h + 1) * 512, b * NB : (b + 1) * NB].rearrange("(i p) m -> p i m", p=P),
             )
 
-        def load_wt(b):
-            nc.sync.dma_start(out=wt_bc[:, b * NB : (b + 1) * NB], in_=wt[b * NB : (b + 1) * NB].partition_broadcast(P))
+        def copy_on(eng, dst, src):
+            if eng == "S":
+                nc.scalar.copy(out=dst, in_=src)
+            else:
+                nc.vector.tensor_copy(out=dst, in_=src)
+
+        def spread_wt(pair, pool):
+            wt_ps[pair, pool] = banks[pool].tile([P, 2, NB], BF16, name="bank")
+            for e in (0, 1):
+                b = 2 * pair + e
+                nc.tensor.matmul(wt_ps[pair, pool][:, e, :], lhsT=identb[:, b : b + 1].to_broadcast([P, P]), rhs=wt_rows[:], start=True, stop=True)
+
+        def copy_wt(pair, pool):
+            nc.scalar.copy(out=wt_bc[:, 2 * pair * NB : (2 * pair + 2) * NB], in_=wt_ps[pair, pool][:].rearrange("p e m -> p (e m)"))
+
+        def pol_f32():
+            nc.scalar.activation(out=polf[:], in_=polb[:], func=COPY)
+
+        def widen(b, h, eng):
+            k2w[b, h] = wide.tile([P, 2 * J2], BF16, name="k2w", bufs=8)
+            copy_on(eng, k2w[b, h][:], kbytes[b][:, 2 * h : 2 * h + 2, :].rearrange("p r l -> p (r l)").bitcast(FP8))
+
+        def word_transposes(key, pool, tile):
+            ps = banks[pool].tile([P, 2, 2, P], F32, name="bank")
+            psum[key] = ps
+            words = tile[:].bitcast(F32)
+            for a in (0, 1):
+                for u in (0, 1):
+                    nc.tensor.transpose(ps[:, a, u, :], words[:, 256 * a + u : 256 * (a + 1) : 2], ident[:])
+
+        def tr_k2(b, h, pool):
+            word_transposes(("k2", b, h), pool, k2w[b, h])
+
+        def ev_k2(b, r):
+            if r == 0:
+                kg[b] = wide.tile([P, 4, P, 4], BF16, name="kg", align_bytes=64)
+            src = psum["k2", b, r // 2][:, r % 2].rearrange("p u n -> p (u n)").bitcast(BF16).rearrange("p (u n e) -> p n u e", u=2, e=2)
+            nc.vector.tensor_tensor(
+                out=kg[b][:, r].rearrange("p n (u e) -> p n u e", u=2),
+                in0=src,
+                in1=ks[:].rearrange("p (o u e) -> p o u e", o=1, u=2).to_broadcast([P, P, 2, 2]),
+                op=MULT,
+            )
+
+        def q_k2(b):
+            kcodes[b] = wide.tile([P, NB], U32, name="kcodes", align_bytes=64, bufs=4)
+            kscales[b] = wide.tile([P, NB], U8, name="kscales", align_bytes=64, bufs=4)
+            nc.vector.quantize_mx(out=kcodes[b][:].bitcast(FP8X4), scales=kscales[b][:], in_=kg[b][:].rearrange("p r m e -> p (r m e)"))
+
+        def tr_d(g, h, pool):
+            word_transposes(("d", g, h), pool, dsb[g, h])
+
+        def ev_words(key, tile, eng):
+            dst = tile.rearrange("p a n e -> p (a n e)").bitcast(F32).rearrange("p (a n u) -> p a n u", a=2, u=2)
+            copy_on(eng, dst, psum[key][:].rearrange("p a u n -> p a n u"))
+
+        def ev_d(g, h, eng):
+            if h == 0:
+                dg[g] = keep.tile([P, 4, P, 4], BF16, name="dg%d" % g, align_bytes=64)
+            ev_words(("d", g, h), dg[g][:, 2 * h : 2 * h + 2], eng)
+
+        def q_d(g):
+            dcodes[g] = keep.tile([P, 512], U32, name="dcodes%d" % g, align_bytes=64)
+            dscales[g] = keep.tile([P, 512], U8, name="dscales%d" % g, align_bytes=64)
+            nc.vector.quantize_mx(out=dcodes[g][:].bitcast(FP8X4), scales=dscales[g][:], in_=dg[g][:].rearrange("p r m e -> p (r m e)"))
+
+        def tr_k1(i, pool):
+            word_transposes(("k1", i), pool, k1sb[i])
+
+        def ev_k1(i, eng):
+            ev_words(("k1", i), k1g[:, 2 * i : 2 * i + 2], eng)
+
+        def q_k1(lo, up):
+            nc.vector.quantize_mx(
+                out=k1codes[:, lo * 256 : up * 256].bitcast(FP8X4),
+                scales=k1scales[:, lo * 256 : up * 256],
+                in_=k1g[:, 2 * lo : 2 * up].rearrange("p a m e -> p (a m e)"),
+            )
+
+        def h_tile(b, g):
+            if b not in hi:
+                hi[b] = wide.tile([P, GROUPS, NB, 4], BF16, name="hi", align_bytes=64)
+            return hi[b][:, g]
+
+        def mx(dst, lc, ls, rc, rs, start=True, stop=True):
+            nc.tensor.matmul_mx(out=dst, lhsT=lc.bitcast(FP8X4), lhsT_scale=ls, rhs=rc.bitcast(FP8X4), rhs_scale=rs, start=start, stop=stop)
+
+        def mm1_quarter(b, g, q, pool):
+            ps = banks[pool].tile([P, 4, P], F32, name="bank")
+            psum["gq", b, g, q] = ps
+            m = slice(q * P, (q + 1) * P)
+            for t in range(4):
+                j = slice(t * P, (t + 1) * P)
+                mx(ps[:, t, :], dcodes[g][:, j], dscales[g][:, j], kcodes[b][:, m], kscales[b][:, m])
+
+        def ev_quarter(b, g, q):
+            nc.vector.tensor_tensor(
+                out=h_tile(b, g)[:, q * P : (q + 1) * P, :],
+                in0=psum["gq", b, g, q][:].rearrange("p t n -> p n t"),
+                in1=polf[:, 4 * g : 4 * g + 4].rearrange("p (o t) -> p o t", o=1).to_broadcast([P, P, 4]),
+                op=MULT,
+            )
+
+        def mm1_plane(b, g, t, w, pool):
+            ps = banks[pool].tile([P, NB], F32, name="bank")
+            psum["g", b, g, t] = ps
+            j = slice(t * P, (t + 1) * P)
+            mx(ps[:, :w], dcodes[g][:, j], dscales[g][:, j], kcodes[b][:, :w], kscales[b][:, :w])
+
+        def ev_plane(b, g, t, w=NB):
+            if t == 0:
+                hp[b, g] = wide.tile([P, 4, NB], BF16, name="hp", align_bytes=64, bufs=6)
+            nc.scalar.activation(out=hp[b, g][:, t, :w], in_=psum["g", b, g, t][:, :w], func=COPY, scale=polf[:, 4 * g + t : 4 * g + t + 1])
+
+        def interleave(b, g, lo, up, eng="S"):
+            dst = h_tile(b, g)[:, lo:up, :].rearrange("p (c i) t -> p c t i", i=4)
+            src = hp[b, g][:, :, lo:up].rearrange("p t (c i) -> p c t i", i=4)
+            copy_on(eng, dst, src)
+
+        def q_h(b, last, lo):
+            up = last + 1
+            if lo == 0:
+                hcodes[b] = wide.tile([P, GROUPS, NB], U32, name="hcodes", align_bytes=64)
+                hscales[b] = wide.tile([P, GROUPS, NB], U8, name="hscales", align_bytes=64)
+            nc.vector.quantize_mx(
+                out=hcodes[b][:, lo:up].rearrange("p g n -> p (g n)").bitcast(FP8X4),
+                scales=hscales[b][:, lo:up].rearrange("p g n -> p (g n)"),
+                in_=hi[b][:, lo:up].rearrange("p g n t -> p (g n t)"),
+            )
+
+        def mm2(b, i, pool):
+            ps = banks[pool].tile([P, NB], F32, name="bank")
+            psum["s", b, i] = ps
+            for g in range(GROUPS):
+                c = slice((2 * i + g) * P, (2 * i + g + 1) * P)
+                mx(ps[:], k1codes[:, c], k1scales[:, c], hcodes[b][:, g], hscales[b][:, g], g == 0, g == GROUPS - 1)
+
+        def sub(b, i):
+            res[b, i] = opool.tile([P, NB], F32, name="res")
+            nc.vector.tensor_tensor(out=res[b, i][:], in0=psum["s", b, i][:], in1=dat[b, i // 4][:, i % 4, :], op=SUB)
+
+        def mul(b, i, eng):
+            if eng == "V":
+                nc.vector.tensor_tensor(out=res[b, i][:], in0=res[b, i][:], in1=wt_ps[b // 2, "w"][:, b % 2, :], op=MULT)
+            else:
+                nc.gpsimd.tensor_tensor(out=res[b, i][:], in0=res[b, i][:], in1=wt_bc[:, b * NB : (b + 1) * NB], op=MULT)
+
+        def store(b, i):
+            nc.sync.dma_start(out=out[i * P : (i + 1) * P, b * NB : (b + 1) * NB], in_=res[b, i][:])
+
+        make_identity(nc, ident[:])
+        nc.vector.memset(wt_rows[:].bitcast(I32), 0)
+        nc.vector.tensor_copy(out=identb[:], in_=ident[:, 0:BLOCKS])
 
         load_k2(0)
-        load_dist(0)
-        load_dist(1)
+        nc.sync.dma_start(out=wt_rows[0:BLOCKS, :], in_=wt.rearrange("(b m) -> b m", b=BLOCKS))
+        load_dist(0, 0)
+        load_dist(0, 1)
+        nc.sync.dma_start(out=ks[:], in_=k2_scale.rearrange("o (p c) -> p (o c)", c=4))
+        load_dist(1, 0)
+        load_dist(1, 1)
         nc.sync.dma_start(out=polb[:].rearrange("p (g t) -> p g t", t=4), in_=pol.rearrange("(g p t) -> p g t", p=P, t=4))
         load_k2(1)
         load_k1(0)
@@ -77,224 +246,159 @@ def tile_nmr_relaxometry_residual_s7_kernel(tc, k1, dist, k2_bytes, k2_scale, po
         load_k2(2)
         load_k1(2)
         load_k1(3)
-        load_data(0, 0)
-        load_wt(0)
-        load_k1(4)
-        load_k1(5)
-        load_data(0, 1)
-        load_k1(6)
-        load_k1(7)
         load_k2(3)
+        load_data(0, 0)
+        for i in range(4, ITILES):
+            load_k1(i)
+        load_data(0, 1)
         for b in range(1, BLOCKS):
-            load_wt(b)
             load_data(b, 0)
             load_data(b, 1)
 
-        psum, k2w, kg, kcodes, kscales = {}, {}, {}, {}, {}
-        dg, dcodes, dscales, k1g, k1codes, k1scales = {}, {}, {}, {}, {}, {}
-        hp, hi, hcodes, hscales, res = {}, {}, {}, {}, {}
-        scale_bc = keep.tile([P, J2], F32, name="scale_bc")
+        HALF = NB // 2
+        vector = [(widen, 0, 0, "V")] + [(ev_k2, 0, r) for r in range(4)] + [(q_d, 0), (q_k2, 0)]
+        vector += [(ev_quarter, 0, 0, 0), (ev_quarter, 0, 0, 1), (q_d, 1), (ev_quarter, 0, 0, 2), (ev_quarter, 0, 0, 3)]
+        vector += [(ev_k2, 1, r) for r in range(4)] + [(ev_quarter, 0, 1, 0), (q_k2, 1)]
+        vector += [(ev_quarter, 0, 1, q) for q in range(1, 4)] + [(q_k1, 0, 2), (q_h, 0, 1, 0), (q_k1, 2, 4)]
+        scalar = [(widen, 0, 1, "S"), (ev_d, 0, 0, "S"), (ev_d, 0, 1, "S"), (pol_f32,), (widen, 1, 0, "S"), (ev_d, 1, 0, "S"), (copy_wt, 1, "a"), (ev_d, 1, 1, "S"), (widen, 1, 1, "S")]
+        scalar += [(copy_wt, 0, "w"), (widen, 2, 0, "S"), (widen, 2, 1, "S")] + [(ev_k1, i, "S") for i in range(ITILES)]
+        tensor = [(spread_wt, 0, "w"), (tr_k2, 0, 0, "v"), (tr_d, 0, 0, "a"), (tr_k2, 0, 1, "v"), (tr_d, 0, 1, "a"), (tr_d, 1, 0, "a"), (spread_wt, 1, "a"), (tr_d, 1, 1, "a")]
+        tensor += [(mm1_quarter, 0, 0, q, "v") for q in range(4)] + [(tr_k2, 1, 0, "v"), (tr_k2, 1, 1, "v"), (tr_k1, 0, "a"), (tr_k1, 1, "a")]
+        tensor += [(mm1_quarter, 0, 1, q, "v") for q in range(2)] + [(tr_k1, 2, "a"), (tr_k1, 3, "a")] + [(mm1_quarter, 0, 1, q, "v") for q in range(2, 4)]
+        tensor += [(tr_k1, 4, "a"), (tr_k1, 5, "a"), (mm1_plane, 1, 0, 0, NB, "a")]
 
-        def evict_words(eng, dst, src):
-            if eng == "S":
-                nc.scalar.copy(out=dst, in_=src)
-            else:
-                nc.vector.tensor_copy(out=dst, in_=src)
+        groups = [(1, 0), (2, 0), (2, 1), (3, 0), (3, 1)]
+        units = []
+        for n, grp in enumerate(groups):
+            between = [(widen, 3, 0, "S"), (widen, 3, 1, "S")] if n == 0 else []
+            units.append([(ev_plane,) + grp + (t, NB) for t in range(4)] + between + [(interleave,) + grp + (0, HALF), (interleave,) + grp + (HALF, NB)])
+        scalar = scalar[:-2] + units[0][:1] + scalar[-2:]
+        units[0] = units[0][1:]
 
-        def scale_bcast():
-            ps = ps_tr.tile([P, 4, P], F32, name="tr")
-            for c in range(4):
-                nc.tensor.transpose(ps[:, c, :], ks[:, c : c + 1].to_broadcast([P, P]), ident[:])
-            nc.vector.tensor_copy(out=scale_bc[:].rearrange("p (n c) -> p n c", c=4), in_=ps[:].rearrange("p c n -> p n c"))
+        def s_(n):
+            return (sub,) + divmod(n, ITILES)
 
-        def widen(b, r):
-            if r == 0:
-                k2w[b] = wide.tile([P, 4, J2], BF16, name="k2w")
-            nc.vector.tensor_tensor(out=k2w[b][:, r, :], in0=kbytes[b][:, r, :].bitcast(FP8), in1=scale_bc[:], op=MULT)
+        def m_(n):
+            return (mul,) + divmod(n, ITILES) + ("V",)
 
-        def widen_sg(b):
-            raw = wide.tile([P, 4, J2], BF16, name="k2raw")
-            nc.scalar.copy(out=raw[:].rearrange("p r l -> p (r l)"), in_=kbytes[b][:].rearrange("p r l -> p (r l)").bitcast(FP8))
-            k2w[b] = wide.tile([P, 4, J2], BF16, name="k2w")
-            for r in range(4):
-                nc.gpsimd.tensor_tensor(out=k2w[b][:, r, :], in0=raw[:, r, :], in1=scale_bc[:], op=MULT)
+        def e_(b, r):
+            return (ev_k2, b, r)
 
-        def pair_transposes(key, words, offs):
-            ps = ps_tr.tile([P, 2, 2, P], F32, name="tr")
-            psum[key] = ps
-            for a, off in enumerate(offs):
-                for u in (0, 1):
-                    nc.tensor.transpose(ps[:, a, u, :], words[:, off + u : off + 256 : 2], ident[:])
+        def h_(q):
+            return (ev_quarter, 1, 1, q)
 
-        def tr_k2(b, h):
-            words = k2w[b][:].rearrange("p r l -> p (r l)").bitcast(F32)
-            pair_transposes(("k2", b, h), words, (512 * h, 512 * h + 256))
+        runs = [
+            [e_(2, 0), e_(2, 1), e_(2, 2), e_(2, 3), (q_k1, 4, 8), s_(0), (q_k2, 2)],
+            [s_(1), h_(0), h_(1), s_(2), h_(2), h_(3), s_(3), s_(4), s_(5), m_(4), (q_h, 1, 1, 0)],
+            [s_(6), s_(7), e_(3, 0), e_(3, 1), s_(8), m_(7), e_(3, 2), e_(3, 3), s_(9), (q_k2, 3)],
+            [s_(10), s_(11), s_(12), m_(11), m_(12), s_(13), (q_h, 2, 1, 0)],
+            [s_(14), s_(15), s_(16), m_(15), s_(17), s_(18), m_(17), s_(19), s_(20), m_(20), s_(21), (q_h, 3, 1, 0)],
+            [s_(22), s_(23), s_(24), m_(23), s_(25), s_(26), m_(25), s_(27), s_(28), m_(27), s_(29), s_(30), m_(29), s_(31), m_(30), m_(31)],
+        ]
+        runs[1][8], runs[1][9] = runs[1][9], runs[1][8]
+        v_tail = [s for run in runs for s in run]
+        on_v = [s[1:3] for s in v_tail if s[0] is mul]
+        gpsimd = [(mul, b, i, "G") for b in range(BLOCKS) for i in range(ITILES) if (b, i) not in on_v]
+        sync = [(store, b, i) for b in range(BLOCKS) for i in range(ITILES)]
 
-        def ev_k2(b, h, eng):
-            if h == 0:
-                kg[b] = wide.tile([P, 4, P, 4], BF16, name="kg", align_bytes=64)
-            dst = kg[b][:].rearrange("p r m e -> p (r m e)").bitcast(F32).rearrange("p (r m u) -> p r m u", r=4, u=2)
-            evict_words(eng, dst[:, 2 * h : 2 * h + 2], psum["k2", b, h][:].rearrange("p a u r -> p a r u"))
+        def maker(step, pool):
+            f, a = step[0], step[1:]
+            if f is ev_k2:
+                return [(tr_k2, a[0], a[1] // 2, pool)] if a[1] % 2 == 0 else []
+            if step == m_(17):
+                return [(spread_wt, 1, "w")]
+            m = {ev_quarter: mm1_quarter, ev_plane: mm1_plane, sub: mm2}.get(f)
+            return [(m,) + a + (pool,)] if m else []
 
-        def q_k2(b):
-            kcodes[b] = wide.tile([P, NB], U32, name="kcodes", align_bytes=64)
-            kscales[b] = wide.tile([P, NB], U8, name="kscales", align_bytes=64)
-            nc.vector.quantize_mx(out=kcodes[b][:].bitcast(FP8X4), scales=kscales[b][:], in_=kg[b][:].rearrange("p r m e -> p (r m e)"))
+        for s in v_tail[:V_AHEAD]:
+            tensor += maker(s, "v")
+        tensor += [(tr_k1, 6, "a"), (tr_k1, 7, "a")]
+        k = 0
+        for n, run in enumerate(runs):
+            s_queue = [m for s in units[n] for m in maker(s, "a")] if n < len(units) else []
+            for pos in range(len(run)):
+                if pos >= S_FROM[n]:
+                    tensor += s_queue[:1]
+                    s_queue = s_queue[1:]
+                for s in v_tail[k + V_AHEAD : k + V_AHEAD + 1]:
+                    tensor += maker(s, "v")
+                k = k + 1
+        vector += v_tail
+        scalar += [s for unit in units for s in unit]
 
-        def tr_d(g, h):
-            pair_transposes(("d", g, h), dsb[g][:].bitcast(F32), (512 * h, 512 * h + 256))
+        def needs(step):
+            f, a = step[0], step[1:]
+            if f is tr_k2:
+                return [(widen,) + a[:2]]
+            if f is ev_k2:
+                return [(tr_k2, a[0], a[1] // 2)] + ([(q_k2, a[0] - 2)] if a[0] >= 2 else [])
+            if f is q_k2:
+                return [(ev_k2, a[0], r) for r in range(4)]
+            if f is ev_d:
+                return [(tr_d,) + a[:2]]
+            if f is q_d:
+                return [(ev_d, a[0], h) for h in (0, 1)]
+            if f is ev_k1:
+                return [(tr_k1, a[0])]
+            if f is q_k1:
+                return [(ev_k1, i) for i in range(a[0], a[1])]
+            if f is mm1_quarter or f is mm1_plane:
+                return [(q_k2, a[0]), (q_d, a[1])]
+            if f is ev_quarter:
+                return [(mm1_quarter,) + a, (pol_f32,)] + ([(q_h, a[0] - 2, 1)] if a[0] >= 2 else [])
+            if f is ev_plane:
+                return [(mm1_plane,) + a[:3], (pol_f32,)]
+            if f is interleave:
+                return [(ev_plane, a[0], a[1], t) for t in range(4)] + ([(q_h, a[0] - 2, 1)] if a[0] >= 2 else [])
+            if f is q_h:
+                gs = range(a[2], a[1] + 1)
+                return [w for w in h_writers[a[0]] if w[2] in gs] + ([(mm2, a[0] - 2, ITILES - 1)] if a[0] >= 2 else [])
+            if f is mm2:
+                return [(q_h, a[0], 1), [s for s in vector if s[0] is q_k1 and s[1] <= a[1] < s[2]][0]]
+            if f is sub:
+                n = a[0] * ITILES + a[1] - RES_BUFS
+                return [(mm2,) + a] + ([(store,) + divmod(n, ITILES)] if n >= 0 else [])
+            if f is mul:
+                return [(sub,) + a[:2], (copy_wt, a[0] // 2) if a[2] == "G" else (spread_wt, a[0] // 2, "w")]
+            if f is store:
+                return [(mul,) + a[:2]]
+            if f is copy_wt:
+                return [(spread_wt,) + a]
+            if step == (spread_wt, 1, "w"):
+                return [(copy_wt, 0)] + [(mul, 1, i) for i in v_tiles(1)] + [(mul, 0, i) for i in v_tiles(0)]
+            return []
 
-        def ev_d(g, h, eng):
-            if h == 0:
-                dg[g] = keep.tile([P, 4, P, 4], BF16, name="dg%d" % g, align_bytes=64)
-            dst = dg[g][:].rearrange("p r m e -> p (r m e)").bitcast(F32).rearrange("p (r m u) -> p r m u", r=4, u=2)
-            evict_words(eng, dst[:, 2 * h : 2 * h + 2], psum["d", g, h][:].rearrange("p a u r -> p a r u"))
+        def key(step):
+            n = {widen: 2, ev_d: 2, tr_d: 2, tr_k2: 2, tr_k1: 1, ev_k1: 1, mm1_plane: 3, ev_plane: 3, interleave: 3, mul: 2, q_h: 2, mm2: 2, mm1_quarter: 3, copy_wt: 1}
+            return step[: 1 + n.get(step[0], len(step))]
 
-        def q_d(g):
-            dcodes[g] = keep.tile([P, 512], U32, name="dcodes%d" % g, align_bytes=64)
-            dscales[g] = keep.tile([P, 512], U8, name="dscales%d" % g, align_bytes=64)
-            nc.vector.quantize_mx(out=dcodes[g][:].bitcast(FP8X4), scales=dscales[g][:], in_=dg[g][:].rearrange("p r m e -> p (r m e)"))
+        def readers(step):
+            f, a = step[0], step[1:]
+            if f is tr_k2:
+                return [(ev_k2, a[0], 2 * a[1]), (ev_k2, a[0], 2 * a[1] + 1)]
+            if f is spread_wt:
+                return [(copy_wt, a[0])]
+            return [({tr_d: ev_d, tr_k1: ev_k1, mm1_quarter: ev_quarter, mm1_plane: ev_plane, mm2: sub}[f],) + key(step)[1:]]
 
-        def tr_k1(i):
-            pair_transposes(("k1", i), k1sb[i][:].bitcast(F32), (0, 256))
+        def v_tiles(b):
+            return [s[2] for s in vector if s[0] is mul and s[1] == b]
 
-        def ev_k1(i, eng):
-            k1g[i] = keep.tile([P, 2, P, 4], BF16, name="k1g%d" % i, align_bytes=64)
-            dst = k1g[i][:].rearrange("p g m e -> p (g m e)").bitcast(F32).rearrange("p (g m u) -> p g m u", g=2, u=2)
-            evict_words(eng, dst, psum["k1", i][:].rearrange("p g u r -> p g r u"))
-
-        def q_k1(i):
-            k1codes[i] = keep.tile([P, 256], U32, name="k1codes%d" % i, align_bytes=64)
-            k1scales[i] = keep.tile([P, 256], U8, name="k1scales%d" % i, align_bytes=64)
-            nc.vector.quantize_mx(out=k1codes[i][:].bitcast(FP8X4), scales=k1scales[i][:], in_=k1g[i][:].rearrange("p g m e -> p (g m e)"))
-
-        def mm1(b, g, t):
-            ps = ps_g.tile([P, NB], F32, name="g_ps")
-            psum["g", b, g, t] = ps
-            cols = slice(t * P, (t + 1) * P)
-            nc.tensor.matmul_mx(
-                out=ps[:],
-                lhsT=dcodes[g][:, cols].bitcast(FP8X4),
-                lhsT_scale=dscales[g][:, cols],
-                rhs=kcodes[b][:].bitcast(FP8X4),
-                rhs_scale=kscales[b][:],
-                start=True,
-                stop=True,
-            )
-
-        def ev_g(b, g, t, eng):
-            if t == 0:
-                hp[b, g] = hpool.tile([P, 4, NB], BF16, name="hp", align_bytes=64)
-            dst = hp[b, g][:, t, :]
-            src = psum["g", b, g, t][:]
-            col = polf[:, 4 * g + t : 4 * g + t + 1]
-            if eng == "S":
-                nc.scalar.activation(out=dst, in_=src, func=COPY, scale=col)
-            else:
-                nc.vector.tensor_scalar(out=dst, in0=src, scalar1=col, scalar2=None, op0=MULT)
-
-        def inter(b, g, half, eng):
-            if half == 0:
-                hi[b, g] = hpool.tile([P, NB, 4], BF16, name="hi", align_bytes=64)
-            cols = slice(half * 256, half * 256 + 256)
-            dst = hi[b, g][:, cols, :].rearrange("p (c i) t -> p c t i", i=4)
-            src = hp[b, g][:, :, cols].rearrange("p t (c i) -> p c t i", i=4)
-            evict_words(eng, dst, src)
-
-        def q_h(b, g):
-            hcodes[b, g] = hcpool.tile([P, NB], U32, name="hcodes", align_bytes=64)
-            hscales[b, g] = hcpool.tile([P, NB], U8, name="hscales", align_bytes=64)
-            nc.vector.quantize_mx(
-                out=hcodes[b, g][:].bitcast(FP8X4), scales=hscales[b, g][:], in_=hi[b, g][:].rearrange("p n t -> p (n t)")
-            )
-
-        def mm2(b, i):
-            ps = ps_s.tile([P, NB], F32, name="s_ps")
-            psum["s", b, i] = ps
-            for g in range(GROUPS):
-                cols = slice(g * P, (g + 1) * P)
-                nc.tensor.matmul_mx(
-                    out=ps[:],
-                    lhsT=k1codes[i][:, cols].bitcast(FP8X4),
-                    lhsT_scale=k1scales[i][:, cols],
-                    rhs=hcodes[b, g][:].bitcast(FP8X4),
-                    rhs_scale=hscales[b, g][:],
-                    start=(g == 0),
-                    stop=(g == GROUPS - 1),
-                )
-
-        def sub(b, i):
-            res[b, i] = opool.tile([P, NB], F32, name="res")
-            nc.vector.tensor_tensor(out=res[b, i][:], in0=psum["s", b, i][:], in1=dat[b, i // 4][:, i % 4, :], op=SUB)
-
-        def mul_store(b, i, eng):
-            if eng == "V":
-                nc.vector.tensor_tensor(out=res[b, i][:], in0=res[b, i][:], in1=wt_bc[:, b * NB : (b + 1) * NB], op=MULT)
-            else:
-                for h in (0, 1):
-                    c = slice(h * 256, h * 256 + 256)
-                    nc.gpsimd.tensor_tensor(out=res[b, i][:, c], in0=res[b, i][:, c], in1=wt_bc[:, b * NB + h * 256 : b * NB + h * 256 + 256], op=MULT)
-            nc.sync.dma_start(out=out[i * P : (i + 1) * P, b * NB : (b + 1) * NB], in_=res[b, i][:])
-
-        def k2_prep(b, engs):
-            tr_k2(b, 0)
-            ev_k2(b, 0, engs[0])
-            tr_k2(b, 1)
-            ev_k2(b, 1, engs[1])
-            q_k2(b)
-
-        scale_bcast()
-        nc.scalar.activation(out=polf[:], in_=polb[:], func=COPY)
-        for r in range(4):
-            widen(0, r)
-        tr_k2(0, 0)
-        ev_k2(0, 0, "S")
-        tr_d(0, 0)
-        ev_d(0, 0, "S")
-        tr_k2(0, 1)
-        ev_k2(0, 1, "S")
-        tr_d(0, 1)
-        ev_d(0, 1, "S")
-        q_k2(0)
-        q_d(0)
-        tr_d(1, 0)
-        ev_d(1, 0, "S")
-        tr_d(1, 1)
-        ev_d(1, 1, "S")
-        q_d(1)
-
-        def h_chain(b, g, evs, ints):
-            for t in range(4):
-                mm1(b, g, t)
-                ev_g(b, g, t, evs[t])
-            inter(b, g, 0, ints[0])
-            inter(b, g, 1, ints[1])
-            q_h(b, g)
-
-        h_chain(0, 0, "SVSV", "VV")
-        h_chain(0, 1, "SVSV", "VS")
-        for i in range(2):
-            tr_k1(i)
-            ev_k1(i, "S")
-            q_k1(i)
-        for r in range(4):
-            widen(1, r)
-        k2_prep(1, "SS")
-        INT = {(b, g): "SS" if g == 0 else "SV" for b in range(1, BLOCKS) for g in range(GROUPS)}
-        for b in range(BLOCKS):
-            nxt = b + 1 if b + 1 < BLOCKS else None
-            nn = b + 2 if b + 2 < BLOCKS else None
-            for i in range(ITILES):
-                mm2(b, i)
-                sub(b, i)
-                if b == 0 and i + 2 < ITILES:
-                    tr_k1(i + 2)
-                    ev_k1(i + 2, "S")
-                    q_k1(i + 2)
-                if nxt is not None and i in (0, 2):
-                    h_chain(nxt, i // 2, "SSSS", INT[nxt, i // 2])
-                if nn is not None and i < 4:
-                    widen(nn, i)
-                if nn is not None and i == 5:
-                    k2_prep(nn, "SS")
-                mul_store(b, i, "V" if i % 3 == 2 or (b == 3 and i > 5) else "G")
+        h_writers = {b: [key(s) for s in vector + scalar if s[0] in (ev_quarter, interleave) and s[1] == b] for b in range(BLOCKS)}
+        extra, rings = {}, {"v": [], "a": []}
+        for step in tensor:
+            if step[-1] != "w":
+                ring = rings[step[-1]]
+                depth = {"v": V_BANKS, "a": A_BANKS}[step[-1]]
+                if len(ring) >= depth:
+                    extra[key(step)] = readers(ring[-depth])
+                ring.append(step)
+        done, queues = set(), [list(tensor), list(vector), list(scalar), list(gpsimd), list(sync)]
+        while any(queues):
+            moved = False
+            for queue in queues:
+                while queue and all(n in done for n in needs(queue[0]) + extra.get(key(queue[0]), [])):
+                    step = queue.pop(0)
+                    step[0](*step[1:])
+                    done.add(key(step))
+                    moved = True
+            assert moved, [q[0] for q in queues if q]

@@ -27,8 +27,12 @@ GROUPS = J1 // 512
 V_BANKS = 4
 A_BANKS = 3
 RES_BUFS = 16
-V_AHEAD = 3
-S_FROM = (0, 2, 0, 0, 0, 0)
+V_LEAD = 3
+S_LEAD = 2
+S_SHIFT = 2
+IL = 2.4
+W_LEAD = 6
+W_AT = 32
 
 
 def tile_nmr_relaxometry_residual_s7_kernel(tc, k1, dist, k2_bytes, k2_scale, pol, data, wt, out):
@@ -37,11 +41,8 @@ def tile_nmr_relaxometry_residual_s7_kernel(tc, k1, dist, k2_bytes, k2_scale, po
         keep = ctx.enter_context(tc.tile_pool(name="keep", bufs=1))
         wide = ctx.enter_context(tc.tile_pool(name="wide", bufs=2))
         opool = ctx.enter_context(tc.tile_pool(name="opool", bufs=RES_BUFS))
-        ps_v = ctx.enter_context(tc.psum_pool(name="ps_v", bufs=V_BANKS))
-        ps_a = ctx.enter_context(tc.psum_pool(name="ps_a", bufs=A_BANKS))
-        ps_w = ctx.enter_context(tc.psum_pool(name="ps_w", bufs=1))
+        ps_pool = ctx.enter_context(tc.psum_pool(name="ps", bufs=1))
         ctx.enter_context(tc.manual_schedule())
-        banks = {"v": ps_v, "a": ps_a, "w": ps_w}
 
         ident = keep.tile([P, P], F32, name="ident")
         identb = keep.tile([P, BLOCKS], BF16, name="identb")
@@ -51,16 +52,20 @@ def tile_nmr_relaxometry_residual_s7_kernel(tc, k1, dist, k2_bytes, k2_scale, po
         polb = keep.tile([P, 8], BF16, name="polb")
         polf = keep.tile([P, 8], F32, name="polf")
         kbytes, dsb, k1sb, dat = {}, {}, {}, {}
-        psum, k2w, kg, kcodes, kscales = {}, {}, {}, {}, {}
+        psum, k2w = {}, {}
+        kg = keep.tile([P, 4 * BLOCKS, P, 4], BF16, name="kg", align_bytes=64)
+        kcodes = keep.tile([P, N2], U32, name="kcodes", align_bytes=64)
+        kscales = keep.tile([P, N2], U8, name="kscales", align_bytes=64)
         dg, dcodes, dscales = {}, {}, {}
         k1g = keep.tile([P, 2 * ITILES, P, 4], BF16, name="k1g", align_bytes=64)
         k1codes = keep.tile([P, 2 * ITILES * P], U32, name="k1codes", align_bytes=64)
         k1scales = keep.tile([P, 2 * ITILES * P], U8, name="k1scales", align_bytes=64)
         hp, hi, hcodes, hscales, res, wt_ps = {}, {}, {}, {}, {}, {}
 
-        def load_k2(b):
-            kbytes[b] = keep.tile([P, 4, J2], U8, name="kbytes%d" % b)
-            nc.sync.dma_start(out=kbytes[b][:], in_=k2_bytes[b * NB : (b + 1) * NB, :].rearrange("(r p) l -> p r l", p=P))
+        def load_k2(b, h):
+            kbytes[b, h] = keep.tile([P, 2, J2], U8, name="kbytes%d_%d" % (b, h))
+            rows = k2_bytes[b * NB + h * 2 * P : b * NB + (h + 1) * 2 * P, :]
+            nc.sync.dma_start(out=kbytes[b, h][:], in_=rows.rearrange("(r p) l -> p r l", p=P))
 
         def load_dist(g, h):
             dsb[g, h] = keep.tile([P, 2 * J2], BF16, name="dsb%d_%d" % (g, h))
@@ -81,27 +86,34 @@ def tile_nmr_relaxometry_residual_s7_kernel(tc, k1, dist, k2_bytes, k2_scale, po
         def copy_on(eng, dst, src):
             if eng == "S":
                 nc.scalar.copy(out=dst, in_=src)
+            elif eng == "G":
+                nc.gpsimd.tensor_copy(out=dst, in_=src)
             else:
                 nc.vector.tensor_copy(out=dst, in_=src)
 
         def spread_wt(pair, pool):
-            wt_ps[pair, pool] = banks[pool].tile([P, 2, NB], BF16, name="bank")
+            wt_ps[pair] = ps_pool.tile([P, 2, NB], BF16, name="bank%d" % pool)
             for e in (0, 1):
                 b = 2 * pair + e
-                nc.tensor.matmul(wt_ps[pair, pool][:, e, :], lhsT=identb[:, b : b + 1].to_broadcast([P, P]), rhs=wt_rows[:], start=True, stop=True)
+                nc.tensor.matmul(wt_ps[pair][:, e, :], lhsT=identb[:, b : b + 1].to_broadcast([P, P]), rhs=wt_rows[:], start=True, stop=True)
 
-        def copy_wt(pair, pool):
-            nc.scalar.copy(out=wt_bc[:, 2 * pair * NB : (2 * pair + 2) * NB], in_=wt_ps[pair, pool][:].rearrange("p e m -> p (e m)"))
+        def load_wt(b):
+            nc.sync.dma_start(out=wt_bc[:, b * NB : (b + 1) * NB], in_=wt[b * NB : (b + 1) * NB].partition_broadcast(P))
 
         def pol_f32():
             nc.scalar.activation(out=polf[:], in_=polb[:], func=COPY)
 
         def widen(b, h, eng):
-            k2w[b, h] = wide.tile([P, 2 * J2], BF16, name="k2w", bufs=8)
-            copy_on(eng, k2w[b, h][:], kbytes[b][:, 2 * h : 2 * h + 2, :].rearrange("p r l -> p (r l)").bitcast(FP8))
+            if b < 2:
+                k2w[b, h] = wide.tile([P, 2 * J2], BF16, name="k2w", bufs=4)
+            elif b == 3:
+                k2w[b, h] = kg[:, 4 + 2 * h : 6 + 2 * h].rearrange("p a n e -> p (a n e)")
+            else:
+                k2w[b, h] = dg[3 - b][:, 2 * h : 2 * h + 2].rearrange("p a n e -> p (a n e)")
+            copy_on(eng, k2w[b, h][:], kbytes[b, h][:].rearrange("p r l -> p (r l)").bitcast(FP8))
 
         def word_transposes(key, pool, tile):
-            ps = banks[pool].tile([P, 2, 2, P], F32, name="bank")
+            ps = ps_pool.tile([P, 2, 2, P], F32, name="bank%d" % pool)
             psum[key] = ps
             words = tile[:].bitcast(F32)
             for a in (0, 1):
@@ -112,20 +124,20 @@ def tile_nmr_relaxometry_residual_s7_kernel(tc, k1, dist, k2_bytes, k2_scale, po
             word_transposes(("k2", b, h), pool, k2w[b, h])
 
         def ev_k2(b, r):
-            if r == 0:
-                kg[b] = wide.tile([P, 4, P, 4], BF16, name="kg", align_bytes=64)
             src = psum["k2", b, r // 2][:, r % 2].rearrange("p u n -> p (u n)").bitcast(BF16).rearrange("p (u n e) -> p n u e", u=2, e=2)
             nc.vector.tensor_tensor(
-                out=kg[b][:, r].rearrange("p n (u e) -> p n u e", u=2),
+                out=kg[:, 4 * b + r].rearrange("p n (u e) -> p n u e", u=2),
                 in0=src,
                 in1=ks[:].rearrange("p (o u e) -> p o u e", o=1, u=2).to_broadcast([P, P, 2, 2]),
                 op=MULT,
             )
 
-        def q_k2(b):
-            kcodes[b] = wide.tile([P, NB], U32, name="kcodes", align_bytes=64, bufs=4)
-            kscales[b] = wide.tile([P, NB], U8, name="kscales", align_bytes=64, bufs=4)
-            nc.vector.quantize_mx(out=kcodes[b][:].bitcast(FP8X4), scales=kscales[b][:], in_=kg[b][:].rearrange("p r m e -> p (r m e)"))
+        def q_k2(lo, up):
+            nc.vector.quantize_mx(
+                out=kcodes[:, lo * NB : up * NB].bitcast(FP8X4),
+                scales=kscales[:, lo * NB : up * NB],
+                in_=kg[:, 4 * lo : 4 * up].rearrange("p r m e -> p (r m e)"),
+            )
 
         def tr_d(g, h, pool):
             word_transposes(("d", g, h), pool, dsb[g, h])
@@ -166,12 +178,12 @@ def tile_nmr_relaxometry_residual_s7_kernel(tc, k1, dist, k2_bytes, k2_scale, po
             nc.tensor.matmul_mx(out=dst, lhsT=lc.bitcast(FP8X4), lhsT_scale=ls, rhs=rc.bitcast(FP8X4), rhs_scale=rs, start=start, stop=stop)
 
         def mm1_quarter(b, g, q, pool):
-            ps = banks[pool].tile([P, 4, P], F32, name="bank")
+            ps = ps_pool.tile([P, 4, P], F32, name="bank%d" % pool)
             psum["gq", b, g, q] = ps
-            m = slice(q * P, (q + 1) * P)
+            m = slice(b * NB + q * P, b * NB + (q + 1) * P)
             for t in range(4):
                 j = slice(t * P, (t + 1) * P)
-                mx(ps[:, t, :], dcodes[g][:, j], dscales[g][:, j], kcodes[b][:, m], kscales[b][:, m])
+                mx(ps[:, t, :], dcodes[g][:, j], dscales[g][:, j], kcodes[:, m], kscales[:, m])
 
         def ev_quarter(b, g, q):
             nc.vector.tensor_tensor(
@@ -182,14 +194,14 @@ def tile_nmr_relaxometry_residual_s7_kernel(tc, k1, dist, k2_bytes, k2_scale, po
             )
 
         def mm1_plane(b, g, t, w, pool):
-            ps = banks[pool].tile([P, NB], F32, name="bank")
+            ps = ps_pool.tile([P, NB], F32, name="bank%d" % pool)
             psum["g", b, g, t] = ps
             j = slice(t * P, (t + 1) * P)
-            mx(ps[:, :w], dcodes[g][:, j], dscales[g][:, j], kcodes[b][:, :w], kscales[b][:, :w])
+            mx(ps[:, :w], dcodes[g][:, j], dscales[g][:, j], kcodes[:, b * NB : b * NB + w], kscales[:, b * NB : b * NB + w])
 
         def ev_plane(b, g, t, w=NB):
             if t == 0:
-                hp[b, g] = wide.tile([P, 4, NB], BF16, name="hp", align_bytes=64, bufs=6)
+                hp[b, g] = wide.tile([P, 4, NB], BF16, name="hp", align_bytes=64, bufs=5)
             nc.scalar.activation(out=hp[b, g][:, t, :w], in_=psum["g", b, g, t][:, :w], func=COPY, scale=polf[:, 4 * g + t : 4 * g + t + 1])
 
         def interleave(b, g, lo, up, eng="S"):
@@ -209,7 +221,7 @@ def tile_nmr_relaxometry_residual_s7_kernel(tc, k1, dist, k2_bytes, k2_scale, po
             )
 
         def mm2(b, i, pool):
-            ps = banks[pool].tile([P, NB], F32, name="bank")
+            ps = ps_pool.tile([P, NB], F32, name="bank%d" % pool)
             psum["s", b, i] = ps
             for g in range(GROUPS):
                 c = slice((2 * i + g) * P, (2 * i + g + 1) * P)
@@ -221,7 +233,7 @@ def tile_nmr_relaxometry_residual_s7_kernel(tc, k1, dist, k2_bytes, k2_scale, po
 
         def mul(b, i, eng):
             if eng == "V":
-                nc.vector.tensor_tensor(out=res[b, i][:], in0=res[b, i][:], in1=wt_ps[b // 2, "w"][:, b % 2, :], op=MULT)
+                nc.vector.tensor_tensor(out=res[b, i][:], in0=res[b, i][:], in1=wt_ps[b // 2][:, b % 2, :], op=MULT)
             else:
                 nc.gpsimd.tensor_tensor(out=res[b, i][:], in0=res[b, i][:], in1=wt_bc[:, b * NB : (b + 1) * NB], op=MULT)
 
@@ -232,48 +244,43 @@ def tile_nmr_relaxometry_residual_s7_kernel(tc, k1, dist, k2_bytes, k2_scale, po
         nc.vector.memset(wt_rows[:].bitcast(I32), 0)
         nc.vector.tensor_copy(out=identb[:], in_=ident[:, 0:BLOCKS])
 
-        load_k2(0)
-        nc.sync.dma_start(out=wt_rows[0:BLOCKS, :], in_=wt.rearrange("(b m) -> b m", b=BLOCKS))
-        load_dist(0, 0)
-        load_dist(0, 1)
+        load_k2(0, 0)
+        load_k2(0, 1)
         nc.sync.dma_start(out=ks[:], in_=k2_scale.rearrange("o (p c) -> p (o c)", c=4))
+        load_dist(0, 0)
+        load_k2(1, 0)
+        load_dist(0, 1)
+        load_k2(1, 1)
         load_dist(1, 0)
         load_dist(1, 1)
+        nc.sync.dma_start(out=wt_rows[0:BLOCKS, :], in_=wt.rearrange("(b m) -> b m", b=BLOCKS))
         nc.sync.dma_start(out=polb[:].rearrange("p (g t) -> p g t", t=4), in_=pol.rearrange("(g p t) -> p g t", p=P, t=4))
-        load_k2(1)
+        load_k2(2, 0)
+        load_k2(2, 1)
         load_k1(0)
         load_k1(1)
-        load_k2(2)
+        load_k2(3, 0)
+        load_k2(3, 1)
         load_k1(2)
         load_k1(3)
-        load_k2(3)
+        load_k1(4)
+        load_k1(5)
+        load_k1(6)
+        load_k1(7)
         load_data(0, 0)
-        for i in range(4, ITILES):
-            load_k1(i)
+        load_wt(0)
         load_data(0, 1)
-        for b in range(1, BLOCKS):
-            load_data(b, 0)
-            load_data(b, 1)
+        load_wt(1)
+        load_data(1, 0)
+        load_data(1, 1)
+        load_wt(2)
+        load_data(2, 0)
+        load_data(2, 1)
+        load_wt(3)
+        load_data(3, 0)
+        load_data(3, 1)
 
         HALF = NB // 2
-        vector = [(widen, 0, 0, "V")] + [(ev_k2, 0, r) for r in range(4)] + [(q_d, 0), (q_k2, 0)]
-        vector += [(ev_quarter, 0, 0, 0), (ev_quarter, 0, 0, 1), (q_d, 1), (ev_quarter, 0, 0, 2), (ev_quarter, 0, 0, 3)]
-        vector += [(ev_k2, 1, r) for r in range(4)] + [(ev_quarter, 0, 1, 0), (q_k2, 1)]
-        vector += [(ev_quarter, 0, 1, q) for q in range(1, 4)] + [(q_k1, 0, 2), (q_h, 0, 1, 0), (q_k1, 2, 4)]
-        scalar = [(widen, 0, 1, "S"), (ev_d, 0, 0, "S"), (ev_d, 0, 1, "S"), (pol_f32,), (widen, 1, 0, "S"), (ev_d, 1, 0, "S"), (copy_wt, 1, "a"), (ev_d, 1, 1, "S"), (widen, 1, 1, "S")]
-        scalar += [(copy_wt, 0, "w"), (widen, 2, 0, "S"), (widen, 2, 1, "S")] + [(ev_k1, i, "S") for i in range(ITILES)]
-        tensor = [(spread_wt, 0, "w"), (tr_k2, 0, 0, "v"), (tr_d, 0, 0, "a"), (tr_k2, 0, 1, "v"), (tr_d, 0, 1, "a"), (tr_d, 1, 0, "a"), (spread_wt, 1, "a"), (tr_d, 1, 1, "a")]
-        tensor += [(mm1_quarter, 0, 0, q, "v") for q in range(4)] + [(tr_k2, 1, 0, "v"), (tr_k2, 1, 1, "v"), (tr_k1, 0, "a"), (tr_k1, 1, "a")]
-        tensor += [(mm1_quarter, 0, 1, q, "v") for q in range(2)] + [(tr_k1, 2, "a"), (tr_k1, 3, "a")] + [(mm1_quarter, 0, 1, q, "v") for q in range(2, 4)]
-        tensor += [(tr_k1, 4, "a"), (tr_k1, 5, "a"), (mm1_plane, 1, 0, 0, NB, "a")]
-
-        groups = [(1, 0), (2, 0), (2, 1), (3, 0), (3, 1)]
-        units = []
-        for n, grp in enumerate(groups):
-            between = [(widen, 3, 0, "S"), (widen, 3, 1, "S")] if n == 0 else []
-            units.append([(ev_plane,) + grp + (t, NB) for t in range(4)] + between + [(interleave,) + grp + (0, HALF), (interleave,) + grp + (HALF, NB)])
-        scalar = scalar[:-2] + units[0][:1] + scalar[-2:]
-        units[0] = units[0][1:]
 
         def s_(n):
             return (sub,) + divmod(n, ITILES)
@@ -284,56 +291,62 @@ def tile_nmr_relaxometry_residual_s7_kernel(tc, k1, dist, k2_bytes, k2_scale, po
         def e_(b, r):
             return (ev_k2, b, r)
 
-        def h_(q):
-            return (ev_quarter, 1, 1, q)
+        def h_(b, q, g=1):
+            return (ev_quarter, b, g, q)
 
+        groups = [(0,0,512),(1,0,512),(2,0,512),(2,1,512),(3,0,512),(3,1,512)]
+        units = [[(ev_plane, b, g, t, w) for t in range(4)] + [(interleave, b, g, lo, lo + HALF) for lo in range(0, w, HALF)] for b, g, w in groups]
+        k1e = [(ev_k1, i, "S") for i in range(ITILES)]
+        v_first = [(widen, 0, 0, "V")] + [(ev_k2, 0, r) for r in range(4)] + [(q_d, 0), (q_k2, 0, 1)]
+        s_first = [(widen, 0, 1, "S"), (ev_d, 0, 0, "S"), (ev_d, 0, 1, "S"), (ev_d, 1, 0, "S"), (ev_d, 1, 1, "S"), (pol_f32,)]
+        tensor = [(tr_k2, 0, 0, "v"), (tr_d, 0, 0, "a"), (tr_k2, 0, 1, "v"), (tr_d, 0, 1, "a"), (tr_k2, 1, 0, "v"), (tr_d, 1, 0, "a"), (tr_d, 1, 1, "a"), (tr_k2, 1, 1, "v")]
+        tensor += [(mm1_plane, 0, 0, t, NB, "a") for t in range(4)] + [(mm1_quarter, 0, 1, q, "v") for q in range(4)]
+        tensor += [(tr_k1, 0, "a"), (tr_k1, 1, "a"), (tr_k2, 2, 0, "v")]
+        v_rest = [e_(1, 0), e_(1, 1), (q_d, 1), e_(1, 2), e_(1, 3)] + [h_(0, q) for q in range(3)] + [(q_k2, 1, 2), h_(0, 3)]
+        v_rest += [e_(2, r) for r in range(4)] + [(q_k2, 2, 3), (q_k1, 0, 4), (q_h, 0, 1, 0)]
+        s_rest = units[0][:4] + k1e[:2] + units[0][4:5] + k1e[2:4] + units[0][5:]
+        s_rest += k1e[4:] + [s for u in units[1:] for s in u]
         runs = [
-            [e_(2, 0), e_(2, 1), e_(2, 2), e_(2, 3), (q_k1, 4, 8), s_(0), (q_k2, 2)],
-            [s_(1), h_(0), h_(1), s_(2), h_(2), h_(3), s_(3), s_(4), s_(5), m_(4), (q_h, 1, 1, 0)],
-            [s_(6), s_(7), e_(3, 0), e_(3, 1), s_(8), m_(7), e_(3, 2), e_(3, 3), s_(9), (q_k2, 3)],
-            [s_(10), s_(11), s_(12), m_(11), m_(12), s_(13), (q_h, 2, 1, 0)],
-            [s_(14), s_(15), s_(16), m_(15), s_(17), s_(18), m_(17), s_(19), s_(20), m_(20), s_(21), (q_h, 3, 1, 0)],
-            [s_(22), s_(23), s_(24), m_(23), s_(25), s_(26), m_(25), s_(27), s_(28), m_(27), s_(29), s_(30), m_(29), s_(31), m_(30), m_(31)],
+            [h_(1, 0), h_(1, 1), s_(0), h_(1, 2), h_(1, 3), s_(1), (q_k1, 4, 8)],
+            [e_(3, 0), e_(3, 1), s_(2), e_(3, 2), e_(3, 3), s_(3), (q_h, 1, 1, 0)],
+            [s_(4), s_(5), s_(6), s_(7), m_(5), m_(7), s_(8), (q_k2, 3, 4)],
+            [s_(9), s_(10), s_(11), s_(12), m_(10), m_(12), s_(13), (q_h, 2, 1, 0)],
+            [s_(14), s_(15), s_(16), s_(17), m_(16), m_(17), s_(18), s_(19), s_(20), m_(19), s_(21), (q_h, 3, 1, 0)],
+            [s_(22), s_(23), s_(24), m_(23), s_(25), s_(26), m_(25), s_(27), s_(28), m_(27), s_(29), s_(30), m_(29), s_(31), m_(31)],
         ]
-        runs[1][8], runs[1][9] = runs[1][9], runs[1][8]
-        v_tail = [s for run in runs for s in run]
-        on_v = [s[1:3] for s in v_tail if s[0] is mul]
-        gpsimd = [(mul, b, i, "G") for b in range(BLOCKS) for i in range(ITILES) if (b, i) not in on_v]
+        v_rest += [s for run in runs for s in run]
+        vector, scalar = v_first + v_rest, s_first + s_rest
+        on_v = [s[1:3] for s in vector if s[0] is mul]
+        gpsimd = [(widen, b, h, "G") for b in range(1, BLOCKS) for h in (0, 1)]
+        gpsimd += [(mul, b, i, "G") for b in range(BLOCKS) for i in range(ITILES) if (b, i) not in on_v]
         sync = [(store, b, i) for b in range(BLOCKS) for i in range(ITILES)]
 
         def maker(step, pool):
             f, a = step[0], step[1:]
             if f is ev_k2:
-                return [(tr_k2, a[0], a[1] // 2, pool)] if a[1] % 2 == 0 else []
-            if step == m_(17):
-                return [(spread_wt, 1, "w")]
-            m = {ev_quarter: mm1_quarter, ev_plane: mm1_plane, sub: mm2}.get(f)
-            return [(m,) + a + (pool,)] if m else []
+                return (tr_k2, a[0], a[1] // 2, pool) if a[1] % 2 == 0 else None
+            m = {ev_quarter: mm1_quarter, ev_plane: mm1_plane, sub: mm2, ev_k1: tr_k1}.get(f)
+            return (m,) + key(step)[1:] + ((a[3],) if f is ev_plane else ()) + (pool,) if m else None
 
-        for s in v_tail[:V_AHEAD]:
-            tensor += maker(s, "v")
-        tensor += [(tr_k1, 6, "a"), (tr_k1, 7, "a")]
-        k = 0
-        for n, run in enumerate(runs):
-            s_queue = [m for s in units[n] for m in maker(s, "a")] if n < len(units) else []
-            for pos in range(len(run)):
-                if pos >= S_FROM[n]:
-                    tensor += s_queue[:1]
-                    s_queue = s_queue[1:]
-                for s in v_tail[k + V_AHEAD : k + V_AHEAD + 1]:
-                    tensor += maker(s, "v")
-                k = k + 1
-        vector += v_tail
-        scalar += [s for unit in units for s in unit]
+        def length(step):
+            if step[0] is interleave:
+                return IL
+            if step[0] is ev_plane:
+                return step[4] / NB
+            if step[0] is q_h or step[0] is q_k1 or step[0] is q_k2 and step[2] - step[1] == 2:
+                return 2
+            return 1
 
         def needs(step):
             f, a = step[0], step[1:]
+            if f is widen and a[0] >= 2:
+                return [(q_d, 1) if a[0] == 2 else (q_k2, 1, 2)]
             if f is tr_k2:
                 return [(widen,) + a[:2]]
             if f is ev_k2:
-                return [(tr_k2, a[0], a[1] // 2)] + ([(q_k2, a[0] - 2)] if a[0] >= 2 else [])
+                return [(tr_k2, a[0], a[1] // 2)]
             if f is q_k2:
-                return [(ev_k2, a[0], r) for r in range(4)]
+                return [(ev_k2, b, r) for b in range(a[0], a[1]) for r in range(4)]
             if f is ev_d:
                 return [(tr_d,) + a[:2]]
             if f is q_d:
@@ -343,7 +356,7 @@ def tile_nmr_relaxometry_residual_s7_kernel(tc, k1, dist, k2_bytes, k2_scale, po
             if f is q_k1:
                 return [(ev_k1, i) for i in range(a[0], a[1])]
             if f is mm1_quarter or f is mm1_plane:
-                return [(q_k2, a[0]), (q_d, a[1])]
+                return [[s for s in vector if s[0] is q_k2 and s[1] <= a[0] < s[2]][0], (q_d, a[1])]
             if f is ev_quarter:
                 return [(mm1_quarter,) + a, (pol_f32,)] + ([(q_h, a[0] - 2, 1)] if a[0] >= 2 else [])
             if f is ev_plane:
@@ -359,46 +372,69 @@ def tile_nmr_relaxometry_residual_s7_kernel(tc, k1, dist, k2_bytes, k2_scale, po
                 n = a[0] * ITILES + a[1] - RES_BUFS
                 return [(mm2,) + a] + ([(store,) + divmod(n, ITILES)] if n >= 0 else [])
             if f is mul:
-                return [(sub,) + a[:2], (copy_wt, a[0] // 2) if a[2] == "G" else (spread_wt, a[0] // 2, "w")]
+                return [(sub,) + a[:2]] + ([] if a[2] == "G" else [(spread_wt, a[0] // 2, "w")])
             if f is store:
                 return [(mul,) + a[:2]]
-            if f is copy_wt:
-                return [(spread_wt,) + a]
             if step == (spread_wt, 1, "w"):
-                return [(copy_wt, 0)] + [(mul, 1, i) for i in v_tiles(1)] + [(mul, 0, i) for i in v_tiles(0)]
+                return [(mul, 1, i) for i in v_tiles(1)] + [(mul, 0, i) for i in v_tiles(0)]
             return []
 
         def key(step):
-            n = {widen: 2, ev_d: 2, tr_d: 2, tr_k2: 2, tr_k1: 1, ev_k1: 1, mm1_plane: 3, ev_plane: 3, interleave: 3, mul: 2, q_h: 2, mm2: 2, mm1_quarter: 3, copy_wt: 1}
+            n = {widen: 2, ev_d: 2, tr_d: 2, tr_k2: 2, tr_k1: 1, ev_k1: 1, mm1_plane: 3, ev_plane: 3, interleave: 3, mul: 2, q_h: 2, mm2: 2, mm1_quarter: 3}
             return step[: 1 + n.get(step[0], len(step))]
 
         def readers(step):
             f, a = step[0], step[1:]
             if f is tr_k2:
                 return [(ev_k2, a[0], 2 * a[1]), (ev_k2, a[0], 2 * a[1] + 1)]
-            if f is spread_wt:
-                return [(copy_wt, a[0])]
             return [({tr_d: ev_d, tr_k1: ev_k1, mm1_quarter: ev_quarter, mm1_plane: ev_plane, mm2: sub}[f],) + key(step)[1:]]
 
         def v_tiles(b):
             return [s[2] for s in vector if s[0] is mul and s[1] == b]
 
         h_writers = {b: [key(s) for s in vector + scalar if s[0] in (ev_quarter, interleave) and s[1] == b] for b in range(BLOCKS)}
-        extra, rings = {}, {"v": [], "a": []}
+
+        begin, end = {}, {}
+        for steps, t in ((v_rest, 0), (s_rest, S_SHIFT)):
+            for step in steps:
+                begin[key(step)] = t
+                t = t + length(step)
+                end[key(step)] = t
+        timed = []
+        for steps, pool, depth, lead in ((v_rest, "v", V_BANKS, V_LEAD), (s_rest, "a", A_BANKS, S_LEAD)):
+            ring = [s for s in tensor if s[-1] == pool]
+            t = -100
+            for step in steps:
+                made = maker(step, pool)
+                if made and made not in tensor:
+                    waits = needs(made) + (readers(ring[-depth - (pool == "a" and begin[key(step)] < W_AT)]) if len(ring) >= depth + 1 else [])
+                    t = max([t, begin[key(step)] - lead] + [end[w] for w in waits if w in end])
+                    timed.append((t, len(timed), made))
+                    ring.append(made)
+        timed.append((begin[key([s for s in v_rest if s[0] is mul][0])] - W_LEAD, len(timed), (spread_wt, 0, "w")))
+        w1 = (spread_wt, 1, "w")
+        timed.append((max(end[w] for w in needs(w1) if w in end), len(timed), w1))
+        tensor += [m for t, k, m in sorted(timed, key=lambda e: e[:2])]
+        extra, last_user, bank_of, free = {}, {}, {}, {"v": [0, 1, 2, 3], "a": [4, 5, 6, 7]}
         for step in tensor:
-            if step[-1] != "w":
-                ring = rings[step[-1]]
-                depth = {"v": V_BANKS, "a": A_BANKS}[step[-1]]
-                if len(ring) >= depth:
-                    extra[key(step)] = readers(ring[-depth])
-                ring.append(step)
+            if step[-1] == "w":
+                bank = 7
+                if bank in free["a"]:
+                    free["a"].remove(bank)
+            else:
+                bank = free[step[-1]].pop(0)
+                free[step[-1]].append(bank)
+            if bank in last_user and last_user[bank][-1] != "w":
+                extra[key(step)] = readers(last_user[bank])
+            last_user[bank] = step
+            bank_of[step] = bank
         done, queues = set(), [list(tensor), list(vector), list(scalar), list(gpsimd), list(sync)]
         while any(queues):
             moved = False
             for queue in queues:
                 while queue and all(n in done for n in needs(queue[0]) + extra.get(key(queue[0]), [])):
                     step = queue.pop(0)
-                    step[0](*step[1:])
+                    step[0](*(step[1:-1] + (bank_of[step],) if step in bank_of else step[1:]))
                     done.add(key(step))
                     moved = True
-            assert moved, [q[0] for q in queues if q]
+            assert moved, [q[0][1:] for q in queues if q]

@@ -14,427 +14,406 @@ U8 = mybir.dt.uint8
 FP8 = mybir.dt.float8_e4m3fn
 FP8X4 = mybir.dt.float8_e4m3fn_x4
 MULT = mybir.AluOpType.mult
-ADD = mybir.AluOpType.add
 SUB = mybir.AluOpType.subtract
 COPY = mybir.ActivationFunctionType.Copy
 
 P = 128
 NB = 512
+HALF = NB // 2
 BLOCKS = N2 // NB
-ITILES = N1 // P
+ROW_TILES = N1 // P
+TILES = BLOCKS * ROW_TILES
 GROUPS = J1 // 512
-
-V_BANKS = 4
-A_BANKS = 3
-RES_BUFS = 16
-V_LEAD = 3
-S_LEAD = 2
-S_SHIFT = 2
-IL = 2.4
-W_LEAD = 6
-W_AT = 32
+RESULT_BUFS = 16
+PLANE_BUFS = 5
+VECTOR_BANKS = (0, 1, 2, 3)
+SCALAR_BANKS = (4, 5, 6, 7)
+WT_BANK = 7
+SCALAR_LEAD = 1
 
 
 def tile_nmr_relaxometry_residual_s7_kernel(tc, k1, dist, k2_bytes, k2_scale, pol, data, wt, out):
     nc = tc.nc
     with ExitStack() as ctx:
         keep = ctx.enter_context(tc.tile_pool(name="keep", bufs=1))
-        wide = ctx.enter_context(tc.tile_pool(name="wide", bufs=2))
-        opool = ctx.enter_context(tc.tile_pool(name="opool", bufs=RES_BUFS))
-        ps_pool = ctx.enter_context(tc.psum_pool(name="ps", bufs=1))
+        turn = ctx.enter_context(tc.tile_pool(name="turn", bufs=2))
+        results = ctx.enter_context(tc.tile_pool(name="results", bufs=RESULT_BUFS))
+        psum = ctx.enter_context(tc.psum_pool(name="psum", bufs=1))
         ctx.enter_context(tc.manual_schedule())
 
         ident = keep.tile([P, P], F32, name="ident")
-        identb = keep.tile([P, BLOCKS], BF16, name="identb")
+        pick = keep.tile([P, BLOCKS], BF16, name="pick")
         wt_rows = keep.tile([P, NB], BF16, name="wt_rows")
-        wt_bc = keep.tile([P, N2], BF16, name="wt_bc")
-        ks = keep.tile([P, 4], F32, name="ks")
-        polb = keep.tile([P, 8], BF16, name="polb")
-        polf = keep.tile([P, 8], F32, name="polf")
-        kbytes, dsb, k1sb, dat = {}, {}, {}, {}
-        psum, k2w = {}, {}
-        kg = keep.tile([P, 4 * BLOCKS, P, 4], BF16, name="kg", align_bytes=64)
-        kcodes = keep.tile([P, N2], U32, name="kcodes", align_bytes=64)
-        kscales = keep.tile([P, N2], U8, name="kscales", align_bytes=64)
-        dg, dcodes, dscales = {}, {}, {}
-        k1g = keep.tile([P, 2 * ITILES, P, 4], BF16, name="k1g", align_bytes=64)
-        k1codes = keep.tile([P, 2 * ITILES * P], U32, name="k1codes", align_bytes=64)
-        k1scales = keep.tile([P, 2 * ITILES * P], U8, name="k1scales", align_bytes=64)
-        hp, hi, hcodes, hscales, res, wt_ps = {}, {}, {}, {}, {}, {}
+        wt_all = keep.tile([P, BLOCKS, NB], BF16, name="wt_all")
+        scale4 = keep.tile([P, 4], F32, name="scale4")
+        pol_bf = keep.tile([P, 4 * GROUPS], BF16, name="pol_bf")
+        pol4 = keep.tile([P, 4 * GROUPS], F32, name="pol4")
+        k2_grouped = keep.tile([P, 4 * BLOCKS, P, 4], BF16, name="k2_grouped", align_bytes=64)
+        k2_codes = keep.tile([P, N2], U32, name="k2_codes", align_bytes=64)
+        k2_scales = keep.tile([P, N2], U8, name="k2_scales", align_bytes=64)
+        k1_grouped = keep.tile([P, GROUPS * ROW_TILES, P, 4], BF16, name="k1_grouped", align_bytes=64)
+        k1_codes = keep.tile([P, GROUPS * N1], U32, name="k1_codes", align_bytes=64)
+        k1_scales = keep.tile([P, GROUPS * N1], U8, name="k1_scales", align_bytes=64)
+        k2_raw, k2_wide, dist_sb, k1_sb, data_sb = {}, {}, {}, {}, {}
+        dist_grouped, dist_codes, dist_scales = {}, {}, {}
+        planes, h_grouped, h_codes, h_scales, result, filled, wt_bank = {}, {}, {}, {}, {}, {}, {}
 
         def load_k2(b, h):
-            kbytes[b, h] = keep.tile([P, 2, J2], U8, name="kbytes%d_%d" % (b, h))
-            rows = k2_bytes[b * NB + h * 2 * P : b * NB + (h + 1) * 2 * P, :]
-            nc.sync.dma_start(out=kbytes[b, h][:], in_=rows.rearrange("(r p) l -> p r l", p=P))
+            k2_raw[b, h] = keep.tile([P, 2, J2], U8, name="k2_raw%d_%d" % (b, h))
+            rows = k2_bytes[b * NB + h * HALF : b * NB + (h + 1) * HALF, :]
+            nc.sync.dma_start(out=k2_raw[b, h][:], in_=rows.rearrange("(r p) l -> p r l", p=P))
 
         def load_dist(g, h):
-            dsb[g, h] = keep.tile([P, 2 * J2], BF16, name="dsb%d_%d" % (g, h))
+            dist_sb[g, h] = keep.tile([P, 2 * J2], BF16, name="dist_sb%d_%d" % (g, h))
             rows = dist[g * 512 : (g + 1) * 512, :].rearrange("(p t) l -> p (t l)", t=4)
-            nc.sync.dma_start(out=dsb[g, h][:], in_=rows[:, h * 2 * J2 : (h + 1) * 2 * J2])
+            nc.sync.dma_start(out=dist_sb[g, h][:], in_=rows[:, h * 2 * J2 : (h + 1) * 2 * J2])
 
         def load_k1(i):
-            k1sb[i] = keep.tile([P, J1], BF16, name="k1sb%d" % i)
-            nc.sync.dma_start(out=k1sb[i][:], in_=k1[i * P : (i + 1) * P, :])
+            k1_sb[i] = keep.tile([P, J1], BF16, name="k1_sb%d" % i)
+            nc.sync.dma_start(out=k1_sb[i][:], in_=k1[i * P : (i + 1) * P, :])
 
         def load_data(b, h):
-            dat[b, h] = keep.tile([P, 4, NB], BF16, name="dat%d_%d" % (b, h))
-            nc.sync.dma_start(
-                out=dat[b, h][:],
-                in_=data[h * 512 : (h + 1) * 512, b * NB : (b + 1) * NB].rearrange("(i p) m -> p i m", p=P),
-            )
-
-        def copy_on(eng, dst, src):
-            if eng == "S":
-                nc.scalar.copy(out=dst, in_=src)
-            elif eng == "G":
-                nc.gpsimd.tensor_copy(out=dst, in_=src)
-            else:
-                nc.vector.tensor_copy(out=dst, in_=src)
-
-        def spread_wt(pair, pool):
-            wt_ps[pair] = ps_pool.tile([P, 2, NB], BF16, name="bank%d" % pool)
-            for e in (0, 1):
-                b = 2 * pair + e
-                nc.tensor.matmul(wt_ps[pair][:, e, :], lhsT=identb[:, b : b + 1].to_broadcast([P, P]), rhs=wt_rows[:], start=True, stop=True)
+            data_sb[b, h] = keep.tile([P, 4, NB], BF16, name="data_sb%d_%d" % (b, h))
+            rows = data[h * 512 : (h + 1) * 512, b * NB : (b + 1) * NB]
+            nc.sync.dma_start(out=data_sb[b, h][:], in_=rows.rearrange("(i p) m -> p i m", p=P))
 
         def load_wt(b):
-            nc.sync.dma_start(out=wt_bc[:, b * NB : (b + 1) * NB], in_=wt[b * NB : (b + 1) * NB].partition_broadcast(P))
+            nc.sync.dma_start(out=wt_all[:, b, :], in_=wt[b * NB : (b + 1) * NB].partition_broadcast(P))
 
-        def pol_f32():
-            nc.scalar.activation(out=polf[:], in_=polb[:], func=COPY)
+        def new_bank(bank, shape, dtype):
+            return psum.tile(shape, dtype, name="bank%d" % bank)
 
-        def widen(b, h, eng):
-            if b < 2:
-                k2w[b, h] = wide.tile([P, 2 * J2], BF16, name="k2w", bufs=4)
-            elif b == 3:
-                k2w[b, h] = kg[:, 4 + 2 * h : 6 + 2 * h].rearrange("p a n e -> p (a n e)")
-            else:
-                k2w[b, h] = dg[3 - b][:, 2 * h : 2 * h + 2].rearrange("p a n e -> p (a n e)")
-            copy_on(eng, k2w[b, h][:], kbytes[b, h][:].rearrange("p r l -> p (r l)").bitcast(FP8))
-
-        def word_transposes(key, pool, tile):
-            ps = ps_pool.tile([P, 2, 2, P], F32, name="bank%d" % pool)
-            psum[key] = ps
-            words = tile[:].bitcast(F32)
+        def turn_words(name, rows, bank):
+            filled[name] = new_bank(bank, [P, 2, 2, P], F32)
+            words = rows.bitcast(F32)
             for a in (0, 1):
                 for u in (0, 1):
-                    nc.tensor.transpose(ps[:, a, u, :], words[:, 256 * a + u : 256 * (a + 1) : 2], ident[:])
+                    nc.tensor.transpose(filled[name][:, a, u, :], words[:, 256 * a + u : 256 * (a + 1) : 2], ident[:])
 
-        def tr_k2(b, h, pool):
-            word_transposes(("k2", b, h), pool, k2w[b, h])
+        def turn_k2(b, h, bank):
+            turn_words(("k2", b, h), k2_wide[b, h], bank)
 
-        def ev_k2(b, r):
-            src = psum["k2", b, r // 2][:, r % 2].rearrange("p u n -> p (u n)").bitcast(BF16).rearrange("p (u n e) -> p n u e", u=2, e=2)
-            nc.vector.tensor_tensor(
-                out=kg[:, 4 * b + r].rearrange("p n (u e) -> p n u e", u=2),
-                in0=src,
-                in1=ks[:].rearrange("p (o u e) -> p o u e", o=1, u=2).to_broadcast([P, P, 2, 2]),
-                op=MULT,
+        def turn_dist(g, h, bank):
+            turn_words(("dist", g, h), dist_sb[g, h][:], bank)
+
+        def turn_k1(i, bank):
+            turn_words(("k1", i), k1_sb[i][:], bank)
+
+        def mx(dst, lhs_codes, lhs_scales, rhs_codes, rhs_scales, start, stop):
+            nc.tensor.matmul_mx(
+                out=dst,
+                lhsT=lhs_codes.bitcast(FP8X4),
+                lhsT_scale=lhs_scales,
+                rhs=rhs_codes.bitcast(FP8X4),
+                rhs_scale=rhs_scales,
+                start=start,
+                stop=stop,
             )
 
-        def q_k2(lo, up):
-            nc.vector.quantize_mx(
-                out=kcodes[:, lo * NB : up * NB].bitcast(FP8X4),
-                scales=kscales[:, lo * NB : up * NB],
-                in_=kg[:, 4 * lo : 4 * up].rearrange("p r m e -> p (r m e)"),
-            )
-
-        def tr_d(g, h, pool):
-            word_transposes(("d", g, h), pool, dsb[g, h])
-
-        def ev_words(key, tile, eng):
-            dst = tile.rearrange("p a n e -> p (a n e)").bitcast(F32).rearrange("p (a n u) -> p a n u", a=2, u=2)
-            copy_on(eng, dst, psum[key][:].rearrange("p a u n -> p a n u"))
-
-        def ev_d(g, h, eng):
-            if h == 0:
-                dg[g] = keep.tile([P, 4, P, 4], BF16, name="dg%d" % g, align_bytes=64)
-            ev_words(("d", g, h), dg[g][:, 2 * h : 2 * h + 2], eng)
-
-        def q_d(g):
-            dcodes[g] = keep.tile([P, 512], U32, name="dcodes%d" % g, align_bytes=64)
-            dscales[g] = keep.tile([P, 512], U8, name="dscales%d" % g, align_bytes=64)
-            nc.vector.quantize_mx(out=dcodes[g][:].bitcast(FP8X4), scales=dscales[g][:], in_=dg[g][:].rearrange("p r m e -> p (r m e)"))
-
-        def tr_k1(i, pool):
-            word_transposes(("k1", i), pool, k1sb[i])
-
-        def ev_k1(i, eng):
-            ev_words(("k1", i), k1g[:, 2 * i : 2 * i + 2], eng)
-
-        def q_k1(lo, up):
-            nc.vector.quantize_mx(
-                out=k1codes[:, lo * 256 : up * 256].bitcast(FP8X4),
-                scales=k1scales[:, lo * 256 : up * 256],
-                in_=k1g[:, 2 * lo : 2 * up].rearrange("p a m e -> p (a m e)"),
-            )
-
-        def h_tile(b, g):
-            if b not in hi:
-                hi[b] = wide.tile([P, GROUPS, NB, 4], BF16, name="hi", align_bytes=64)
-            return hi[b][:, g]
-
-        def mx(dst, lc, ls, rc, rs, start=True, stop=True):
-            nc.tensor.matmul_mx(out=dst, lhsT=lc.bitcast(FP8X4), lhsT_scale=ls, rhs=rc.bitcast(FP8X4), rhs_scale=rs, start=start, stop=stop)
-
-        def mm1_quarter(b, g, q, pool):
-            ps = ps_pool.tile([P, 4, P], F32, name="bank%d" % pool)
-            psum["gq", b, g, q] = ps
+        def g_quarter(b, g, q, bank):
+            filled["quarter", b, g, q] = new_bank(bank, [P, 4, P], F32)
             m = slice(b * NB + q * P, b * NB + (q + 1) * P)
             for t in range(4):
                 j = slice(t * P, (t + 1) * P)
-                mx(ps[:, t, :], dcodes[g][:, j], dscales[g][:, j], kcodes[:, m], kscales[:, m])
+                mx(filled["quarter", b, g, q][:, t, :], dist_codes[g][:, j], dist_scales[g][:, j], k2_codes[:, m], k2_scales[:, m], True, True)
 
-        def ev_quarter(b, g, q):
+        def g_plane(b, g, t, bank):
+            filled["plane", b, g, t] = new_bank(bank, [P, NB], F32)
+            j, m = slice(t * P, (t + 1) * P), slice(b * NB, (b + 1) * NB)
+            mx(filled["plane", b, g, t][:], dist_codes[g][:, j], dist_scales[g][:, j], k2_codes[:, m], k2_scales[:, m], True, True)
+
+        def signal(n, bank):
+            b, i = divmod(n, ROW_TILES)
+            filled["signal", n] = new_bank(bank, [P, NB], F32)
+            for g in range(GROUPS):
+                c, m = slice((GROUPS * i + g) * P, (GROUPS * i + g + 1) * P), slice(g * NB, (g + 1) * NB)
+                mx(filled["signal", n][:], k1_codes[:, c], k1_scales[:, c], h_codes[b][:, m], h_scales[b][:, m], g == 0, g == GROUPS - 1)
+
+        def spread_wt(pair, bank):
+            wt_bank[pair] = new_bank(bank, [P, 2, NB], BF16)
+            for e in (0, 1):
+                b = 2 * pair + e
+                nc.tensor.matmul(wt_bank[pair][:, e, :], lhsT=pick[:, b : b + 1].to_broadcast([P, P]), rhs=wt_rows[:], start=True, stop=True)
+
+        def flat(grouped):
+            return grouped.rearrange("p a n t -> p (a n t)")
+
+        def widen(b, h, copy):
+            if b < 2:
+                wide = turn.tile([P, 2 * J2], BF16, name="wide", bufs=4)
+                k2_wide[b, h] = wide[:]
+            elif b == 2:
+                k2_wide[b, h] = flat(dist_grouped[1][:, 2 * h : 2 * h + 2])
+            else:
+                k2_wide[b, h] = flat(k2_grouped[:, 4 + 2 * h : 6 + 2 * h])
+            copy(out=k2_wide[b, h], in_=k2_raw[b, h][:].rearrange("p r l -> p (r l)").bitcast(FP8))
+
+        def scale_k2(b, r):
+            words = filled["k2", b, r // 2][:, r % 2].rearrange("p u n -> p (u n)")
             nc.vector.tensor_tensor(
-                out=h_tile(b, g)[:, q * P : (q + 1) * P, :],
-                in0=psum["gq", b, g, q][:].rearrange("p t n -> p n t"),
-                in1=polf[:, 4 * g : 4 * g + 4].rearrange("p (o t) -> p o t", o=1).to_broadcast([P, P, 4]),
+                out=k2_grouped[:, 4 * b + r].rearrange("p n (u e) -> p n u e", u=2),
+                in0=words.bitcast(BF16).rearrange("p (u n e) -> p n u e", u=2, e=2),
+                in1=scale4[:].rearrange("p (o u e) -> p o u e", o=1, u=2).to_broadcast([P, P, 2, 2]),
                 op=MULT,
             )
 
-        def mm1_plane(b, g, t, w, pool):
-            ps = ps_pool.tile([P, NB], F32, name="bank%d" % pool)
-            psum["g", b, g, t] = ps
-            j = slice(t * P, (t + 1) * P)
-            mx(ps[:, :w], dcodes[g][:, j], dscales[g][:, j], kcodes[:, b * NB : b * NB + w], kscales[:, b * NB : b * NB + w])
+        def group_words(name, grouped):
+            dst = flat(grouped).bitcast(F32).rearrange("p (a n u) -> p a n u", a=2, u=2)
+            nc.scalar.copy(out=dst, in_=filled[name][:].rearrange("p a u n -> p a n u"))
 
-        def ev_plane(b, g, t, w=NB):
-            if t == 0:
-                hp[b, g] = wide.tile([P, 4, NB], BF16, name="hp", align_bytes=64, bufs=5)
-            nc.scalar.activation(out=hp[b, g][:, t, :w], in_=psum["g", b, g, t][:, :w], func=COPY, scale=polf[:, 4 * g + t : 4 * g + t + 1])
+        def group_dist(g, h):
+            if h == 0:
+                dist_grouped[g] = keep.tile([P, 4, P, 4], BF16, name="dist_grouped%d" % g, align_bytes=64)
+            group_words(("dist", g, h), dist_grouped[g][:, 2 * h : 2 * h + 2])
 
-        def interleave(b, g, lo, up, eng="S"):
-            dst = h_tile(b, g)[:, lo:up, :].rearrange("p (c i) t -> p c t i", i=4)
-            src = hp[b, g][:, :, lo:up].rearrange("p t (c i) -> p c t i", i=4)
-            copy_on(eng, dst, src)
+        def group_k1(i):
+            group_words(("k1", i), k1_grouped[:, GROUPS * i : GROUPS * (i + 1)])
 
-        def q_h(b, last, lo):
-            up = last + 1
-            if lo == 0:
-                hcodes[b] = wide.tile([P, GROUPS, NB], U32, name="hcodes", align_bytes=64)
-                hscales[b] = wide.tile([P, GROUPS, NB], U8, name="hscales", align_bytes=64)
-            nc.vector.quantize_mx(
-                out=hcodes[b][:, lo:up].rearrange("p g n -> p (g n)").bitcast(FP8X4),
-                scales=hscales[b][:, lo:up].rearrange("p g n -> p (g n)"),
-                in_=hi[b][:, lo:up].rearrange("p g n t -> p (g n t)"),
+        def pol_to_f32():
+            nc.scalar.activation(out=pol4[:], in_=pol_bf[:], func=COPY)
+
+        def h_columns(b, g, lo, up):
+            if b not in h_grouped:
+                h_grouped[b] = turn.tile([P, GROUPS * NB, 4], BF16, name="h_grouped", align_bytes=64)
+            return h_grouped[b][:, g * NB + lo : g * NB + up, :]
+
+        def h_quarter(b, g, q):
+            nc.vector.tensor_tensor(
+                out=h_columns(b, g, q * P, (q + 1) * P),
+                in0=filled["quarter", b, g, q][:].rearrange("p t n -> p n t"),
+                in1=pol4[:, 4 * g : 4 * g + 4].rearrange("p (o t) -> p o t", o=1).to_broadcast([P, P, 4]),
+                op=MULT,
             )
 
-        def mm2(b, i, pool):
-            ps = ps_pool.tile([P, NB], F32, name="bank%d" % pool)
-            psum["s", b, i] = ps
-            for g in range(GROUPS):
-                c = slice((2 * i + g) * P, (2 * i + g + 1) * P)
-                mx(ps[:], k1codes[:, c], k1scales[:, c], hcodes[b][:, g], hscales[b][:, g], g == 0, g == GROUPS - 1)
+        def h_plane(b, g, t):
+            if t == 0:
+                planes[b, g] = turn.tile([P, 4, NB], BF16, name="planes", align_bytes=64, bufs=PLANE_BUFS)
+            nc.scalar.activation(out=planes[b, g][:, t, :], in_=filled["plane", b, g, t][:], func=COPY, scale=pol4[:, 4 * g + t : 4 * g + t + 1])
 
-        def sub(b, i):
-            res[b, i] = opool.tile([P, NB], F32, name="res")
-            nc.vector.tensor_tensor(out=res[b, i][:], in0=psum["s", b, i][:], in1=dat[b, i // 4][:, i % 4, :], op=SUB)
+        def group_planes(b, g, h):
+            lo, up = h * HALF, (h + 1) * HALF
+            dst = h_columns(b, g, lo, up).rearrange("p (c i) t -> p c t i", i=4)
+            nc.scalar.copy(out=dst, in_=planes[b, g][:, :, lo:up].rearrange("p t (c i) -> p c t i", i=4))
 
-        def mul(b, i, eng):
-            if eng == "V":
-                nc.vector.tensor_tensor(out=res[b, i][:], in0=res[b, i][:], in1=wt_ps[b // 2][:, b % 2, :], op=MULT)
-            else:
-                nc.gpsimd.tensor_tensor(out=res[b, i][:], in0=res[b, i][:], in1=wt_bc[:, b * NB : (b + 1) * NB], op=MULT)
+        def quantise(codes, scales, grouped):
+            nc.vector.quantize_mx(out=codes.bitcast(FP8X4), scales=scales, in_=grouped)
 
-        def store(b, i):
-            nc.sync.dma_start(out=out[i * P : (i + 1) * P, b * NB : (b + 1) * NB], in_=res[b, i][:])
+        def q_k2(b):
+            m = slice(b * NB, (b + 1) * NB)
+            quantise(k2_codes[:, m], k2_scales[:, m], flat(k2_grouped[:, 4 * b : 4 * b + 4]))
+
+        def q_dist(g):
+            dist_codes[g] = keep.tile([P, 512], U32, name="dist_codes%d" % g, align_bytes=64)
+            dist_scales[g] = keep.tile([P, 512], U8, name="dist_scales%d" % g, align_bytes=64)
+            quantise(dist_codes[g][:], dist_scales[g][:], flat(dist_grouped[g][:]))
+
+        def q_k1(h):
+            c = slice(h * N1, (h + 1) * N1)
+            quantise(k1_codes[:, c], k1_scales[:, c], flat(k1_grouped[:, h * ROW_TILES : (h + 1) * ROW_TILES]))
+
+        def q_h(b):
+            h_codes[b] = turn.tile([P, GROUPS * NB], U32, name="h_codes", align_bytes=64)
+            h_scales[b] = turn.tile([P, GROUPS * NB], U8, name="h_scales", align_bytes=64)
+            quantise(h_codes[b][:], h_scales[b][:], h_grouped[b][:].rearrange("p n t -> p (n t)"))
+
+        def subtract(n):
+            b, i = divmod(n, ROW_TILES)
+            result[n] = results.tile([P, NB], F32, name="result")
+            nc.vector.tensor_tensor(out=result[n][:], in0=filled["signal", n][:], in1=data_sb[b, i // 4][:, i % 4, :], op=SUB)
+
+        def weigh_vector(n):
+            b = n // ROW_TILES
+            nc.vector.tensor_tensor(out=result[n][:], in0=result[n][:], in1=wt_bank[b // 2][:, b % 2, :], op=MULT)
+
+        def weigh_gpsimd(n):
+            nc.gpsimd.tensor_tensor(out=result[n][:], in0=result[n][:], in1=wt_all[:, n // ROW_TILES, :], op=MULT)
+
+        def store(n):
+            b, i = divmod(n, ROW_TILES)
+            nc.sync.dma_start(out=out[i * P : (i + 1) * P, b * NB : (b + 1) * NB], in_=result[n][:])
 
         make_identity(nc, ident[:])
         nc.vector.memset(wt_rows[:].bitcast(I32), 0)
-        nc.vector.tensor_copy(out=identb[:], in_=ident[:, 0:BLOCKS])
+        nc.vector.tensor_copy(out=pick[:], in_=ident[:, 0:BLOCKS])
 
         load_k2(0, 0)
         load_k2(0, 1)
-        nc.sync.dma_start(out=ks[:], in_=k2_scale.rearrange("o (p c) -> p (o c)", c=4))
-        load_dist(0, 0)
-        load_k2(1, 0)
-        load_dist(0, 1)
-        load_k2(1, 1)
+        nc.sync.dma_start(out=scale4[:], in_=k2_scale.rearrange("o (p t) -> p (o t)", t=4))
+        for h in (0, 1):
+            load_dist(0, h)
+            load_k2(1, h)
         load_dist(1, 0)
         load_dist(1, 1)
         nc.sync.dma_start(out=wt_rows[0:BLOCKS, :], in_=wt.rearrange("(b m) -> b m", b=BLOCKS))
-        nc.sync.dma_start(out=polb[:].rearrange("p (g t) -> p g t", t=4), in_=pol.rearrange("(g p t) -> p g t", p=P, t=4))
-        load_k2(2, 0)
-        load_k2(2, 1)
-        load_k1(0)
-        load_k1(1)
-        load_k2(3, 0)
-        load_k2(3, 1)
-        load_k1(2)
-        load_k1(3)
-        load_k1(4)
-        load_k1(5)
-        load_k1(6)
-        load_k1(7)
+        nc.sync.dma_start(out=pol_bf[:].rearrange("p (g t) -> p g t", t=4), in_=pol.rearrange("(g p t) -> p g t", p=P, t=4))
+        for b in (2, 3):
+            load_k2(b, 0)
+            load_k2(b, 1)
+            load_k1(2 * b - 4)
+            load_k1(2 * b - 3)
+        for i in range(4, ROW_TILES):
+            load_k1(i)
         load_data(0, 0)
         load_wt(0)
         load_data(0, 1)
-        load_wt(1)
-        load_data(1, 0)
-        load_data(1, 1)
-        load_wt(2)
-        load_data(2, 0)
-        load_data(2, 1)
-        load_wt(3)
-        load_data(3, 0)
-        load_data(3, 1)
+        for b in range(1, BLOCKS):
+            load_wt(b)
+            load_data(b, 0)
+            load_data(b, 1)
 
-        HALF = NB // 2
+        def steps(f, *heads, count):
+            return [(f,) + heads + (k,) for k in range(count)]
 
-        def s_(n):
-            return (sub,) + divmod(n, ITILES)
+        def among(tiles, fillers):
+            return [s for k, n in enumerate(tiles) for s in fillers[2 * k : 2 * k + 2] + [(subtract, n)]]
 
-        def m_(n):
-            return (mul,) + divmod(n, ITILES) + ("V",)
+        def five(first):
+            subs = [(subtract, n) for n in range(first, first + 5)]
+            return subs[:4] + [(weigh_vector, first + 1), (weigh_vector, first + 3)] + subs[4:]
 
-        def e_(b, r):
-            return (ev_k2, b, r)
+        def alternate(first, last):
+            order = [(subtract, first)]
+            for n in range(first + 1, last, 2):
+                order.extend([(subtract, n), (subtract, n + 1), (weigh_vector, n)])
+            return order + [(subtract, last), (weigh_vector, last)]
 
-        def h_(b, q, g=1):
-            return (ev_quarter, b, g, q)
+        def group(b, g):
+            return steps(h_plane, b, g, count=4) + steps(group_planes, b, g, count=2)
 
-        groups = [(0,0,512),(1,0,512),(2,0,512),(2,1,512),(3,0,512),(3,1,512)]
-        units = [[(ev_plane, b, g, t, w) for t in range(4)] + [(interleave, b, g, lo, lo + HALF) for lo in range(0, w, HALF)] for b, g, w in groups]
-        k1e = [(ev_k1, i, "S") for i in range(ITILES)]
-        v_first = [(widen, 0, 0, "V")] + [(ev_k2, 0, r) for r in range(4)] + [(q_d, 0), (q_k2, 0, 1)]
-        s_first = [(widen, 0, 1, "S"), (ev_d, 0, 0, "S"), (ev_d, 0, 1, "S"), (ev_d, 1, 0, "S"), (ev_d, 1, 1, "S"), (pol_f32,)]
-        tensor = [(tr_k2, 0, 0, "v"), (tr_d, 0, 0, "a"), (tr_k2, 0, 1, "v"), (tr_d, 0, 1, "a"), (tr_k2, 1, 0, "v"), (tr_d, 1, 0, "a"), (tr_d, 1, 1, "a"), (tr_k2, 1, 1, "v")]
-        tensor += [(mm1_plane, 0, 0, t, NB, "a") for t in range(4)] + [(mm1_quarter, 0, 1, q, "v") for q in range(4)]
-        tensor += [(tr_k1, 0, "a"), (tr_k1, 1, "a"), (tr_k2, 2, 0, "v")]
-        v_rest = [e_(1, 0), e_(1, 1), (q_d, 1), e_(1, 2), e_(1, 3)] + [h_(0, q) for q in range(3)] + [(q_k2, 1, 2), h_(0, 3)]
-        v_rest += [e_(2, r) for r in range(4)] + [(q_k2, 2, 3), (q_k1, 0, 4), (q_h, 0, 1, 0)]
-        s_rest = units[0][:4] + k1e[:2] + units[0][4:5] + k1e[2:4] + units[0][5:]
-        s_rest += k1e[4:] + [s for u in units[1:] for s in u]
-        runs = [
-            [h_(1, 0), h_(1, 1), s_(0), h_(1, 2), h_(1, 3), s_(1), (q_k1, 4, 8)],
-            [e_(3, 0), e_(3, 1), s_(2), e_(3, 2), e_(3, 3), s_(3), (q_h, 1, 1, 0)],
-            [s_(4), s_(5), s_(6), s_(7), m_(5), m_(7), s_(8), (q_k2, 3, 4)],
-            [s_(9), s_(10), s_(11), s_(12), m_(10), m_(12), s_(13), (q_h, 2, 1, 0)],
-            [s_(14), s_(15), s_(16), s_(17), m_(16), m_(17), s_(18), s_(19), s_(20), m_(19), s_(21), (q_h, 3, 1, 0)],
-            [s_(22), s_(23), s_(24), m_(23), s_(25), s_(26), m_(25), s_(27), s_(28), m_(27), s_(29), s_(30), m_(29), s_(31), m_(31)],
+        k1_steps = steps(group_k1, count=ROW_TILES)
+        quarters = steps(h_quarter, 0, 1, count=4)
+        first_group, second_group = group(0, 0), group(1, 0)
+        woven = [s for pair in zip(k1_steps[4:], second_group[:4]) for s in pair]
+        crossing = [(subtract, n) for n in range(14, 18)] + [(weigh_vector, 16), (weigh_vector, 17)]
+        crossing = crossing + [(subtract, n) for n in range(18, 21)] + [(weigh_vector, 19), (subtract, 21)]
+        opening = (
+            [(widen, 0, 0, nc.vector.tensor_copy)] + steps(scale_k2, 0, count=4) + [(q_dist, 0), (q_k2, 0)] + steps(scale_k2, 1, count=2) + [(q_dist, 1)],
+            [(widen, 0, 1, nc.scalar.copy)] + steps(group_dist, 0, count=2) + steps(group_dist, 1, count=2) + [(pol_to_f32,)],
+        )
+        phases = [
+            (steps(scale_k2, 1, count=4)[2:] + quarters[:3] + [(q_k2, 1)], first_group[:4] + k1_steps[:2]),
+            (quarters[3:] + steps(scale_k2, 2, count=4), first_group[4:5] + k1_steps[2:4] + first_group[5:]),
+            ([(q_k2, 2), (q_k1, 0), (q_h, 0)], woven[:4]),
+            (among((0, 1), steps(h_quarter, 1, 1, count=4)) + [(q_k1, 1)], woven[4:] + second_group[4:]),
+            (among((2, 3), steps(scale_k2, 3, count=4)) + [(q_h, 1)], group(2, 0)),
+            (five(4) + [(q_k2, 3)], group(2, 1)),
+            (five(9) + [(q_h, 2)], group(3, 0)),
+            (crossing + [(q_h, 3)], group(3, 1)),
+            (alternate(22, TILES - 1), []),
         ]
-        v_rest += [s for run in runs for s in run]
-        vector, scalar = v_first + v_rest, s_first + s_rest
-        on_v = [s[1:3] for s in vector if s[0] is mul]
-        gpsimd = [(widen, b, h, "G") for b in range(1, BLOCKS) for h in (0, 1)]
-        gpsimd += [(mul, b, i, "G") for b in range(BLOCKS) for i in range(ITILES) if (b, i) not in on_v]
-        sync = [(store, b, i) for b in range(BLOCKS) for i in range(ITILES)]
+        on_vector = [s[1] for v, a in phases for s in v if s[0] is weigh_vector]
+        h_writers = {b: [s for v, a in phases for s in v + a if s[0] in (h_quarter, group_planes) and s[1] == b] for b in range(BLOCKS)}
+        refill_after = {(h_plane, 2, 0, 3): 0, (weigh_vector, 12): 1}
 
-        def maker(step, pool):
-            f, a = step[0], step[1:]
-            if f is ev_k2:
-                return (tr_k2, a[0], a[1] // 2, pool) if a[1] % 2 == 0 else None
-            m = {ev_quarter: mm1_quarter, ev_plane: mm1_plane, sub: mm2, ev_k1: tr_k1}.get(f)
-            return (m,) + key(step)[1:] + ((a[3],) if f is ev_plane else ()) + (pool,) if m else None
+        maker = {scale_k2: turn_k2, group_dist: turn_dist, group_k1: turn_k1, h_quarter: g_quarter, h_plane: g_plane, subtract: signal}
 
-        def length(step):
-            if step[0] is interleave:
-                return IL
-            if step[0] is ev_plane:
-                return step[4] / NB
-            if step[0] is q_h or step[0] is q_k1 or step[0] is q_k2 and step[2] - step[1] == 2:
-                return 2
-            return 1
+        def made_by(step):
+            if step[0] is scale_k2:
+                return (turn_k2, step[1], step[2] // 2)
+            return (maker[step[0]],) + step[1:]
+
+        def fills(mine):
+            order = []
+            for step in mine:
+                if step[0] in maker and made_by(step) not in order + waiting["opening"]:
+                    order.append(made_by(step))
+            return order
 
         def needs(step):
             f, a = step[0], step[1:]
-            if f is widen and a[0] >= 2:
-                return [(q_d, 1) if a[0] == 2 else (q_k2, 1, 2)]
-            if f is tr_k2:
-                return [(widen,) + a[:2]]
-            if f is ev_k2:
-                return [(tr_k2, a[0], a[1] // 2)]
+            h_free = [(q_h, a[0] - 2)] if f in (h_quarter, group_planes) and a[0] >= 2 else []
+            if f is widen:
+                return {2: [(q_dist, 1)], 3: [(q_k2, 1)]}.get(a[0], [])
+            if f is turn_k2:
+                return [(widen,) + a]
+            if f in (g_quarter, g_plane):
+                return [(q_k2, a[0]), (q_dist, a[1])]
+            if f is signal:
+                return [(q_h, a[0] // ROW_TILES), (q_k1, a[0] % ROW_TILES // 4)]
+            if f in (h_quarter, h_plane):
+                return [made_by(step), (pol_to_f32,)] + h_free
+            if f is subtract:
+                return [made_by(step)] + ([(store, a[0] - RESULT_BUFS)] if a[0] >= RESULT_BUFS else [])
+            if f in maker:
+                return [made_by(step)]
+            if f is group_planes:
+                return steps(h_plane, a[0], a[1], count=4) + h_free
             if f is q_k2:
-                return [(ev_k2, b, r) for b in range(a[0], a[1]) for r in range(4)]
-            if f is ev_d:
-                return [(tr_d,) + a[:2]]
-            if f is q_d:
-                return [(ev_d, a[0], h) for h in (0, 1)]
-            if f is ev_k1:
-                return [(tr_k1, a[0])]
+                return steps(scale_k2, a[0], count=4)
+            if f is q_dist:
+                return steps(group_dist, a[0], count=2)
             if f is q_k1:
-                return [(ev_k1, i) for i in range(a[0], a[1])]
-            if f is mm1_quarter or f is mm1_plane:
-                return [[s for s in vector if s[0] is q_k2 and s[1] <= a[0] < s[2]][0], (q_d, a[1])]
-            if f is ev_quarter:
-                return [(mm1_quarter,) + a, (pol_f32,)] + ([(q_h, a[0] - 2, 1)] if a[0] >= 2 else [])
-            if f is ev_plane:
-                return [(mm1_plane,) + a[:3], (pol_f32,)]
-            if f is interleave:
-                return [(ev_plane, a[0], a[1], t) for t in range(4)] + ([(q_h, a[0] - 2, 1)] if a[0] >= 2 else [])
+                return k1_steps[4 * a[0] : 4 * a[0] + 4]
             if f is q_h:
-                gs = range(a[2], a[1] + 1)
-                return [w for w in h_writers[a[0]] if w[2] in gs] + ([(mm2, a[0] - 2, ITILES - 1)] if a[0] >= 2 else [])
-            if f is mm2:
-                return [(q_h, a[0], 1), [s for s in vector if s[0] is q_k1 and s[1] <= a[1] < s[2]][0]]
-            if f is sub:
-                n = a[0] * ITILES + a[1] - RES_BUFS
-                return [(mm2,) + a] + ([(store,) + divmod(n, ITILES)] if n >= 0 else [])
-            if f is mul:
-                return [(sub,) + a[:2]] + ([] if a[2] == "G" else [(spread_wt, a[0] // 2, "w")])
+                return h_writers[a[0]] + ([(signal, ROW_TILES * (a[0] - 1) - 1)] if a[0] >= 2 else [])
+            if f is weigh_vector:
+                return [(subtract, a[0]), (spread_wt, a[0] // (2 * ROW_TILES))]
+            if f is weigh_gpsimd:
+                return [(subtract, a[0])]
             if f is store:
-                return [(mul,) + a[:2]]
-            if step == (spread_wt, 1, "w"):
-                return [(mul, 1, i) for i in v_tiles(1)] + [(mul, 0, i) for i in v_tiles(0)]
+                return [(weigh_vector if a[0] in on_vector else weigh_gpsimd, a[0])]
             return []
 
-        def key(step):
-            n = {widen: 2, ev_d: 2, tr_d: 2, tr_k2: 2, tr_k1: 1, ev_k1: 1, mm1_plane: 3, ev_plane: 3, interleave: 3, mul: 2, q_h: 2, mm2: 2, mm1_quarter: 3}
-            return step[: 1 + n.get(step[0], len(step))]
+        def banks_worth(step):
+            return 2 if step[0] in (group_planes, q_k1, q_h) else 1
 
-        def readers(step):
-            f, a = step[0], step[1:]
-            if f is tr_k2:
-                return [(ev_k2, a[0], 2 * a[1]), (ev_k2, a[0], 2 * a[1] + 1)]
-            return [({tr_d: ev_d, tr_k1: ev_k1, mm1_quarter: ev_quarter, mm1_plane: ev_plane, mm2: sub}[f],) + key(step)[1:]]
+        every = [s for v, a in [opening] + phases for s in v + a]
+        readers = {}
+        for step in every:
+            if step[0] in maker:
+                readers.setdefault(made_by(step), []).append(step)
+        waiting = {"opening": [(turn_k2, 0, 0), (turn_dist, 0, 0), (turn_k2, 0, 1), (turn_dist, 0, 1)]}
+        waiting["opening"].extend([(turn_k2, 1, 0), (turn_dist, 1, 0), (turn_dist, 1, 1), (turn_k2, 1, 1)])
+        waiting["for vector"] = fills([s for v, a in phases for s in v])
+        waiting["for scalar"] = fills([s for v, a in phases for s in a])
+        waiting["wt"] = []
+        waiting["gpsimd"] = [(widen, b, h, nc.gpsimd.tensor_copy) for b in range(1, BLOCKS) for h in (0, 1)]
+        waiting["gpsimd"].extend((weigh_gpsimd, n) for n in range(TILES) if n not in on_vector)
+        waiting["stores"] = steps(store, count=TILES)
+        vector_banks, scalar_banks, wt_banks = list(VECTOR_BANKS), list(SCALAR_BANKS), [WT_BANK]
+        banks_of = {turn_k2: vector_banks, g_quarter: vector_banks, signal: vector_banks, spread_wt: wt_banks}
+        banks_of.update({turn_dist: scalar_banks, turn_k1: scalar_banks, g_plane: scalar_banks})
+        written, last_fill = set(), {}
 
-        def v_tiles(b):
-            return [s[2] for s in vector if s[0] is mul and s[1] == b]
+        def ready(step):
+            before = last_fill.get(banks_of[step[0]][0]) if step[0] in banks_of else None
+            return all(s in written for s in needs(step[:3] if step[0] is widen else step) + readers.get(before, []))
 
-        h_writers = {b: [key(s) for s in vector + scalar if s[0] in (ev_quarter, interleave) and s[1] == b] for b in range(BLOCKS)}
-
-        begin, end = {}, {}
-        for steps, t in ((v_rest, 0), (s_rest, S_SHIFT)):
-            for step in steps:
-                begin[key(step)] = t
-                t = t + length(step)
-                end[key(step)] = t
-        timed = []
-        for steps, pool, depth, lead in ((v_rest, "v", V_BANKS, V_LEAD), (s_rest, "a", A_BANKS, S_LEAD)):
-            ring = [s for s in tensor if s[-1] == pool]
-            t = -100
-            for step in steps:
-                made = maker(step, pool)
-                if made and made not in tensor:
-                    waits = needs(made) + (readers(ring[-depth - (pool == "a" and begin[key(step)] < W_AT)]) if len(ring) >= depth + 1 else [])
-                    t = max([t, begin[key(step)] - lead] + [end[w] for w in waits if w in end])
-                    timed.append((t, len(timed), made))
-                    ring.append(made)
-        timed.append((begin[key([s for s in v_rest if s[0] is mul][0])] - W_LEAD, len(timed), (spread_wt, 0, "w")))
-        w1 = (spread_wt, 1, "w")
-        timed.append((max(end[w] for w in needs(w1) if w in end), len(timed), w1))
-        tensor += [m for t, k, m in sorted(timed, key=lambda e: e[:2])]
-        extra, last_user, bank_of, free = {}, {}, {}, {"v": [0, 1, 2, 3], "a": [4, 5, 6, 7]}
-        for step in tensor:
-            if step[-1] == "w":
-                bank = 7
-                if bank in free["a"]:
-                    free["a"].remove(bank)
+        def write(step):
+            if step[0] in banks_of:
+                bank = banks_of[step[0]].pop(0)
+                banks_of[step[0]].append(bank)
+                last_fill[bank] = step
+                step[0](*step[1:], bank)
             else:
-                bank = free[step[-1]].pop(0)
-                free[step[-1]].append(bank)
-            if bank in last_user and last_user[bank][-1] != "w":
-                extra[key(step)] = readers(last_user[bank])
-            last_user[bank] = step
-            bank_of[step] = bank
-        done, queues = set(), [list(tensor), list(vector), list(scalar), list(gpsimd), list(sync)]
-        while any(queues):
-            moved = False
-            for queue in queues:
-                while queue and all(n in done for n in needs(queue[0]) + extra.get(key(queue[0]), [])):
-                    step = queue.pop(0)
-                    step[0](*(step[1:-1] + (bank_of[step],) if step in bank_of else step[1:]))
-                    done.add(key(step))
-                    moved = True
-            assert moved, [q[0][1:] for q in queues if q]
+                step[0](*step[1:])
+            written.add(step[:3] if step[0] is widen else step)
+
+        def follow():
+            for name, queue in waiting.items():
+                held = name in ("for vector", "for scalar") and waiting["opening"]
+                while queue and not held and ready(queue[0]):
+                    write(queue.pop(0))
+
+        def write_phase(v, a, lead):
+            v, a = list(v), list(a)
+            v_all, a_all = sum(map(banks_worth, v)), sum(map(banks_worth, a))
+            v_done, a_done = lead, 0
+            while v or a:
+                follow()
+                if v and ready(v[0]) and (not a or not ready(a[0]) or v_done * a_all <= a_done * v_all):
+                    step = v.pop(0)
+                    v_done = v_done + banks_worth(step)
+                else:
+                    step = a.pop(0)
+                    a_done = a_done + banks_worth(step)
+                write(step)
+                if step in refill_after:
+                    if WT_BANK in scalar_banks:
+                        scalar_banks.remove(WT_BANK)
+                    waiting["wt"].append((spread_wt, refill_after[step]))
+
+        write_phase(*opening, 0)
+        for v, a in phases:
+            write_phase(v, a, SCALAR_LEAD)
+        follow()

@@ -135,6 +135,11 @@ def tile_nmr_relaxometry_residual_s7_kernel(tc, k1, dist, k2_bytes, k2_scale, po
                 b = 2 * pair + e
                 nc.tensor.matmul(wt_bank[pair][:, e, :], lhsT=pick[:, b : b + 1].to_broadcast([P, P]), rhs=wt_rows[:], start=True, stop=True)
 
+        def warm_up(count, bank):
+            idle = new_bank(bank, [P, P], F32)
+            for k in range(count):
+                nc.tensor.matmul(idle[:], lhsT=ident[:], rhs=ident[:], start=True, stop=True)
+
         def flat(grouped):
             return grouped.rearrange("p a n t -> p (a n t)")
 
@@ -362,8 +367,8 @@ def tile_nmr_relaxometry_residual_s7_kernel(tc, k1, dist, k2_bytes, k2_scale, po
         for step in every:
             if step[0] in maker:
                 readers.setdefault(made_by(step), []).append(step)
-        waiting = {"opening": [(turn_k2, 0, 0), (turn_dist, 0, 0), (turn_k2, 0, 1), (turn_dist, 0, 1)]}
-        waiting["opening"].extend([(turn_k2, 1, 0), (turn_dist, 1, 0), (turn_dist, 1, 1), (turn_k2, 1, 1)])
+        waiting = {"opening": [(warm_up, 5), (turn_k2, 0, 0), (turn_dist, 0, 0), (warm_up, 1), (turn_k2, 0, 1), (turn_dist, 0, 1)]}
+        waiting["opening"].extend([(turn_k2, 1, 0), (warm_up, 1), (turn_dist, 1, 0), (turn_dist, 1, 1), (turn_k2, 1, 1)])
         waiting["for vector"] = fills([s for v, a in phases for s in v])
         waiting["for scalar"] = fills([s for v, a in phases for s in a])
         waiting["wt"] = []
@@ -371,7 +376,7 @@ def tile_nmr_relaxometry_residual_s7_kernel(tc, k1, dist, k2_bytes, k2_scale, po
         waiting["gpsimd"].extend((weigh_gpsimd, n) for n in range(TILES) if n not in on_vector)
         waiting["stores"] = steps(store, count=TILES)
         vector_banks, scalar_banks, wt_banks = list(VECTOR_BANKS), list(SCALAR_BANKS), [WT_BANK]
-        banks_of = {turn_k2: vector_banks, g_quarter: vector_banks, signal: vector_banks, spread_wt: wt_banks}
+        banks_of = {turn_k2: vector_banks, g_quarter: vector_banks, signal: vector_banks, spread_wt: wt_banks, warm_up: wt_banks}
         banks_of.update({turn_dist: scalar_banks, turn_k1: scalar_banks, g_plane: scalar_banks})
         written, last_fill = set(), {}
 

@@ -8,7 +8,6 @@ FLOPS = 2 * J1 * N2 * J2 + 2 * N1 * N2 * J1
 
 F32 = mybir.dt.float32
 BF16 = mybir.dt.bfloat16
-I32 = mybir.dt.int32
 U32 = mybir.dt.uint32
 U8 = mybir.dt.uint8
 FP8 = mybir.dt.float8_e4m3fn
@@ -18,18 +17,22 @@ SUB = mybir.AluOpType.subtract
 COPY = mybir.ActivationFunctionType.Copy
 
 P = 128
-NB = 512
-HALF = NB // 2
-BLOCKS = N2 // NB
+BANK = 512
+CHUNK = 256
+CHUNKS = N2 // CHUNK
 ROW_TILES = N1 // P
-TILES = BLOCKS * ROW_TILES
 GROUPS = J1 // 512
+WIDTHS = (512, 512, 512, 512)
 RESULT_BUFS = 16
-PLANE_BUFS = 5
+PLANE_BUFS = 3
+CODE_BUFS = 2
+H_BUFS = 2
+SCALAR_LEAD = 1
 VECTOR_BANKS = (0, 1, 2, 3)
 SCALAR_BANKS = (4, 5, 6, 7)
 WT_BANK = 7
-SCALAR_LEAD = 1
+STARTS = tuple(sum(WIDTHS[:b]) for b in range(len(WIDTHS)))
+UNITS = tuple((b, i) for b, w in enumerate(WIDTHS) for i in range(0, ROW_TILES, BANK // w))
 
 
 def tile_nmr_relaxometry_residual_s7_kernel(tc, k1, dist, k2_bytes, k2_scale, pol, data, wt, out):
@@ -42,26 +45,32 @@ def tile_nmr_relaxometry_residual_s7_kernel(tc, k1, dist, k2_bytes, k2_scale, po
         ctx.enter_context(tc.manual_schedule())
 
         ident = keep.tile([P, P], F32, name="ident")
-        pick = keep.tile([P, BLOCKS], BF16, name="pick")
-        wt_rows = keep.tile([P, NB], BF16, name="wt_rows")
-        wt_all = keep.tile([P, BLOCKS, NB], BF16, name="wt_all")
+        zeros = keep.tile([P, P], F32, name="zeros")
+        ident_bf = keep.tile([P, P], BF16, name="ident_bf")
         scale4 = keep.tile([P, 4], F32, name="scale4")
         pol_bf = keep.tile([P, 4 * GROUPS], BF16, name="pol_bf")
         pol4 = keep.tile([P, 4 * GROUPS], F32, name="pol4")
-        k2_grouped = keep.tile([P, 4 * BLOCKS, P, 4], BF16, name="k2_grouped", align_bytes=64)
+        k2_grouped = keep.tile([P, 2 * CHUNKS, P, 4], BF16, name="k2_grouped", align_bytes=64)
         k2_codes = keep.tile([P, N2], U32, name="k2_codes", align_bytes=64)
         k2_scales = keep.tile([P, N2], U8, name="k2_scales", align_bytes=64)
         k1_grouped = keep.tile([P, GROUPS * ROW_TILES, P, 4], BF16, name="k1_grouped", align_bytes=64)
         k1_codes = keep.tile([P, GROUPS * N1], U32, name="k1_codes", align_bytes=64)
         k1_scales = keep.tile([P, GROUPS * N1], U8, name="k1_scales", align_bytes=64)
-        k2_raw, k2_wide, dist_sb, k1_sb, data_sb = {}, {}, {}, {}, {}
+        k2_raw, k2_wide, dist_sb, k1_sb, data_sb, wt_sb = {}, {}, {}, {}, {}, {}
         dist_grouped, dist_codes, dist_scales = {}, {}, {}
         planes, h_grouped, h_codes, h_scales, result, filled, wt_bank = {}, {}, {}, {}, {}, {}, {}
 
-        def load_k2(b, h):
-            k2_raw[b, h] = keep.tile([P, 2, J2], U8, name="k2_raw%d_%d" % (b, h))
-            rows = k2_bytes[b * NB + h * HALF : b * NB + (h + 1) * HALF, :]
-            nc.sync.dma_start(out=k2_raw[b, h][:], in_=rows.rearrange("(r p) l -> p r l", p=P))
+        def load_k2(r, count):
+            raw = keep.tile([P, count, J2], U8, name="k2_raw%d" % r)
+            nc.sync.dma_start(out=raw[:], in_=k2_bytes[r * P : (r + count) * P, :].rearrange("(r p) l -> p r l", p=P))
+            for e in range(count):
+                k2_raw[r + e] = (raw, e)
+
+        def load_scale():
+            nc.sync.dma_start(out=scale4[:], in_=k2_scale.rearrange("o (p t) -> p (o t)", t=4))
+
+        def load_pol():
+            nc.sync.dma_start(out=pol_bf[:].rearrange("p (g t) -> p g t", t=4), in_=pol.rearrange("(g p t) -> p g t", p=P, t=4))
 
         def load_dist(g, h):
             dist_sb[g, h] = keep.tile([P, 2 * J2], BF16, name="dist_sb%d_%d" % (g, h))
@@ -72,32 +81,49 @@ def tile_nmr_relaxometry_residual_s7_kernel(tc, k1, dist, k2_bytes, k2_scale, po
             k1_sb[i] = keep.tile([P, J1], BF16, name="k1_sb%d" % i)
             nc.sync.dma_start(out=k1_sb[i][:], in_=k1[i * P : (i + 1) * P, :])
 
-        def load_data(b, h):
-            data_sb[b, h] = keep.tile([P, 4, NB], BF16, name="data_sb%d_%d" % (b, h))
-            rows = data[h * 512 : (h + 1) * 512, b * NB : (b + 1) * NB]
-            nc.sync.dma_start(out=data_sb[b, h][:], in_=rows.rearrange("(i p) m -> p i m", p=P))
+        def load_data(s, h):
+            data_sb[s, h] = keep.tile([P, 4, BANK], BF16, name="data_sb%d_%d" % (s, h))
+            rows = data[h * 512 : (h + 1) * 512, s * BANK : (s + 1) * BANK]
+            nc.sync.dma_start(out=data_sb[s, h][:], in_=rows.rearrange("(i p) m -> p i m", p=P))
 
-        def load_wt(b):
-            nc.sync.dma_start(out=wt_all[:, b, :], in_=wt[b * NB : (b + 1) * NB].partition_broadcast(P))
+        def load_wt(s):
+            wt_sb[s] = keep.tile([P, BANK], BF16, name="wt_sb%d" % s)
+            nc.sync.dma_start(out=wt_sb[s][:], in_=wt[s * BANK : (s + 1) * BANK].partition_broadcast(P))
+
+        def span(n):
+            return STARTS[UNITS[n][0]] // BANK
+
+        def within_span(n):
+            b = UNITS[n][0]
+            return slice(STARTS[b] % BANK, STARTS[b] % BANK + WIDTHS[b])
+
+        def store(n):
+            b, i = UNITS[n]
+            rows = out[i * P : (i + BANK // WIDTHS[b]) * P, STARTS[b] : STARTS[b] + WIDTHS[b]]
+            nc.sync.dma_start(out=rows.rearrange("(i p) m -> p i m", p=P), in_=result[n][:])
 
         def new_bank(bank, shape, dtype):
             return psum.tile(shape, dtype, name="bank%d" % bank)
 
-        def turn_words(name, rows, bank):
-            filled[name] = new_bank(bank, [P, 2, 2, P], F32)
-            words = rows.bitcast(F32)
-            for a in (0, 1):
+        def turn_words(name, runs, bank):
+            filled[name] = new_bank(bank, [P, len(runs), 2, P], F32)
+            for a, run in enumerate(runs):
                 for u in (0, 1):
-                    nc.tensor.transpose(filled[name][:, a, u, :], words[:, 256 * a + u : 256 * (a + 1) : 2], ident[:])
+                    nc.tensor.transpose(filled[name][:, a, u, :], run.bitcast(F32)[:, u : 256 : 2], ident[:])
 
-        def turn_k2(b, h, bank):
-            turn_words(("k2", b, h), k2_wide[b, h], bank)
+        def halves(rows):
+            return [rows[:, 0:512], rows[:, 512:1024]]
+
+        def turn_k2(r, count, bank):
+            turn_words(("k2", r), [k2_wide[r + e] for e in range(count)], bank)
+            for e in range(count):
+                filled["k2 tile", r + e] = filled["k2", r][:, e]
 
         def turn_dist(g, h, bank):
-            turn_words(("dist", g, h), dist_sb[g, h][:], bank)
+            turn_words(("dist", g, h), halves(dist_sb[g, h]), bank)
 
         def turn_k1(i, bank):
-            turn_words(("k1", i), k1_sb[i][:], bank)
+            turn_words(("k1", i), halves(k1_sb[i]), bank)
 
         def mx(dst, lhs_codes, lhs_scales, rhs_codes, rhs_scales, start, stop):
             nc.tensor.matmul_mx(
@@ -110,53 +136,64 @@ def tile_nmr_relaxometry_residual_s7_kernel(tc, k1, dist, k2_bytes, k2_scale, po
                 stop=stop,
             )
 
+        def first_product(dst, g, t, m):
+            j = slice(t * P, (t + 1) * P)
+            mx(dst, dist_codes[g][:, j], dist_scales[g][:, j], k2_codes[:, m], k2_scales[:, m], True, True)
+
         def g_quarter(b, g, q, bank):
             filled["quarter", b, g, q] = new_bank(bank, [P, 4, P], F32)
-            m = slice(b * NB + q * P, b * NB + (q + 1) * P)
             for t in range(4):
-                j = slice(t * P, (t + 1) * P)
-                mx(filled["quarter", b, g, q][:, t, :], dist_codes[g][:, j], dist_scales[g][:, j], k2_codes[:, m], k2_scales[:, m], True, True)
+                first_product(filled["quarter", b, g, q][:, t, :], g, t, slice(STARTS[b] + q * P, STARTS[b] + (q + 1) * P))
 
-        def g_plane(b, g, t, bank):
-            filled["plane", b, g, t] = new_bank(bank, [P, NB], F32)
-            j, m = slice(t * P, (t + 1) * P), slice(b * NB, (b + 1) * NB)
-            mx(filled["plane", b, g, t][:], dist_codes[g][:, j], dist_scales[g][:, j], k2_codes[:, m], k2_scales[:, m], True, True)
+        def g_planes(b, g, lo, w, k, bank):
+            count = BANK // w
+            filled["planes", b, g, lo, k] = new_bank(bank, [P, count, w], F32)
+            for e in range(count):
+                first_product(filled["planes", b, g, lo, k][:, e, :], g, count * k + e, slice(STARTS[b] + lo, STARTS[b] + lo + w))
 
         def signal(n, bank):
-            b, i = divmod(n, ROW_TILES)
-            filled["signal", n] = new_bank(bank, [P, NB], F32)
-            for g in range(GROUPS):
-                c, m = slice((GROUPS * i + g) * P, (GROUPS * i + g + 1) * P), slice(g * NB, (g + 1) * NB)
-                mx(filled["signal", n][:], k1_codes[:, c], k1_scales[:, c], h_codes[b][:, m], h_scales[b][:, m], g == 0, g == GROUPS - 1)
+            b, i = UNITS[n]
+            w = WIDTHS[b]
+            filled["signal", n] = new_bank(bank, [P, BANK // w, w], F32)
+            for e in range(BANK // w):
+                for g in range(GROUPS):
+                    c, m = slice((GROUPS * (i + e) + g) * P, (GROUPS * (i + e) + g + 1) * P), slice(g * w, (g + 1) * w)
+                    mx(filled["signal", n][:, e, :], k1_codes[:, c], k1_scales[:, c], h_codes[b][:, m], h_scales[b][:, m], g == 0, g == GROUPS - 1)
 
-        def spread_wt(pair, bank):
-            wt_bank[pair] = new_bank(bank, [P, 2, NB], BF16)
-            for e in (0, 1):
-                b = 2 * pair + e
-                nc.tensor.matmul(wt_bank[pair][:, e, :], lhsT=pick[:, b : b + 1].to_broadcast([P, P]), rhs=wt_rows[:], start=True, stop=True)
+        def spread_wt(spans, bank):
+            tile = new_bank(bank, [P, 2, BANK], BF16)
+            for e, s in enumerate(spans):
+                wt_bank[s] = tile[:, e, :]
+                nc.tensor.matmul(wt_bank[s], lhsT=ident_bf[:], rhs=wt_sb[s][:], start=True, stop=True)
 
-        def warm_up(count, bank):
+        def warm_up(count, k, bank):
             idle = new_bank(bank, [P, P], F32)
-            for k in range(count):
-                nc.tensor.matmul(idle[:], lhsT=ident[:], rhs=ident[:], start=True, stop=True)
+            for r in range(count):
+                nc.tensor.matmul(idle[:], lhsT=zeros[:], rhs=zeros[:], start=True, stop=True)
 
         def flat(grouped):
             return grouped.rearrange("p a n t -> p (a n t)")
 
-        def widen(b, h, copy):
-            if b < 2:
-                wide = turn.tile([P, 2 * J2], BF16, name="wide", bufs=4)
-                k2_wide[b, h] = wide[:]
-            elif b == 2:
-                k2_wide[b, h] = flat(dist_grouped[1][:, 2 * h : 2 * h + 2])
-            else:
-                k2_wide[b, h] = flat(k2_grouped[:, 4 + 2 * h : 6 + 2 * h])
-            copy(out=k2_wide[b, h], in_=k2_raw[b, h][:].rearrange("p r l -> p (r l)").bitcast(FP8))
+        def widen(r, count, copy):
+            wide = flat(reuse[r][1]()) if r in reuse else keep.tile([P, count * J2], BF16, name="wide%d" % r)[:]
+            raw, e = k2_raw[r]
+            copy(out=wide, in_=raw[:, e : e + count].rearrange("p r l -> p (r l)").bitcast(FP8))
+            for e in range(count):
+                k2_wide[r + e] = wide[:, e * J2 : (e + 1) * J2]
 
-        def scale_k2(b, r):
-            words = filled["k2", b, r // 2][:, r % 2].rearrange("p u n -> p (u n)")
+        def widen_vector(r, count):
+            widen(r, count, nc.vector.tensor_copy)
+
+        def widen_gpsimd(r, count):
+            widen(r, count, nc.gpsimd.tensor_copy)
+
+        def widen_scalar(r, count):
+            widen(r, count, nc.scalar.copy)
+
+        def scale_k2(r):
+            words = filled["k2 tile", r].rearrange("p u n -> p (u n)")
             nc.vector.tensor_tensor(
-                out=k2_grouped[:, 4 * b + r].rearrange("p n (u e) -> p n u e", u=2),
+                out=k2_grouped[:, r].rearrange("p n (u e) -> p n u e", u=2),
                 in0=words.bitcast(BF16).rearrange("p (u n e) -> p n u e", u=2, e=2),
                 in1=scale4[:].rearrange("p (o u e) -> p o u e", o=1, u=2).to_broadcast([P, P, 2, 2]),
                 op=MULT,
@@ -177,10 +214,13 @@ def tile_nmr_relaxometry_residual_s7_kernel(tc, k1, dist, k2_bytes, k2_scale, po
         def pol_to_f32():
             nc.scalar.activation(out=pol4[:], in_=pol_bf[:], func=COPY)
 
+        def ident_to_bf16():
+            nc.scalar.copy(out=ident_bf[:], in_=ident[:])
+
         def h_columns(b, g, lo, up):
             if b not in h_grouped:
-                h_grouped[b] = turn.tile([P, GROUPS * NB, 4], BF16, name="h_grouped", align_bytes=64)
-            return h_grouped[b][:, g * NB + lo : g * NB + up, :]
+                h_grouped[b] = turn.tile([P, GROUPS * BANK, 4], BF16, name="h_grouped", align_bytes=64, bufs=H_BUFS)
+            return h_grouped[b][:, g * WIDTHS[b] + lo : g * WIDTHS[b] + up, :]
 
         def h_quarter(b, g, q):
             nc.vector.tensor_tensor(
@@ -190,209 +230,251 @@ def tile_nmr_relaxometry_residual_s7_kernel(tc, k1, dist, k2_bytes, k2_scale, po
                 op=MULT,
             )
 
-        def h_plane(b, g, t):
-            if t == 0:
-                planes[b, g] = turn.tile([P, 4, NB], BF16, name="planes", align_bytes=64, bufs=PLANE_BUFS)
-            nc.scalar.activation(out=planes[b, g][:, t, :], in_=filled["plane", b, g, t][:], func=COPY, scale=pol4[:, 4 * g + t : 4 * g + t + 1])
+        def h_planes(b, g, lo, w, k):
+            count = BANK // w
+            if k == 0:
+                planes[b, g, lo] = turn.tile([P, 4, BANK], BF16, name="planes", align_bytes=64, bufs=PLANE_BUFS)
+            for e in range(count):
+                t = count * k + e
+                dst = planes[b, g, lo][:, t, 0:w]
+                nc.scalar.activation(out=dst, in_=filled["planes", b, g, lo, k][:, e, :], func=COPY, scale=pol4[:, 4 * g + t : 4 * g + t + 1])
 
-        def group_planes(b, g, h):
-            lo, up = h * HALF, (h + 1) * HALF
-            dst = h_columns(b, g, lo, up).rearrange("p (c i) t -> p c t i", i=4)
-            nc.scalar.copy(out=dst, in_=planes[b, g][:, :, lo:up].rearrange("p t (c i) -> p c t i", i=4))
+        def group_planes(b, g, lo, h):
+            dst = h_columns(b, g, lo + h * CHUNK, lo + (h + 1) * CHUNK).rearrange("p (c i) t -> p c t i", i=4)
+            nc.scalar.copy(out=dst, in_=planes[b, g, lo][:, :, h * CHUNK : (h + 1) * CHUNK].rearrange("p t (c i) -> p c t i", i=4))
 
         def quantise(codes, scales, grouped):
             nc.vector.quantize_mx(out=codes.bitcast(FP8X4), scales=scales, in_=grouped)
 
-        def q_k2(b):
-            m = slice(b * NB, (b + 1) * NB)
-            quantise(k2_codes[:, m], k2_scales[:, m], flat(k2_grouped[:, 4 * b : 4 * b + 4]))
+        def q_k2(c, count):
+            m = slice(c * CHUNK, (c + count) * CHUNK)
+            quantise(k2_codes[:, m], k2_scales[:, m], flat(k2_grouped[:, 2 * c : 2 * (c + count)]))
 
         def q_dist(g):
             dist_codes[g] = keep.tile([P, 512], U32, name="dist_codes%d" % g, align_bytes=64)
             dist_scales[g] = keep.tile([P, 512], U8, name="dist_scales%d" % g, align_bytes=64)
             quantise(dist_codes[g][:], dist_scales[g][:], flat(dist_grouped[g][:]))
 
-        def q_k1(h):
-            c = slice(h * N1, (h + 1) * N1)
-            quantise(k1_codes[:, c], k1_scales[:, c], flat(k1_grouped[:, h * ROW_TILES : (h + 1) * ROW_TILES]))
+        def q_k1(i, count):
+            c = slice(i * GROUPS * P, (i + count) * GROUPS * P)
+            quantise(k1_codes[:, c], k1_scales[:, c], flat(k1_grouped[:, GROUPS * i : GROUPS * (i + count)]))
 
         def q_h(b):
-            h_codes[b] = turn.tile([P, GROUPS * NB], U32, name="h_codes", align_bytes=64)
-            h_scales[b] = turn.tile([P, GROUPS * NB], U8, name="h_scales", align_bytes=64)
-            quantise(h_codes[b][:], h_scales[b][:], h_grouped[b][:].rearrange("p n t -> p (n t)"))
+            m = slice(0, GROUPS * WIDTHS[b])
+            h_codes[b] = turn.tile([P, GROUPS * BANK], U32, name="h_codes", align_bytes=64, bufs=CODE_BUFS)
+            h_scales[b] = turn.tile([P, GROUPS * BANK], U8, name="h_scales", align_bytes=64, bufs=CODE_BUFS)
+            quantise(h_codes[b][:, m], h_scales[b][:, m], h_grouped[b][:, m, :].rearrange("p n t -> p (n t)"))
 
         def subtract(n):
-            b, i = divmod(n, ROW_TILES)
-            result[n] = results.tile([P, NB], F32, name="result")
-            nc.vector.tensor_tensor(out=result[n][:], in0=filled["signal", n][:], in1=data_sb[b, i // 4][:, i % 4, :], op=SUB)
+            b, i = UNITS[n]
+            count = BANK // WIDTHS[b]
+            result[n] = results.tile([P, count, WIDTHS[b]], F32, name="result")
+            nc.vector.tensor_tensor(out=result[n][:], in0=filled["signal", n][:], in1=data_sb[span(n), i // 4][:, i % 4 : i % 4 + count, within_span(n)], op=SUB)
+
+        def weigh(n, engine, weights):
+            w = WIDTHS[UNITS[n][0]]
+            spread = weights[:, within_span(n)].rearrange("p (o m) -> p o m", o=1).to_broadcast([P, BANK // w, w])
+            engine.tensor_tensor(out=result[n][:], in0=result[n][:], in1=spread, op=MULT)
 
         def weigh_vector(n):
-            b = n // ROW_TILES
-            nc.vector.tensor_tensor(out=result[n][:], in0=result[n][:], in1=wt_bank[b // 2][:, b % 2, :], op=MULT)
+            weigh(n, nc.vector, wt_bank[span(n)])
 
         def weigh_gpsimd(n):
-            nc.gpsimd.tensor_tensor(out=result[n][:], in0=result[n][:], in1=wt_all[:, n // ROW_TILES, :], op=MULT)
+            weigh(n, nc.gpsimd, wt_sb[span(n)])
 
-        def store(n):
-            b, i = divmod(n, ROW_TILES)
-            nc.sync.dma_start(out=out[i * P : (i + 1) * P, b * NB : (b + 1) * NB], in_=result[n][:])
+        def steps(f, *heads, count, first=0):
+            return [(f,) + heads + (k,) for k in range(first, first + count)]
 
-        make_identity(nc, ident[:])
-        nc.vector.memset(wt_rows[:].bitcast(I32), 0)
-        nc.vector.tensor_copy(out=pick[:], in_=ident[:, 0:BLOCKS])
+        def K(c):
+            return steps(scale_k2, count=2, first=2 * c)
 
-        load_k2(0, 0)
-        load_k2(0, 1)
-        nc.sync.dma_start(out=scale4[:], in_=k2_scale.rearrange("o (p t) -> p (o t)", t=4))
-        for h in (0, 1):
-            load_dist(0, h)
-            load_k2(1, h)
-        load_dist(1, 0)
-        load_dist(1, 1)
-        nc.sync.dma_start(out=wt_rows[0:BLOCKS, :], in_=wt.rearrange("(b m) -> b m", b=BLOCKS))
-        nc.sync.dma_start(out=pol_bf[:].rearrange("p (g t) -> p g t", t=4), in_=pol.rearrange("(g p t) -> p g t", p=P, t=4))
-        for b in (2, 3):
-            load_k2(b, 0)
-            load_k2(b, 1)
-            load_k1(2 * b - 4)
-            load_k1(2 * b - 3)
-        for i in range(4, ROW_TILES):
-            load_k1(i)
-        load_data(0, 0)
-        load_wt(0)
-        load_data(0, 1)
-        for b in range(1, BLOCKS):
-            load_wt(b)
-            load_data(b, 0)
-            load_data(b, 1)
+        def PL(b, g, lo, w):
+            return steps(h_planes, b, g, lo, w, count=4 * w // BANK)
 
-        def steps(f, *heads, count):
-            return [(f,) + heads + (k,) for k in range(count)]
+        def GP(b, g, lo, w):
+            return steps(g_planes, b, g, lo, w, count=4 * w // BANK)
 
-        def among(tiles, fillers):
-            return [s for k, n in enumerate(tiles) for s in fillers[2 * k : 2 * k + 2] + [(subtract, n)]]
+        def IL(b, g, lo, w):
+            return steps(group_planes, b, g, lo, count=w // CHUNK)
+
+        def part(b, g, lo, w):
+            return PL(b, g, lo, w) + IL(b, g, lo, w)
+
+        def Q(b, g, first):
+            return steps(h_quarter, b, g, count=2, first=first)
+
+        def GQ(b, g, first):
+            return steps(g_quarter, b, g, count=2, first=first)
+
+        S, W, E, T2, T1, SG = subtract, weigh_vector, group_k1, turn_k2, turn_k1, signal
+
+        def Q4(b, g):
+            return Q(b, g, 0) + Q(b, g, 2)
 
         def five(first):
-            subs = [(subtract, n) for n in range(first, first + 5)]
-            return subs[:4] + [(weigh_vector, first + 1), (weigh_vector, first + 3)] + subs[4:]
+            subs = [(S, n) for n in range(first, first + 5)]
+            return subs[:4] + [(W, first + 1), (W, first + 3)] + subs[4:]
 
         def alternate(first, last):
-            order = [(subtract, first)]
+            order = [(S, first)]
             for n in range(first + 1, last, 2):
-                order.extend([(subtract, n), (subtract, n + 1), (weigh_vector, n)])
-            return order + [(subtract, last), (weigh_vector, last)]
+                order.extend([(S, n), (S, n + 1), (W, n)])
+            return order + [(S, last), (W, last)]
 
-        def group(b, g):
-            return steps(h_plane, b, g, count=4) + steps(group_planes, b, g, count=2)
+        D, TD = group_dist, turn_dist
 
-        k1_steps = steps(group_k1, count=ROW_TILES)
-        quarters = steps(h_quarter, 0, 1, count=4)
-        first_group, second_group = group(0, 0), group(1, 0)
-        woven = [s for pair in zip(k1_steps[4:], second_group[:4]) for s in pair]
-        crossing = [(subtract, n) for n in range(14, 18)] + [(weigh_vector, 16), (weigh_vector, 17)]
-        crossing = crossing + [(subtract, n) for n in range(18, 21)] + [(weigh_vector, 19), (subtract, 21)]
-        opening = (
-            [(widen, 0, 0, nc.vector.tensor_copy)] + steps(scale_k2, 0, count=4) + [(q_dist, 0), (q_k2, 0)] + steps(scale_k2, 1, count=2) + [(q_dist, 1)],
-            [(widen, 0, 1, nc.scalar.copy)] + steps(group_dist, 0, count=2) + steps(group_dist, 1, count=2) + [(pol_to_f32,)],
-        )
+        turns = [(T2, 0, 1), (T2, 1, 1)] + [(T2, r, 2) for r in range(2, 16, 2)]
+        reuse = {6: ((q_dist, 0), lambda: dist_grouped[0][:, 0:2]), 8: ((q_dist, 1), lambda: dist_grouped[1][:, 0:2]), 10: ((q_dist, 1), lambda: dist_grouped[1][:, 2:4])}
+        reuse.update({12: ((q_k2, 2, 2), lambda: k2_grouped[:, 4:6]), 14: ((q_h, 0), lambda: h_grouped[0][:, 0:CHUNK].rearrange("p (a n) t -> p a n t", a=2))})
         phases = [
-            (steps(scale_k2, 1, count=4)[2:] + quarters[:3] + [(q_k2, 1)], first_group[:4] + k1_steps[:2]),
-            (quarters[3:] + steps(scale_k2, 2, count=4), first_group[4:5] + k1_steps[2:4] + first_group[5:]),
-            ([(q_k2, 2), (q_k1, 0), (q_h, 0)], woven[:4]),
-            (among((0, 1), steps(h_quarter, 1, 1, count=4)) + [(q_k1, 1)], woven[4:] + second_group[4:]),
-            (among((2, 3), steps(scale_k2, 3, count=4)) + [(q_h, 1)], group(2, 0)),
-            (five(4) + [(q_k2, 3)], group(2, 1)),
-            (five(9) + [(q_h, 2)], group(3, 0)),
-            (crossing + [(q_h, 3)], group(3, 1)),
-            (alternate(22, TILES - 1), []),
+            ([(widen_vector, 0, 1)] + K(0) + K(1) + [(q_k2, 0, 2), (q_dist, 0)] + K(2) + [(q_dist, 1)],
+             [(widen_scalar, 1, 1), (widen_scalar, 2, 1), (ident_to_bf16,)] + steps(D, 0, count=2) + steps(D, 1, count=2) + [(pol_to_f32,)]),
+            (K(3) + Q4(0, 1)[:3] + [(q_k2, 2, 2)], PL(0, 0, 0, 512) + [(E, 0), (E, 1)]),
+            (Q4(0, 1)[3:] + K(4), IL(0, 0, 0, 512)),
+            ([(q_k1, 0, 2), (q_h, 0)] + K(5), [(E, 2), (E, 3)] + PL(1, 0, 0, 512)[:3]),
+            ([(S, 0), (q_k1, 2, 2)] + Q4(1, 1)[:2] + [(S, 1), (q_k2, 4, 2)], PL(1, 0, 0, 512)[3:] + IL(1, 0, 0, 512)),
+            ([Q4(1, 1)[2], (S, 2), Q4(1, 1)[3], K(6)[0], (S, 3)], steps(E, count=4, first=4)),
+            ([(q_k1, 4, 4), K(6)[1], K(7)[0], (S, 4), (q_h, 1)], PL(2, 0, 0, 512) + PL(2, 1, 0, 512)[:1] + IL(2, 0, 0, 512)[:1]),
+            ([(S, 5), (S, 6), K(7)[1], (W, 6), (S, 7), (q_k2, 6, 2)], IL(2, 0, 0, 512)[1:] + PL(2, 1, 0, 512)[1:]),
+            (five(8) + [(q_h, 2)], IL(2, 1, 0, 512) + PL(3, 0, 0, 512)),
+            ([(S, 13), (S, 14), (S, 15), (S, 16), (S, 17), (W, 16), (W, 17)], PL(3, 1, 0, 512)[:1] + IL(3, 0, 0, 512) + PL(3, 1, 0, 512)[1:]),
+            ([(S, 18), (S, 19), (S, 20), (W, 19), (W, 20), (S, 21), (q_h, 3)], IL(3, 1, 0, 512)),
+            (alternate(22, 31), []),
         ]
-        on_vector = [s[1] for v, a in phases for s in v if s[0] is weigh_vector]
-        h_writers = {b: [s for v, a in phases for s in v + a if s[0] in (h_quarter, group_planes) and s[1] == b] for b in range(BLOCKS)}
-        refill_after = {(h_plane, 2, 0, 3): 0, (weigh_vector, 12): 1}
+        spread_after = {PL(2, 0, 0, 512)[0]: (spread_wt, (0, 1)), (W, 11): (spread_wt, (2, 3))}
+        behind = {(T1, 4): [(SG, 1)]}
+        on_vector = [s[1] for v, a in phases for s in v if s[0] is W]
+        tiles = [(weigh_gpsimd, n) for n in range(len(UNITS)) if n not in on_vector]
+        gpsimd = [(widen_gpsimd, 3, 1)] + [(widen_gpsimd, r, 2) for r in range(4, 16, 2)] + tiles
+        opening = [(warm_up, 5, 0), (T2, 0, 1), (T2, 1, 1), (warm_up, 1, 1), (T2, 2, 2), (TD, 0, 0), (TD, 0, 1), (warm_up, 2, 2), (T2, 4, 2), (TD, 1, 0), (TD, 1, 1)]
+        sync = [(load_k2, 0, 1), (load_k2, 1, 1), (load_k2, 2, 2), (load_scale,), (load_dist, 0, 0), (load_k2, 4, 2), (load_dist, 0, 1), (load_k2, 6, 2), (load_dist, 1, 0), (load_dist, 1, 1), (load_pol,)]
+        sync += [(load_k2, 8, 2), (load_k2, 10, 2), (load_k1, 0), (load_k1, 1), (load_k2, 12, 2), (load_k2, 14, 2)] + steps(load_k1, count=6, first=2) + [(load_data, 0, 0), (load_wt, 0), (load_data, 0, 1)]
+        for b in range(1, N2 // BANK):
+            sync += [(load_wt, b), (load_data, b, 0), (load_data, b, 1)]
+        sync += steps(store, count=len(UNITS))
 
-        maker = {scale_k2: turn_k2, group_dist: turn_dist, group_k1: turn_k1, h_quarter: g_quarter, h_plane: g_plane, subtract: signal}
+        maker = {scale_k2: turn_k2, group_dist: turn_dist, group_k1: turn_k1, h_quarter: g_quarter, h_planes: g_planes, subtract: signal}
+        vector, scalar = [s for v, a in phases for s in v], [s for v, a in phases for s in a]
+        every = vector + scalar + gpsimd
 
         def made_by(step):
-            if step[0] is scale_k2:
-                return (turn_k2, step[1], step[2] // 2)
-            return (maker[step[0]],) + step[1:]
+            return covering(turns, step[1])[0] if step[0] is scale_k2 else (maker[step[0]],) + step[1:]
 
-        def fills(mine):
-            order = []
-            for step in mine:
-                if step[0] in maker and made_by(step) not in order + waiting["opening"]:
-                    order.append(made_by(step))
-            return order
+        def covering(among, k):
+            return [s for s in among if s[1] <= k < s[1] + s[2]]
 
-        def needs(step):
-            f, a = step[0], step[1:]
-            h_free = [(q_h, a[0] - 2)] if f in (h_quarter, group_planes) and a[0] >= 2 else []
-            if f is widen:
-                return {2: [(q_dist, 1)], 3: [(q_k2, 1)]}.get(a[0], [])
-            if f is turn_k2:
-                return [(widen,) + a]
-            if f in (g_quarter, g_plane):
-                return [(q_k2, a[0]), (q_dist, a[1])]
-            if f is signal:
-                return [(q_h, a[0] // ROW_TILES), (q_k1, a[0] % ROW_TILES // 4)]
-            if f in (h_quarter, h_plane):
-                return [made_by(step), (pol_to_f32,)] + h_free
-            if f is subtract:
-                return [made_by(step)] + ([(store, a[0] - RESULT_BUFS)] if a[0] >= RESULT_BUFS else [])
-            if f in maker:
-                return [made_by(step)]
-            if f is group_planes:
-                return steps(h_plane, a[0], a[1], count=4) + h_free
-            if f is q_k2:
-                return steps(scale_k2, a[0], count=4)
-            if f is q_dist:
-                return steps(group_dist, a[0], count=2)
-            if f is q_k1:
-                return k1_steps[4 * a[0] : 4 * a[0] + 4]
-            if f is q_h:
-                return h_writers[a[0]] + ([(signal, ROW_TILES * (a[0] - 1) - 1)] if a[0] >= 2 else [])
-            if f is weigh_vector:
-                return [(subtract, a[0]), (spread_wt, a[0] // (2 * ROW_TILES))]
-            if f is weigh_gpsimd:
-                return [(subtract, a[0])]
-            if f is store:
-                return [(weigh_vector if a[0] in on_vector else weigh_gpsimd, a[0])]
-            return []
+        def all_of(f, among):
+            return [s for s in among if s[0] is f]
 
-        def banks_worth(step):
-            return 2 if step[0] in (group_planes, q_k1, q_h) else 1
+        def units_of(b):
+            return [n for n in range(len(UNITS)) if UNITS[n][0] == b]
 
-        every = [s for v, a in [opening] + phases for s in v + a]
+        widenings = [s for s in every if s[0] in (widen_vector, widen_scalar, widen_gpsimd)]
+        weighings = {s[1]: s for s in every if s[0] in (weigh_vector, weigh_gpsimd)}
+        plane_sets = [s[1:4] for s in scalar if s[0] is h_planes and s[5] == 0]
+        spreads = list(spread_after.values())
         readers = {}
         for step in every:
             if step[0] in maker:
                 readers.setdefault(made_by(step), []).append(step)
-        waiting = {"opening": [(warm_up, 5), (turn_k2, 0, 0), (turn_dist, 0, 0), (warm_up, 1), (turn_k2, 0, 1), (turn_dist, 0, 1)]}
-        waiting["opening"].extend([(turn_k2, 1, 0), (warm_up, 1), (turn_dist, 1, 0), (turn_dist, 1, 1), (turn_k2, 1, 1)])
-        waiting["for vector"] = fills([s for v, a in phases for s in v])
-        waiting["for scalar"] = fills([s for v, a in phases for s in a])
-        waiting["wt"] = []
-        waiting["gpsimd"] = [(widen, b, h, nc.gpsimd.tensor_copy) for b in range(1, BLOCKS) for h in (0, 1)]
-        waiting["gpsimd"].extend((weigh_gpsimd, n) for n in range(TILES) if n not in on_vector)
-        waiting["stores"] = steps(store, count=TILES)
+            if step[0] is weigh_vector:
+                readers.setdefault([s for s in spreads if span(step[1]) in s[1]][0], []).append(step)
+
+        def needs(step):
+            f, a = step[0], step[1:]
+            if step in widenings:
+                earlier = [reuse[a[0]][0]] if a[0] in reuse else []
+                return covering(all_of(load_k2, sync), a[0]) + earlier
+            if f is turn_k2:
+                return [s for r in range(a[0], a[0] + a[1]) for s in covering(widenings, r)]
+            if f is turn_dist:
+                return [(load_dist,) + a]
+            if f is turn_k1:
+                return [(load_k1,) + a]
+            if f in (g_quarter, g_planes):
+                lo, w = (a[2] * P, P) if f is g_quarter else a[2:4]
+                first, last = (STARTS[a[0]] + lo) // CHUNK, (STARTS[a[0]] + lo + w - 1) // CHUNK
+                return covering(all_of(q_k2, vector), first) + covering(all_of(q_k2, vector), last) + [(q_dist, a[1])]
+            if f is signal:
+                b, i = UNITS[a[0]]
+                return [(q_h, b)] + covering(all_of(q_k1, vector), i) + covering(all_of(q_k1, vector), i + BANK // WIDTHS[b] - 1)
+            if f is spread_wt:
+                return [(ident_to_bf16,)] + [(load_wt, b) for b in a[0]]
+            h_free = []
+            if f in (h_quarter, group_planes) and a[0] >= H_BUFS:
+                h_free = [(q_h, a[0] - H_BUFS)] + [covering(turns, c)[0] for c in reuse if reuse[c][0] == (q_h, a[0] - H_BUFS)]
+            if f is h_quarter:
+                return [made_by(step), (pol_to_f32,)] + h_free
+            if f is h_planes:
+                k = plane_sets.index(a[:3]) - PLANE_BUFS
+                earlier = [s for s in scalar if s[0] is group_planes and s[1:4] == plane_sets[k]] if k >= 0 else []
+                return [made_by(step), (pol_to_f32,)] + earlier
+            if f is group_planes:
+                return [s for s in scalar if s[0] is h_planes and s[1:4] == a[:3]] + h_free
+            if f is subtract:
+                b, i = UNITS[a[0]]
+                return [made_by(step), (load_data, span(a[0]), i // 4)] + ([(store, a[0] - RESULT_BUFS)] if a[0] >= RESULT_BUFS else [])
+            if f is scale_k2:
+                return [made_by(step), (load_scale,)]
+            if f in maker:
+                return [made_by(step)]
+            if f is pol_to_f32:
+                return [(load_pol,)]
+            if f is q_k2:
+                return steps(scale_k2, count=2 * a[1], first=2 * a[0])
+            if f is q_dist:
+                return steps(group_dist, a[0], count=2)
+            if f is q_k1:
+                return steps(group_k1, count=a[1], first=a[0])
+            if f is q_h:
+                writers = [s for s in every if s[0] in (h_quarter, group_planes) and s[1] == a[0]]
+                return writers + ([(signal, n) for n in units_of(a[0] - CODE_BUFS)] if a[0] >= CODE_BUFS else [])
+            if f is weigh_vector:
+                return [(subtract, a[0])] + [s for s in spreads if span(a[0]) in s[1]]
+            if f is weigh_gpsimd:
+                return [(subtract, a[0]), (load_wt, span(a[0]))]
+            if f is store:
+                return [weighings[a[0]]]
+            return []
+
         vector_banks, scalar_banks, wt_banks = list(VECTOR_BANKS), list(SCALAR_BANKS), [WT_BANK]
         banks_of = {turn_k2: vector_banks, g_quarter: vector_banks, signal: vector_banks, spread_wt: wt_banks, warm_up: wt_banks}
-        banks_of.update({turn_dist: scalar_banks, turn_k1: scalar_banks, g_plane: scalar_banks})
+        banks_of.update({turn_dist: scalar_banks, turn_k1: scalar_banks, g_planes: scalar_banks})
         written, last_fill = set(), {}
 
+        def free_banks(step):
+            return [bank for bank in banks_of[step[0]] if all(s in written for s in readers.get(last_fill.get(bank), []))]
+
         def ready(step):
-            before = last_fill.get(banks_of[step[0]][0]) if step[0] in banks_of else None
-            return all(s in written for s in needs(step[:3] if step[0] is widen else step) + readers.get(before, []))
+            return all(s in written for s in needs(step) + behind.get(step, [])) and (step[0] not in banks_of or free_banks(step))
 
         def write(step):
             if step[0] in banks_of:
-                bank = banks_of[step[0]].pop(0)
+                bank = free_banks(step)[0]
+                banks_of[step[0]].remove(bank)
                 banks_of[step[0]].append(bank)
                 last_fill[bank] = step
                 step[0](*step[1:], bank)
             else:
                 step[0](*step[1:])
-            written.add(step[:3] if step[0] is widen else step)
+            written.add(step)
+
+        def fills(mine):
+            order = []
+            for step in mine:
+                if step[0] in maker and made_by(step) not in order + opening:
+                    order.append(made_by(step))
+            return order
+
+        def banks_worth(step):
+            f = step[0]
+            if f in (q_k2, q_k1):
+                return step[2] * 0.5
+            if f is q_h:
+                return WIDTHS[step[1]] // CHUNK
+            return 2 if f is group_planes else 1
+
+        waiting = {"sync": list(sync), "opening": list(opening), "for vector": fills(vector), "for scalar": fills(scalar), "wt": [], "gpsimd": list(gpsimd)}
 
         def follow():
             for name, queue in waiting.items():
@@ -400,25 +482,25 @@ def tile_nmr_relaxometry_residual_s7_kernel(tc, k1, dist, k2_bytes, k2_scale, po
                 while queue and not held and ready(queue[0]):
                     write(queue.pop(0))
 
-        def write_phase(v, a, lead):
+        nc.vector.memset(zeros[:], 0.0)
+        make_identity(nc, ident[:])
+        for v, a in phases:
             v, a = list(v), list(a)
             v_all, a_all = sum(map(banks_worth, v)), sum(map(banks_worth, a))
-            v_done, a_done = lead, 0
+            v_done, a_done = SCALAR_LEAD, 0
             while v or a:
                 follow()
                 if v and ready(v[0]) and (not a or not ready(a[0]) or v_done * a_all <= a_done * v_all):
                     step = v.pop(0)
                     v_done = v_done + banks_worth(step)
                 else:
-                    step = a.pop(0)
+                    step = a.pop(0) if a else v.pop(0)
+                    assert ready(step)
                     a_done = a_done + banks_worth(step)
                 write(step)
-                if step in refill_after:
+                if step in spread_after:
                     if WT_BANK in scalar_banks:
                         scalar_banks.remove(WT_BANK)
-                    waiting["wt"].append((spread_wt, refill_after[step]))
-
-        write_phase(*opening, 0)
-        for v, a in phases:
-            write_phase(v, a, SCALAR_LEAD)
+                    waiting["wt"].append(spread_after[step])
         follow()
+        assert not any(waiting.values())

@@ -97,10 +97,16 @@ def tile_nmr_relaxometry_residual_s7_kernel(tc, k1, dist, k2_bytes, k2_scale, po
             b = UNITS[n][0]
             return slice(STARTS[b] % BANK, STARTS[b] % BANK + WIDTHS[b])
 
-        def store(n):
+        def put(n, queue):
             b, i = UNITS[n]
             rows = out[i * P : (i + BANK // WIDTHS[b]) * P, STARTS[b] : STARTS[b] + WIDTHS[b]]
-            nc.sync.dma_start(out=rows.rearrange("(i p) m -> p i m", p=P), in_=result[n][:])
+            queue.dma_start(out=rows.rearrange("(i p) m -> p i m", p=P), in_=result[n][:])
+
+        def store(n):
+            put(n, nc.sync)
+
+        def store_scalar(n):
+            put(n, nc.scalar)
 
         def new_bank(bank, shape, dtype):
             return psum.tile(shape, dtype, name="bank%d" % bank)
@@ -324,16 +330,16 @@ def tile_nmr_relaxometry_residual_s7_kernel(tc, k1, dist, k2_bytes, k2_scale, po
         D, TD = group_dist, turn_dist
 
         turns = [(T2, 0, 1), (T2, 1, 1)] + [(T2, r, 2) for r in range(2, 16, 2)]
-        reuse = {6: ((q_dist, 0), lambda: dist_grouped[0][:, 0:2]), 8: ((q_dist, 1), lambda: dist_grouped[1][:, 0:2]), 10: ((q_dist, 1), lambda: dist_grouped[1][:, 2:4])}
+        reuse = {7: ((q_dist, 0), lambda: dist_grouped[0][:, 0:1]), 8: ((q_dist, 1), lambda: dist_grouped[1][:, 0:2]), 10: ((q_dist, 1), lambda: dist_grouped[1][:, 2:4])}
         reuse.update({12: ((q_k2, 2, 2), lambda: k2_grouped[:, 4:6]), 14: ((q_h, 0), lambda: h_grouped[0][:, 0:CHUNK].rearrange("p (a n) t -> p a n t", a=2))})
         phases = [
             ([(widen_vector, 0, 1)] + K(0) + K(1) + [(q_k2, 0, 2), (q_dist, 0)] + K(2) + [(q_dist, 1)],
              [(widen_scalar, 1, 1), (widen_scalar, 2, 1), (ident_to_bf16,)] + steps(D, 0, count=2) + steps(D, 1, count=2) + [(pol_to_f32,)]),
-            (K(3) + Q4(0, 1)[:3] + [(q_k2, 2, 2)], PL(0, 0, 0, 512) + [(E, 0), (E, 1)]),
-            (Q4(0, 1)[3:] + K(4), IL(0, 0, 0, 512)),
+            (K(3) + Q4(0, 1)[:3] + [(q_k2, 2, 2)], PL(0, 0, 0, 512) + IL(0, 0, 0, 512)[:1]),
+            (Q4(0, 1)[3:] + K(4), [(E, 0), (E, 1)] + IL(0, 0, 0, 512)[1:]),
             ([(q_k1, 0, 2), (q_h, 0)] + K(5), [(E, 2), (E, 3)] + PL(1, 0, 0, 512)[:3]),
-            ([(S, 0), (q_k1, 2, 2)] + Q4(1, 1)[:2] + [(S, 1), (q_k2, 4, 2)], PL(1, 0, 0, 512)[3:] + IL(1, 0, 0, 512)),
-            ([Q4(1, 1)[2], (S, 2), Q4(1, 1)[3], K(6)[0], (S, 3)], steps(E, count=4, first=4)),
+            ([(S, 0), (q_k1, 2, 2)] + Q4(1, 1)[:2] + [(S, 1), (q_k2, 4, 2)], PL(1, 0, 0, 512)[3:] + [(E, 4), (E, 5)] + IL(1, 0, 0, 512)[:1]),
+            ([Q4(1, 1)[2], (S, 2), Q4(1, 1)[3], K(6)[0], (S, 3)], [(E, 6), (E, 7)] + IL(1, 0, 0, 512)[1:]),
             ([(q_k1, 4, 4), K(6)[1], K(7)[0], (S, 4), (q_h, 1)], PL(2, 0, 0, 512) + PL(2, 1, 0, 512)[:1] + IL(2, 0, 0, 512)[:1]),
             ([(S, 5), (S, 6), K(7)[1], (W, 6), (S, 7), (q_k2, 6, 2)], IL(2, 0, 0, 512)[1:] + PL(2, 1, 0, 512)[1:]),
             (five(8) + [(q_h, 2)], IL(2, 1, 0, 512) + PL(3, 0, 0, 512)),
@@ -341,12 +347,13 @@ def tile_nmr_relaxometry_residual_s7_kernel(tc, k1, dist, k2_bytes, k2_scale, po
             ([(S, 18), (S, 19), (S, 20), (W, 19), (W, 20), (S, 21), (q_h, 3)], IL(3, 1, 0, 512)),
             (alternate(22, 31), []),
         ]
-        spread_after = {PL(2, 0, 0, 512)[0]: (spread_wt, (0, 1)), (W, 11): (spread_wt, (2, 3))}
-        behind = {(T1, 4): [(SG, 1)]}
+        spread_after = {PL(2, 0, 0, 512)[0]: (spread_wt, (0, 1)), (W, 11): (spread_wt, (2,)), (W, 20): (spread_wt, (2, 3))}
+        behind = {GP(2, 0, 0, 512)[1]: [(SG, 3)], (T1, 6): [(SG, 1)]}
+        borrowing = GP(1, 0, 0, 512)[2:]
         on_vector = [s[1] for v, a in phases for s in v if s[0] is W]
         tiles = [(weigh_gpsimd, n) for n in range(len(UNITS)) if n not in on_vector]
-        gpsimd = [(widen_gpsimd, 3, 1)] + [(widen_gpsimd, r, 2) for r in range(4, 16, 2)] + tiles
-        opening = [(warm_up, 5, 0), (T2, 0, 1), (T2, 1, 1), (warm_up, 1, 1), (T2, 2, 2), (TD, 0, 0), (TD, 0, 1), (warm_up, 2, 2), (T2, 4, 2), (TD, 1, 0), (TD, 1, 1)]
+        gpsimd = [(widen_gpsimd, 3, 1), (widen_gpsimd, 4, 2), (widen_gpsimd, 6, 1), (widen_gpsimd, 7, 1)] + [(widen_gpsimd, r, 2) for r in range(8, 16, 2)] + tiles
+        opening = [(warm_up, 4, 0), (T2, 0, 1), (T2, 1, 1), (warm_up, 2, 1), (T2, 2, 2), (TD, 0, 0), (TD, 0, 1), (warm_up, 1, 2), (T2, 4, 2), (TD, 1, 0), (TD, 1, 1)]
         sync = [(load_k2, 0, 1), (load_k2, 1, 1), (load_k2, 2, 2), (load_scale,), (load_dist, 0, 0), (load_k2, 4, 2), (load_dist, 0, 1), (load_k2, 6, 2), (load_dist, 1, 0), (load_dist, 1, 1), (load_pol,)]
         sync += [(load_k2, 8, 2), (load_k2, 10, 2), (load_k1, 0), (load_k1, 1), (load_k2, 12, 2), (load_k2, 14, 2)] + steps(load_k1, count=6, first=2) + [(load_data, 0, 0), (load_wt, 0), (load_data, 0, 1)]
         for b in range(1, N2 // BANK):
@@ -372,13 +379,18 @@ def tile_nmr_relaxometry_residual_s7_kernel(tc, k1, dist, k2_bytes, k2_scale, po
         widenings = [s for s in every if s[0] in (widen_vector, widen_scalar, widen_gpsimd)]
         weighings = {s[1]: s for s in every if s[0] in (weigh_vector, weigh_gpsimd)}
         plane_sets = [s[1:4] for s in scalar if s[0] is h_planes and s[5] == 0]
-        spreads = list(spread_after.values())
+
+        def spread_for(step):
+            asked = [s for s in merged[: merged.index(step)] if s in spread_after]
+            return spread_after[asked[-1]]
+
+        merged = [s for v, a in phases for s in a + v]
         readers = {}
         for step in every:
             if step[0] in maker:
                 readers.setdefault(made_by(step), []).append(step)
             if step[0] is weigh_vector:
-                readers.setdefault([s for s in spreads if span(step[1]) in s[1]][0], []).append(step)
+                readers.setdefault(spread_for(step), []).append(step)
 
         def needs(step):
             f, a = step[0], step[1:]
@@ -430,10 +442,10 @@ def tile_nmr_relaxometry_residual_s7_kernel(tc, k1, dist, k2_bytes, k2_scale, po
                 writers = [s for s in every if s[0] in (h_quarter, group_planes) and s[1] == a[0]]
                 return writers + ([(signal, n) for n in units_of(a[0] - CODE_BUFS)] if a[0] >= CODE_BUFS else [])
             if f is weigh_vector:
-                return [(subtract, a[0])] + [s for s in spreads if span(a[0]) in s[1]]
+                return [(subtract, a[0])] + [spread_for(step)]
             if f is weigh_gpsimd:
                 return [(subtract, a[0]), (load_wt, span(a[0]))]
-            if f is store:
+            if f in (store, store_scalar):
                 return [weighings[a[0]]]
             return []
 
@@ -442,8 +454,11 @@ def tile_nmr_relaxometry_residual_s7_kernel(tc, k1, dist, k2_bytes, k2_scale, po
         banks_of.update({turn_dist: scalar_banks, turn_k1: scalar_banks, g_planes: scalar_banks})
         written, last_fill = set(), {}
 
+        def banks_for(step):
+            return vector_banks if step in borrowing else banks_of[step[0]]
+
         def free_banks(step):
-            return [bank for bank in banks_of[step[0]] if all(s in written for s in readers.get(last_fill.get(bank), []))]
+            return [bank for bank in banks_for(step) if all(s in written for s in readers.get(last_fill.get(bank), []))]
 
         def ready(step):
             return all(s in written for s in needs(step) + behind.get(step, [])) and (step[0] not in banks_of or free_banks(step))
@@ -451,8 +466,8 @@ def tile_nmr_relaxometry_residual_s7_kernel(tc, k1, dist, k2_bytes, k2_scale, po
         def write(step):
             if step[0] in banks_of:
                 bank = free_banks(step)[0]
-                banks_of[step[0]].remove(bank)
-                banks_of[step[0]].append(bank)
+                banks_for(step).remove(bank)
+                banks_for(step).append(bank)
                 last_fill[bank] = step
                 step[0](*step[1:], bank)
             else:

@@ -97,16 +97,9 @@ def tile_nmr_relaxometry_residual_s7_kernel(tc, k1, dist, k2_bytes, k2_scale, po
             b = UNITS[n][0]
             return slice(STARTS[b] % BANK, STARTS[b] % BANK + WIDTHS[b])
 
-        def put(n, queue):
+        def store(n, lo=0, up=BANK):
             b, i = UNITS[n]
-            rows = out[i * P : (i + BANK // WIDTHS[b]) * P, STARTS[b] : STARTS[b] + WIDTHS[b]]
-            queue.dma_start(out=rows.rearrange("(i p) m -> p i m", p=P), in_=result[n][:])
-
-        def store(n):
-            put(n, nc.sync)
-
-        def store_scalar(n):
-            put(n, nc.scalar)
+            nc.sync.dma_start(out=out[i * P : (i + 1) * P, STARTS[b] + lo : STARTS[b] + up], in_=result[n][:, lo:up])
 
         def new_bank(bank, shape, dtype):
             return psum.tile(shape, dtype, name="bank%d" % bank)
@@ -271,22 +264,17 @@ def tile_nmr_relaxometry_residual_s7_kernel(tc, k1, dist, k2_bytes, k2_scale, po
             h_scales[b] = turn.tile([P, GROUPS * BANK], U8, name="h_scales", align_bytes=64, bufs=CODE_BUFS)
             quantise(h_codes[b][:, m], h_scales[b][:, m], h_grouped[b][:, m, :].rearrange("p n t -> p (n t)"))
 
-        def subtract(n):
+        def subtract(n, lo=0, up=BANK):
             b, i = UNITS[n]
-            count = BANK // WIDTHS[b]
-            result[n] = results.tile([P, count, WIDTHS[b]], F32, name="result")
-            nc.vector.tensor_tensor(out=result[n][:], in0=filled["signal", n][:], in1=data_sb[span(n), i // 4][:, i % 4 : i % 4 + count, within_span(n)], op=SUB)
+            if lo == 0:
+                result[n] = results.tile([P, BANK], F32, name="result")
+            nc.vector.tensor_tensor(out=result[n][:, lo:up], in0=filled["signal", n][:, 0, lo:up], in1=data_sb[b, i // 4][:, i % 4, lo:up], op=SUB)
 
-        def weigh(n, engine, weights):
-            w = WIDTHS[UNITS[n][0]]
-            spread = weights[:, within_span(n)].rearrange("p (o m) -> p o m", o=1).to_broadcast([P, BANK // w, w])
-            engine.tensor_tensor(out=result[n][:], in0=result[n][:], in1=spread, op=MULT)
+        def weigh_vector(n, lo=0, up=BANK):
+            nc.vector.tensor_tensor(out=result[n][:, lo:up], in0=result[n][:, lo:up], in1=wt_bank[span(n)][:, lo:up], op=MULT)
 
-        def weigh_vector(n):
-            weigh(n, nc.vector, wt_bank[span(n)])
-
-        def weigh_gpsimd(n):
-            weigh(n, nc.gpsimd, wt_sb[span(n)])
+        def weigh_gpsimd(n, lo=0, up=BANK):
+            nc.gpsimd.tensor_tensor(out=result[n][:, lo:up], in0=result[n][:, lo:up], in1=wt_sb[span(n)][:, lo:up], op=MULT)
 
         def steps(f, *heads, count, first=0):
             return [(f,) + heads + (k,) for k in range(first, first + count)]
@@ -333,8 +321,8 @@ def tile_nmr_relaxometry_residual_s7_kernel(tc, k1, dist, k2_bytes, k2_scale, po
         reuse = {7: ((q_dist, 0), lambda: dist_grouped[0][:, 0:1]), 8: ((q_dist, 1), lambda: dist_grouped[1][:, 0:2]), 10: ((q_dist, 1), lambda: dist_grouped[1][:, 2:4])}
         reuse.update({12: ((q_k2, 2, 2), lambda: k2_grouped[:, 4:6]), 14: ((q_h, 0), lambda: h_grouped[0][:, 0:CHUNK].rearrange("p (a n) t -> p a n t", a=2))})
         phases = [
-            ([(widen_vector, 0, 1)] + K(0) + K(1) + [(q_k2, 0, 2), (q_dist, 0)] + K(2) + [(q_dist, 1)],
-             [(widen_scalar, 1, 1), (widen_scalar, 2, 1), (ident_to_bf16,)] + steps(D, 0, count=2) + steps(D, 1, count=2) + [(pol_to_f32,)]),
+            ([(widen_vector, 0, 1), (widen_vector, 1, 1)] + K(0) + K(1) + [(q_k2, 0, 1), (q_k2, 1, 1), (q_dist, 0)] + K(2) + [(q_dist, 1)],
+             [(widen_scalar, 2, 1), (ident_to_bf16,)] + steps(D, 0, count=2) + [(pol_to_f32,)] + steps(D, 1, count=2)),
             (K(3) + Q4(0, 1)[:3] + [(q_k2, 2, 2)], PL(0, 0, 0, 512) + IL(0, 0, 0, 512)[:1]),
             (Q4(0, 1)[3:] + K(4), [(E, 0), (E, 1)] + IL(0, 0, 0, 512)[1:]),
             ([(q_k1, 0, 2), (q_h, 0)] + K(5), [(E, 2), (E, 3)] + PL(1, 0, 0, 512)[:3]),
@@ -342,30 +330,32 @@ def tile_nmr_relaxometry_residual_s7_kernel(tc, k1, dist, k2_bytes, k2_scale, po
             ([Q4(1, 1)[2], (S, 2), Q4(1, 1)[3], K(6)[0], (S, 3)], [(E, 6), (E, 7)] + IL(1, 0, 0, 512)[1:]),
             ([(q_k1, 4, 4), K(6)[1], K(7)[0], (S, 4), (q_h, 1)], PL(2, 0, 0, 512) + PL(2, 1, 0, 512)[:1] + IL(2, 0, 0, 512)[:1]),
             ([(S, 5), (S, 6), K(7)[1], (W, 6), (S, 7), (q_k2, 6, 2)], IL(2, 0, 0, 512)[1:] + PL(2, 1, 0, 512)[1:]),
-            (five(8) + [(q_h, 2)], IL(2, 1, 0, 512) + PL(3, 0, 0, 512)),
-            ([(S, 13), (S, 14), (S, 15), (S, 16), (S, 17), (W, 16), (W, 17)], PL(3, 1, 0, 512)[:1] + IL(3, 0, 0, 512) + PL(3, 1, 0, 512)[1:]),
+            (five(8)[:2], IL(2, 1, 0, 512)),
+            (five(8)[2:], PL(3, 0, 0, 512) + PL(3, 1, 0, 512)[:1]),
+            ([(q_h, 2)], IL(3, 0, 0, 512)[:1]),
+            ([(S, 13), (S, 14), (S, 15), (S, 16), (S, 17), (W, 16), (W, 17)], PL(3, 1, 0, 512)[1:] + IL(3, 0, 0, 512)[1:]),
             ([(S, 18), (S, 19), (S, 20), (W, 19), (W, 20), (S, 21), (q_h, 3)], IL(3, 1, 0, 512)),
-            (alternate(22, 31), []),
+            (alternate(22, 31)[:-2] + [(S, 31, 0, 256), (S, 31, 256, 512), (W, 30, 256, 512), (W, 31, 0, 256), (W, 31, 256, 512)], []),
         ]
         spread_after = {PL(2, 0, 0, 512)[0]: (spread_wt, (0, 1)), (W, 11): (spread_wt, (2,)), (W, 20): (spread_wt, (2, 3))}
-        behind = {GP(2, 0, 0, 512)[1]: [(SG, 3)], (T1, 6): [(SG, 1)]}
+        behind = {(T1, 5): [(SG, 0)], (T1, 2): [(T2, 8, 2)], GP(0, 0, 0, 512)[2]: [(T2, 6, 2)], GP(2, 0, 0, 512)[1]: [(SG, 3)], (T1, 6): [(SG, 1)]}
         borrowing = GP(1, 0, 0, 512)[2:]
         on_vector = [s[1] for v, a in phases for s in v if s[0] is W]
-        tiles = [(weigh_gpsimd, n) for n in range(len(UNITS)) if n not in on_vector]
+        tiles = [(weigh_gpsimd, n) for n in range(len(UNITS)) if n not in on_vector] + [(weigh_gpsimd, 30, 0, 256)]
         gpsimd = [(widen_gpsimd, 3, 1), (widen_gpsimd, 4, 2), (widen_gpsimd, 6, 1), (widen_gpsimd, 7, 1)] + [(widen_gpsimd, r, 2) for r in range(8, 16, 2)] + tiles
         opening = [(warm_up, 4, 0), (T2, 0, 1), (T2, 1, 1), (warm_up, 2, 1), (T2, 2, 2), (TD, 0, 0), (TD, 0, 1), (warm_up, 1, 2), (T2, 4, 2), (TD, 1, 0), (TD, 1, 1)]
-        sync = [(load_k2, 0, 1), (load_k2, 1, 1), (load_k2, 2, 2), (load_scale,), (load_dist, 0, 0), (load_k2, 4, 2), (load_dist, 0, 1), (load_k2, 6, 2), (load_dist, 1, 0), (load_dist, 1, 1), (load_pol,)]
+        sync = [(load_k2, 0, 1), (load_k2, 1, 1), (load_k2, 2, 2), (load_scale,), (load_dist, 0, 0), (load_k2, 4, 2), (load_dist, 0, 1), (load_k2, 6, 2), (load_pol,), (load_dist, 1, 0), (load_dist, 1, 1)]
         sync += [(load_k2, 8, 2), (load_k2, 10, 2), (load_k1, 0), (load_k1, 1), (load_k2, 12, 2), (load_k2, 14, 2)] + steps(load_k1, count=6, first=2) + [(load_data, 0, 0), (load_wt, 0), (load_data, 0, 1)]
         for b in range(1, N2 // BANK):
             sync += [(load_wt, b), (load_data, b, 0), (load_data, b, 1)]
-        sync += steps(store, count=len(UNITS))
+        sync += steps(store, count=30) + [(store, n, lo, lo + 256) for n in (30, 31) for lo in (0, 256)]
 
         maker = {scale_k2: turn_k2, group_dist: turn_dist, group_k1: turn_k1, h_quarter: g_quarter, h_planes: g_planes, subtract: signal}
         vector, scalar = [s for v, a in phases for s in v], [s for v, a in phases for s in a]
         every = vector + scalar + gpsimd
 
         def made_by(step):
-            return covering(turns, step[1])[0] if step[0] is scale_k2 else (maker[step[0]],) + step[1:]
+            return covering(turns, step[1])[0] if step[0] is scale_k2 else (maker[step[0]],) + (step[1:2] if step[0] is subtract else step[1:])
 
         def covering(among, k):
             return [s for s in among if s[1] <= k < s[1] + s[2]]
@@ -377,7 +367,7 @@ def tile_nmr_relaxometry_residual_s7_kernel(tc, k1, dist, k2_bytes, k2_scale, po
             return [n for n in range(len(UNITS)) if UNITS[n][0] == b]
 
         widenings = [s for s in every if s[0] in (widen_vector, widen_scalar, widen_gpsimd)]
-        weighings = {s[1]: s for s in every if s[0] in (weigh_vector, weigh_gpsimd)}
+        weighings = {s[1:]: s for s in every if s[0] in (weigh_vector, weigh_gpsimd)}
         plane_sets = [s[1:4] for s in scalar if s[0] is h_planes and s[5] == 0]
 
         def spread_for(step):
@@ -391,6 +381,9 @@ def tile_nmr_relaxometry_residual_s7_kernel(tc, k1, dist, k2_bytes, k2_scale, po
                 readers.setdefault(made_by(step), []).append(step)
             if step[0] is weigh_vector:
                 readers.setdefault(spread_for(step), []).append(step)
+
+        def subtractions(a):
+            return [(subtract,) + a] if (subtract,) + a in vector else [(subtract, a[0])]
 
         def needs(step):
             f, a = step[0], step[1:]
@@ -442,11 +435,11 @@ def tile_nmr_relaxometry_residual_s7_kernel(tc, k1, dist, k2_bytes, k2_scale, po
                 writers = [s for s in every if s[0] in (h_quarter, group_planes) and s[1] == a[0]]
                 return writers + ([(signal, n) for n in units_of(a[0] - CODE_BUFS)] if a[0] >= CODE_BUFS else [])
             if f is weigh_vector:
-                return [(subtract, a[0])] + [spread_for(step)]
+                return subtractions(a) + [spread_for(step)]
             if f is weigh_gpsimd:
-                return [(subtract, a[0]), (load_wt, span(a[0]))]
-            if f in (store, store_scalar):
-                return [weighings[a[0]]]
+                return subtractions(a) + [(load_wt, span(a[0]))]
+            if f is store:
+                return [weighings[a]]
             return []
 
         vector_banks, scalar_banks, wt_banks = list(VECTOR_BANKS), list(SCALAR_BANKS), [WT_BANK]

@@ -326,24 +326,24 @@ def tile_nmr_relaxometry_residual_s7_kernel(tc, k1, dist, k2_bytes, k2_scale, po
             (K(3) + Q4(0, 1)[:3] + [(q_k2, 2, 2)], PL(0, 0, 0, 512) + IL(0, 0, 0, 512)[:1]),
             (Q4(0, 1)[3:] + K(4), [(E, 0), (E, 1)] + IL(0, 0, 0, 512)[1:]),
             ([(q_k1, 0, 2), (q_h, 0)] + K(5), [(E, 2), (E, 3)] + PL(1, 0, 0, 512)[:3]),
-            ([(S, 0), (q_k1, 2, 2)] + Q4(1, 1)[:2] + [(S, 1), (q_k2, 4, 2)], PL(1, 0, 0, 512)[3:] + [(E, 4), (E, 5)] + IL(1, 0, 0, 512)[:1]),
-            ([Q4(1, 1)[2], (S, 2), Q4(1, 1)[3], K(6)[0], (S, 3)], [(E, 6), (E, 7)] + IL(1, 0, 0, 512)[1:]),
-            ([(q_k1, 4, 4), K(6)[1], K(7)[0], (S, 4), (q_h, 1)], PL(2, 0, 0, 512) + PL(2, 1, 0, 512)[:1] + IL(2, 0, 0, 512)[:1]),
-            ([(S, 5), (S, 6), K(7)[1], (W, 6), (S, 7), (q_k2, 6, 2)], IL(2, 0, 0, 512)[1:] + PL(2, 1, 0, 512)[1:]),
-            (five(8)[:2], IL(2, 1, 0, 512)),
-            (five(8)[2:], PL(3, 0, 0, 512) + PL(3, 1, 0, 512)[:1]),
-            ([(q_h, 2)], IL(3, 0, 0, 512)[:1]),
-            ([(S, 13), (S, 14), (S, 15), (S, 16), (S, 17), (W, 16), (W, 17)], PL(3, 1, 0, 512)[1:] + IL(3, 0, 0, 512)[1:]),
-            ([(S, 18), (S, 19), (S, 20), (W, 19), (W, 20), (S, 21), (q_h, 3)], IL(3, 1, 0, 512)),
+            ([(S, 0), (q_k1, 2, 2)] + Q4(1, 1)[2:] + [(S, 1), (q_k2, 4, 2)], PL(1, 0, 0, 512)[3:] + [(E, 4), (E, 5)] + IL(1, 0, 0, 512)[:1] + PL(1, 1, 0, 256)),
+            ([K(6)[0], (S, 2), K(6)[1], K(7)[0], (S, 3)], IL(1, 0, 0, 512)[1:] + [(E, 6), (E, 7)]),
+            ([(q_k1, 4, 4), K(7)[1], (W, 1), (S, 4)], IL(1, 1, 0, 256) + PL(2, 0, 0, 512)),
+            ([(q_h, 1), (S, 5), (S, 6)], PL(2, 1, 0, 512)[:1] + IL(2, 0, 0, 512)),
+            ([(S, 8), (W, 6), (S, 7), (q_k2, 6, 2)], PL(2, 1, 0, 512)[1:]),
+            ([(S, 9), (S, 10), (S, 11), (S, 12)], IL(2, 1, 0, 512)),
+            ([(W, 10), (W, 11), (S, 13), (q_h, 2)], PL(3, 0, 0, 512) + PL(3, 1, 0, 512)[:1]),
+            ([(S, 14), (W, 12), (S, 15), (S, 16), (S, 17)], IL(3, 0, 0, 512)[:1] + PL(3, 1, 0, 512)[1:]),
+            ([(S, 19), (W, 16), (S, 18), (S, 20), (W, 18), (W, 20), (S, 21), (q_h, 3)], IL(3, 0, 0, 512)[1:] + IL(3, 1, 0, 512)),
             (alternate(22, 31)[:-2] + [(S, 31, 0, 256), (S, 31, 256, 512), (W, 30, 256, 512), (W, 31, 0, 256), (W, 31, 256, 512)], []),
         ]
-        spread_after = {PL(2, 0, 0, 512)[0]: (spread_wt, (0, 1)), (W, 11): (spread_wt, (2,)), (W, 20): (spread_wt, (2, 3))}
-        behind = {(T1, 5): [(SG, 0)], (T1, 2): [(T2, 8, 2)], GP(0, 0, 0, 512)[2]: [(T2, 6, 2)], GP(2, 0, 0, 512)[1]: [(SG, 3)], (T1, 6): [(SG, 1)]}
+        spread_after = {(E, 6): (spread_wt, (0, 1)), (W, 12): (spread_wt, (2,)), (W, 20): (spread_wt, (2, 3))}
+        behind = {(T1, 5): [(SG, 0)], (T1, 2): [(T2, 8, 2)], GP(0, 0, 0, 512)[2]: [(T2, 6, 2)], GP(2, 0, 0, 512)[0]: [(SG, 3)], (T1, 6): [(T2, 14, 2)], GP(2, 1, 0, 512)[1]: [(SG, 8)], (SG, 5): [GP(2, 0, 0, 512)[3]], GP(3, 1, 0, 512)[0]: [(SG, 15)], GP(1, 1, 0, 256)[0]: [(SG, 1)]}
         borrowing = GP(1, 0, 0, 512)[2:]
         on_vector = [s[1] for v, a in phases for s in v if s[0] is W]
         tiles = [(weigh_gpsimd, n) for n in range(len(UNITS)) if n not in on_vector] + [(weigh_gpsimd, 30, 0, 256)]
         gpsimd = [(widen_gpsimd, 3, 1), (widen_gpsimd, 4, 2), (widen_gpsimd, 6, 1), (widen_gpsimd, 7, 1)] + [(widen_gpsimd, r, 2) for r in range(8, 16, 2)] + tiles
-        opening = [(warm_up, 4, 0), (T2, 0, 1), (T2, 1, 1), (warm_up, 2, 1), (T2, 2, 2), (TD, 0, 0), (TD, 0, 1), (warm_up, 1, 2), (T2, 4, 2), (TD, 1, 0), (TD, 1, 1)]
+        opening = [(warm_up, 4, 0), (T2, 0, 1), (T2, 1, 1), (warm_up, 1, 1), (T2, 2, 2), (TD, 0, 0), (TD, 0, 1), (warm_up, 1, 2), (T2, 4, 2), (TD, 1, 0), (TD, 1, 1)]
         sync = [(load_k2, 0, 1), (load_k2, 1, 1), (load_k2, 2, 2), (load_scale,), (load_dist, 0, 0), (load_k2, 4, 2), (load_dist, 0, 1), (load_k2, 6, 2), (load_pol,), (load_dist, 1, 0), (load_dist, 1, 1)]
         sync += [(load_k2, 8, 2), (load_k2, 10, 2), (load_k1, 0), (load_k1, 1), (load_k2, 12, 2), (load_k2, 14, 2)] + steps(load_k1, count=6, first=2) + [(load_data, 0, 0), (load_wt, 0), (load_data, 0, 1)]
         for b in range(1, N2 // BANK):

@@ -327,18 +327,21 @@ def tile_nmr_relaxometry_residual_s7_kernel(tc, k1, dist, k2_bytes, k2_scale, po
             (Q4(0, 1)[3:] + K(4), [(E, 0), (E, 1)] + IL(0, 0, 0, 512)[1:]),
             ([(q_k1, 0, 2), (q_h, 0)] + K(5), [(E, 2), (E, 3)] + PL(1, 0, 0, 512)[:3]),
             ([(S, 0), (q_k1, 2, 2)] + Q4(1, 1)[2:] + [(S, 1), (q_k2, 4, 2)], PL(1, 0, 0, 512)[3:] + [(E, 4), (E, 5)] + IL(1, 0, 0, 512)[:1] + PL(1, 1, 0, 256)),
-            ([K(6)[0], (S, 2), K(6)[1], K(7)[0], (S, 3)], IL(1, 0, 0, 512)[1:] + [(E, 6), (E, 7)]),
-            ([(q_k1, 4, 4), K(7)[1], (W, 1), (S, 4)], IL(1, 1, 0, 256) + PL(2, 0, 0, 512)),
-            ([(q_h, 1), (S, 5), (S, 6)], PL(2, 1, 0, 512)[:1] + IL(2, 0, 0, 512)),
-            ([(S, 8), (W, 6), (S, 7), (q_k2, 6, 2)], PL(2, 1, 0, 512)[1:]),
-            ([(S, 9), (S, 10), (S, 11), (S, 12)], IL(2, 1, 0, 512)),
-            ([(W, 10), (W, 11), (S, 13), (q_h, 2)], PL(3, 0, 0, 512) + PL(3, 1, 0, 512)[:1]),
-            ([(S, 14), (W, 12), (S, 15), (S, 16), (S, 17)], IL(3, 0, 0, 512)[:1] + PL(3, 1, 0, 512)[1:]),
-            ([(S, 19), (W, 16), (S, 18), (S, 20), (W, 18), (W, 20), (S, 21), (q_h, 3)], IL(3, 0, 0, 512)[1:] + IL(3, 1, 0, 512)),
-            (alternate(22, 31)[:-2] + [(S, 31, 0, 256), (S, 31, 256, 512), (W, 30, 256, 512), (W, 31, 0, 256), (W, 31, 256, 512)], []),
+            ([(S, 2)] + K(6) + K(7), IL(1, 0, 0, 512)[1:] + [(E, 6), (E, 7)]),
+            ([(q_k1, 4, 4)], IL(1, 1, 0, 256) + PL(2, 0, 0, 512)[:1]),
+            ([(q_h, 1), (q_k2, 6, 2)], PL(2, 0, 0, 512)[1:]),
+            ([(S, 3), (S, 4), (S, 5)], PL(2, 1, 0, 512)[:1] + IL(2, 0, 0, 512)[:1]),
+            ([(S, 6), (W, 5), (S, 7)], PL(2, 1, 0, 512)[1:]),
+            ([(S, 8), (S, 9), (W, 7), (S, 10), (S, 11), (W, 9)], IL(2, 0, 0, 512)[1:] + IL(2, 1, 0, 512)),
+            ([(W, 11), (S, 12), (q_h, 2)], PL(3, 0, 0, 512)),
+            ([(S, 13), (S, 14), (S, 15)], PL(3, 1, 0, 512)[:1] + IL(3, 0, 0, 512)[:1]),
+            ([(S, 16), (S, 17), (S, 18)], PL(3, 1, 0, 512)[1:]),
+            ([(W, 16), (S, 19), (S, 20), (W, 18), (S, 21), (W, 20), (S, 22), (S, 23), (q_h, 3)], IL(3, 0, 0, 512)[1:] + IL(3, 1, 0, 512)),
+            ([(W, 21), (W, 22)] + alternate(24, 31)[:-2] + [(S, 31, 0, 256), (S, 31, 256, 512), (W, 30, 256, 512), (W, 31, 0, 256), (W, 31, 256, 512)], []),
         ]
-        spread_after = {(E, 6): (spread_wt, (0, 1)), (W, 12): (spread_wt, (2,)), (W, 20): (spread_wt, (2, 3))}
-        behind = {(T1, 5): [(SG, 0)], (T1, 2): [(T2, 8, 2)], GP(0, 0, 0, 512)[2]: [(T2, 6, 2)], GP(2, 0, 0, 512)[0]: [(SG, 3)], (T1, 6): [(T2, 14, 2)], GP(2, 1, 0, 512)[1]: [(SG, 8)], (SG, 5): [GP(2, 0, 0, 512)[3]], GP(3, 1, 0, 512)[0]: [(SG, 15)], GP(1, 1, 0, 256)[0]: [(SG, 1)]}
+        spread_after = {PL(2, 0, 0, 512)[1]: (spread_wt, (0, 1)), (W, 11): (spread_wt, (2,)), (W, 20): (spread_wt, (2, 3))}
+        behind = {(T1, 5): [(SG, 0)], (T1, 2): [(T2, 8, 2)], GP(0, 0, 0, 512)[2]: [(T2, 6, 2)], (T1, 6): [(T2, 14, 2)], GP(1, 1, 0, 256)[0]: [(SG, 1)], (SG, 6): GP(2, 1, 0, 512)[:1]}
+        behind.update({GP(3, 1, 0, 512)[k]: [(SG, 15 + k)] for k in (1, 2, 3)})
         borrowing = GP(1, 0, 0, 512)[2:]
         on_vector = [s[1] for v, a in phases for s in v if s[0] is W]
         tiles = [(weigh_gpsimd, n) for n in range(len(UNITS)) if n not in on_vector] + [(weigh_gpsimd, 30, 0, 256)]

@@ -20,19 +20,18 @@ P = 128
 BANK = 512
 CHUNK = 256
 CHUNKS = N2 // CHUNK
+BLOCKS = N2 // BANK
 ROW_TILES = N1 // P
+TILES = BLOCKS * ROW_TILES
 GROUPS = J1 // 512
-WIDTHS = (512, 512, 512, 512)
 RESULT_BUFS = 16
 PLANE_BUFS = 3
-CODE_BUFS = 2
 H_BUFS = 2
 SCALAR_LEAD = 1
+FIRST_WARM_UPS = 3
 VECTOR_BANKS = (0, 1, 2, 3)
 SCALAR_BANKS = (4, 5, 6, 7)
 WT_BANK = 7
-STARTS = tuple(sum(WIDTHS[:b]) for b in range(len(WIDTHS)))
-UNITS = tuple((b, i) for b, w in enumerate(WIDTHS) for i in range(0, ROW_TILES, BANK // w))
 
 
 def tile_nmr_relaxometry_residual_s7_kernel(tc, k1, dist, k2_bytes, k2_scale, pol, data, wt, out):
@@ -45,7 +44,6 @@ def tile_nmr_relaxometry_residual_s7_kernel(tc, k1, dist, k2_bytes, k2_scale, po
         ctx.enter_context(tc.manual_schedule())
 
         ident = keep.tile([P, P], F32, name="ident")
-        zeros = keep.tile([P, P], F32, name="zeros")
         ident_bf = keep.tile([P, P], BF16, name="ident_bf")
         scale4 = keep.tile([P, 4], F32, name="scale4")
         pol_bf = keep.tile([P, 4 * GROUPS], BF16, name="pol_bf")
@@ -81,25 +79,18 @@ def tile_nmr_relaxometry_residual_s7_kernel(tc, k1, dist, k2_bytes, k2_scale, po
             k1_sb[i] = keep.tile([P, J1], BF16, name="k1_sb%d" % i)
             nc.sync.dma_start(out=k1_sb[i][:], in_=k1[i * P : (i + 1) * P, :])
 
-        def load_data(s, h):
-            data_sb[s, h] = keep.tile([P, 4, BANK], BF16, name="data_sb%d_%d" % (s, h))
-            rows = data[h * 512 : (h + 1) * 512, s * BANK : (s + 1) * BANK]
-            nc.sync.dma_start(out=data_sb[s, h][:], in_=rows.rearrange("(i p) m -> p i m", p=P))
+        def load_data(b, h):
+            data_sb[b, h] = keep.tile([P, 4, BANK], BF16, name="data_sb%d_%d" % (b, h))
+            rows = data[h * 512 : (h + 1) * 512, b * BANK : (b + 1) * BANK]
+            nc.sync.dma_start(out=data_sb[b, h][:], in_=rows.rearrange("(i p) m -> p i m", p=P))
 
-        def load_wt(s):
-            wt_sb[s] = keep.tile([P, BANK], BF16, name="wt_sb%d" % s)
-            nc.sync.dma_start(out=wt_sb[s][:], in_=wt[s * BANK : (s + 1) * BANK].partition_broadcast(P))
-
-        def span(n):
-            return STARTS[UNITS[n][0]] // BANK
-
-        def within_span(n):
-            b = UNITS[n][0]
-            return slice(STARTS[b] % BANK, STARTS[b] % BANK + WIDTHS[b])
+        def load_wt(b):
+            wt_sb[b] = keep.tile([P, BANK], BF16, name="wt_sb%d" % b)
+            nc.sync.dma_start(out=wt_sb[b][:], in_=wt[b * BANK : (b + 1) * BANK].partition_broadcast(P))
 
         def store(n, lo=0, up=BANK):
-            b, i = UNITS[n]
-            nc.sync.dma_start(out=out[i * P : (i + 1) * P, STARTS[b] + lo : STARTS[b] + up], in_=result[n][:, lo:up])
+            b, i = divmod(n, ROW_TILES)
+            nc.sync.dma_start(out=out[i * P : (i + 1) * P, b * BANK + lo : b * BANK + up], in_=result[n][:, lo:up])
 
         def new_bank(bank, shape, dtype):
             return psum.tile(shape, dtype, name="bank%d" % bank)
@@ -110,7 +101,7 @@ def tile_nmr_relaxometry_residual_s7_kernel(tc, k1, dist, k2_bytes, k2_scale, po
                 for u in (0, 1):
                     nc.tensor.transpose(filled[name][:, a, u, :], run.bitcast(F32)[:, u : 256 : 2], ident[:])
 
-        def halves(rows):
+        def two_runs(rows):
             return [rows[:, 0:512], rows[:, 512:1024]]
 
         def turn_k2(r, count, bank):
@@ -119,10 +110,10 @@ def tile_nmr_relaxometry_residual_s7_kernel(tc, k1, dist, k2_bytes, k2_scale, po
                 filled["k2 tile", r + e] = filled["k2", r][:, e]
 
         def turn_dist(g, h, bank):
-            turn_words(("dist", g, h), halves(dist_sb[g, h]), bank)
+            turn_words(("dist", g, h), two_runs(dist_sb[g, h]), bank)
 
         def turn_k1(i, bank):
-            turn_words(("k1", i), halves(k1_sb[i]), bank)
+            turn_words(("k1", i), two_runs(k1_sb[i]), bank)
 
         def mx(dst, lhs_codes, lhs_scales, rhs_codes, rhs_scales, start, stop):
             nc.tensor.matmul_mx(
@@ -142,39 +133,46 @@ def tile_nmr_relaxometry_residual_s7_kernel(tc, k1, dist, k2_bytes, k2_scale, po
         def g_quarter(b, g, q, bank):
             filled["quarter", b, g, q] = new_bank(bank, [P, 4, P], F32)
             for t in range(4):
-                first_product(filled["quarter", b, g, q][:, t, :], g, t, slice(STARTS[b] + q * P, STARTS[b] + (q + 1) * P))
+                first_product(filled["quarter", b, g, q][:, t, :], g, t, slice(b * BANK + q * P, b * BANK + (q + 1) * P))
 
         def g_planes(b, g, lo, w, k, bank):
             count = BANK // w
             filled["planes", b, g, lo, k] = new_bank(bank, [P, count, w], F32)
             for e in range(count):
-                first_product(filled["planes", b, g, lo, k][:, e, :], g, count * k + e, slice(STARTS[b] + lo, STARTS[b] + lo + w))
+                first_product(filled["planes", b, g, lo, k][:, e, :], g, count * k + e, slice(b * BANK + lo, b * BANK + lo + w))
 
         def signal(n, bank):
-            b, i = UNITS[n]
-            w = WIDTHS[b]
-            filled["signal", n] = new_bank(bank, [P, BANK // w, w], F32)
-            for e in range(BANK // w):
-                for g in range(GROUPS):
-                    c, m = slice((GROUPS * (i + e) + g) * P, (GROUPS * (i + e) + g + 1) * P), slice(g * w, (g + 1) * w)
-                    mx(filled["signal", n][:, e, :], k1_codes[:, c], k1_scales[:, c], h_codes[b][:, m], h_scales[b][:, m], g == 0, g == GROUPS - 1)
+            b, i = divmod(n, ROW_TILES)
+            filled["signal", n] = new_bank(bank, [P, BANK], F32)
+            for g in range(GROUPS):
+                c, m = slice((GROUPS * i + g) * P, (GROUPS * i + g + 1) * P), slice(g * BANK, (g + 1) * BANK)
+                mx(filled["signal", n][:], k1_codes[:, c], k1_scales[:, c], h_codes[b][:, m], h_scales[b][:, m], g == 0, g == GROUPS - 1)
 
-        def spread_wt(spans, bank):
-            tile = new_bank(bank, [P, 2, BANK], BF16)
-            for e, s in enumerate(spans):
-                wt_bank[s] = tile[:, e, :]
-                nc.tensor.matmul(wt_bank[s], lhsT=ident_bf[:], rhs=wt_sb[s][:], start=True, stop=True)
+        def spread_wt(blocks, bank):
+            both = new_bank(bank, [P, 2, BANK], BF16)
+            for e, b in enumerate(blocks):
+                wt_bank[b] = both[:, e, :]
+                nc.tensor.matmul(wt_bank[b], lhsT=ident_bf[:], rhs=wt_sb[b][:], start=True, stop=True)
 
         def warm_up(count, k, bank):
             idle = new_bank(bank, [P, P], F32)
             for r in range(count):
-                nc.tensor.matmul(idle[:], lhsT=zeros[:], rhs=zeros[:], start=True, stop=True)
+                nc.tensor.matmul(idle[:], lhsT=ident[:], rhs=ident[:], start=True, stop=True)
 
         def flat(grouped):
             return grouped.rearrange("p a n t -> p (a n t)")
 
+        def spent(r):
+            return {
+                7: lambda: dist_grouped[0][:, 0:1],
+                8: lambda: dist_grouped[1][:, 0:2],
+                10: lambda: dist_grouped[1][:, 2:4],
+                12: lambda: k2_grouped[:, 4:6],
+                14: lambda: h_grouped[0][:, 0:CHUNK].rearrange("p (a n) t -> p a n t", a=2),
+            }[r]()
+
         def widen(r, count, copy):
-            wide = flat(reuse[r][1]()) if r in reuse else keep.tile([P, count * J2], BF16, name="wide%d" % r)[:]
+            wide = flat(spent(r)) if r in reuse else keep.tile([P, count * J2], BF16, name="wide%d" % r)[:]
             raw, e = k2_raw[r]
             copy(out=wide, in_=raw[:, e : e + count].rearrange("p r l -> p (r l)").bitcast(FP8))
             for e in range(count):
@@ -219,7 +217,7 @@ def tile_nmr_relaxometry_residual_s7_kernel(tc, k1, dist, k2_bytes, k2_scale, po
         def h_columns(b, g, lo, up):
             if b not in h_grouped:
                 h_grouped[b] = turn.tile([P, GROUPS * BANK, 4], BF16, name="h_grouped", align_bytes=64, bufs=H_BUFS)
-            return h_grouped[b][:, g * WIDTHS[b] + lo : g * WIDTHS[b] + up, :]
+            return h_grouped[b][:, g * BANK + lo : g * BANK + up, :]
 
         def h_quarter(b, g, q):
             nc.vector.tensor_tensor(
@@ -259,115 +257,127 @@ def tile_nmr_relaxometry_residual_s7_kernel(tc, k1, dist, k2_bytes, k2_scale, po
             quantise(k1_codes[:, c], k1_scales[:, c], flat(k1_grouped[:, GROUPS * i : GROUPS * (i + count)]))
 
         def q_h(b):
-            m = slice(0, GROUPS * WIDTHS[b])
-            h_codes[b] = turn.tile([P, GROUPS * BANK], U32, name="h_codes", align_bytes=64, bufs=CODE_BUFS)
-            h_scales[b] = turn.tile([P, GROUPS * BANK], U8, name="h_scales", align_bytes=64, bufs=CODE_BUFS)
-            quantise(h_codes[b][:, m], h_scales[b][:, m], h_grouped[b][:, m, :].rearrange("p n t -> p (n t)"))
+            h_codes[b] = turn.tile([P, GROUPS * BANK], U32, name="h_codes", align_bytes=64, bufs=H_BUFS)
+            h_scales[b] = turn.tile([P, GROUPS * BANK], U8, name="h_scales", align_bytes=64, bufs=H_BUFS)
+            quantise(h_codes[b][:], h_scales[b][:], h_grouped[b][:].rearrange("p n t -> p (n t)"))
 
         def subtract(n, lo=0, up=BANK):
-            b, i = UNITS[n]
+            b, i = divmod(n, ROW_TILES)
             if lo == 0:
                 result[n] = results.tile([P, BANK], F32, name="result")
-            nc.vector.tensor_tensor(out=result[n][:, lo:up], in0=filled["signal", n][:, 0, lo:up], in1=data_sb[b, i // 4][:, i % 4, lo:up], op=SUB)
+            nc.vector.tensor_tensor(out=result[n][:, lo:up], in0=filled["signal", n][:, lo:up], in1=data_sb[b, i // 4][:, i % 4, lo:up], op=SUB)
 
         def weigh_vector(n, lo=0, up=BANK):
-            nc.vector.tensor_tensor(out=result[n][:, lo:up], in0=result[n][:, lo:up], in1=wt_bank[span(n)][:, lo:up], op=MULT)
+            nc.vector.tensor_tensor(out=result[n][:, lo:up], in0=result[n][:, lo:up], in1=wt_bank[n // ROW_TILES][:, lo:up], op=MULT)
 
         def weigh_gpsimd(n, lo=0, up=BANK):
-            nc.gpsimd.tensor_tensor(out=result[n][:, lo:up], in0=result[n][:, lo:up], in1=wt_sb[span(n)][:, lo:up], op=MULT)
+            nc.gpsimd.tensor_tensor(out=result[n][:, lo:up], in0=result[n][:, lo:up], in1=wt_sb[n // ROW_TILES][:, lo:up], op=MULT)
 
         def steps(f, *heads, count, first=0):
             return [(f,) + heads + (k,) for k in range(first, first + count)]
 
-        def K(c):
+        def scale_chunk(c):
             return steps(scale_k2, count=2, first=2 * c)
 
-        def PL(b, g, lo, w):
-            return steps(h_planes, b, g, lo, w, count=4 * w // BANK)
+        def quarters(b, g):
+            return steps(h_quarter, b, g, count=4)
 
-        def GP(b, g, lo, w):
-            return steps(g_planes, b, g, lo, w, count=4 * w // BANK)
+        def empty_planes(b, g, w=BANK):
+            return steps(h_planes, b, g, 0, w, count=4 * w // BANK)
 
-        def IL(b, g, lo, w):
-            return steps(group_planes, b, g, lo, count=w // CHUNK)
+        def fill_planes(b, g, w=BANK):
+            return steps(g_planes, b, g, 0, w, count=4 * w // BANK)
 
-        def part(b, g, lo, w):
-            return PL(b, g, lo, w) + IL(b, g, lo, w)
+        def regroup(b, g, w=BANK):
+            return steps(group_planes, b, g, 0, count=w // CHUNK)
 
-        def Q(b, g, first):
-            return steps(h_quarter, b, g, count=2, first=first)
+        def subs(first, last):
+            return steps(subtract, count=last - first + 1, first=first)
 
-        def GQ(b, g, first):
-            return steps(g_quarter, b, g, count=2, first=first)
+        def weigh(*tiles):
+            return [(weigh_vector, n) for n in tiles]
 
-        S, W, E, T2, T1, SG = subtract, weigh_vector, group_k1, turn_k2, turn_k1, signal
-
-        def Q4(b, g):
-            return Q(b, g, 0) + Q(b, g, 2)
-
-        def five(first):
-            subs = [(S, n) for n in range(first, first + 5)]
-            return subs[:4] + [(W, first + 1), (W, first + 3)] + subs[4:]
-
-        def alternate(first, last):
-            order = [(S, first)]
+        def in_turn(first, last):
+            order = subs(first, first)
             for n in range(first + 1, last, 2):
-                order.extend([(S, n), (S, n + 1), (W, n)])
-            return order + [(S, last), (W, last)]
+                order = order + subs(n, n + 1) + weigh(n)
+            return order
 
-        D, TD = group_dist, turn_dist
+        def by_halves(f, n):
+            return [(f, n, 0, CHUNK), (f, n, CHUNK, BANK)]
 
-        turns = [(T2, 0, 1), (T2, 1, 1)] + [(T2, r, 2) for r in range(2, 16, 2)]
-        reuse = {7: ((q_dist, 0), lambda: dist_grouped[0][:, 0:1]), 8: ((q_dist, 1), lambda: dist_grouped[1][:, 0:2]), 10: ((q_dist, 1), lambda: dist_grouped[1][:, 2:4])}
-        reuse.update({12: ((q_k2, 2, 2), lambda: k2_grouped[:, 4:6]), 14: ((q_h, 0), lambda: h_grouped[0][:, 0:CHUNK].rearrange("p (a n) t -> p a n t", a=2))})
         phases = [
-            ([(widen_vector, 0, 1), (widen_vector, 1, 1)] + K(0) + K(1) + [(q_k2, 0, 1), (q_k2, 1, 1), (q_dist, 0)] + K(2) + [(q_dist, 1)],
-             [(widen_scalar, 2, 1), (ident_to_bf16,)] + steps(D, 0, count=2) + [(pol_to_f32,)] + steps(D, 1, count=2)),
-            (K(3) + Q4(0, 1)[:3] + [(q_k2, 2, 2)], PL(0, 0, 0, 512) + IL(0, 0, 0, 512)[:1]),
-            (Q4(0, 1)[3:] + K(4), [(E, 0), (E, 1)] + IL(0, 0, 0, 512)[1:]),
-            ([(q_k1, 0, 2), (q_h, 0)] + K(5), [(E, 2), (E, 3)] + PL(1, 0, 0, 512)[:3]),
-            ([(S, 0), (q_k1, 2, 2)] + Q4(1, 1)[2:] + [(S, 1), (q_k2, 4, 2)], PL(1, 0, 0, 512)[3:] + [(E, 4), (E, 5)] + IL(1, 0, 0, 512)[:1] + PL(1, 1, 0, 256)),
-            ([(S, 2)] + K(6) + K(7), IL(1, 0, 0, 512)[1:] + [(E, 6), (E, 7)]),
-            ([(q_k1, 4, 4)], IL(1, 1, 0, 256) + PL(2, 0, 0, 512)[:1]),
-            ([(q_h, 1), (q_k2, 6, 2)], PL(2, 0, 0, 512)[1:]),
-            ([(S, 3), (S, 4), (S, 5)], PL(2, 1, 0, 512)[:1] + IL(2, 0, 0, 512)[:1]),
-            ([(S, 6), (W, 5), (S, 7)], PL(2, 1, 0, 512)[1:]),
-            ([(S, 8), (S, 9), (W, 7), (S, 10), (S, 11), (W, 9)], IL(2, 0, 0, 512)[1:] + IL(2, 1, 0, 512)),
-            ([(W, 11), (S, 12), (q_h, 2)], PL(3, 0, 0, 512)),
-            ([(S, 13), (S, 14), (S, 15)], PL(3, 1, 0, 512)[:1] + IL(3, 0, 0, 512)[:1]),
-            ([(S, 16), (S, 17), (S, 18)], PL(3, 1, 0, 512)[1:]),
-            ([(W, 16), (S, 19), (S, 20), (W, 18), (S, 21), (W, 20), (S, 22), (S, 23), (q_h, 3)], IL(3, 0, 0, 512)[1:] + IL(3, 1, 0, 512)),
-            ([(W, 21), (W, 22)] + alternate(24, 31)[:-2] + [(S, 31, 0, 256), (S, 31, 256, 512), (W, 30, 256, 512), (W, 31, 0, 256), (W, 31, 256, 512)], []),
+            (
+                [(widen_vector, 0, 1), (widen_vector, 1, 1)] + scale_chunk(0) + scale_chunk(1)
+                + [(q_k2, 0, 1), (q_k2, 1, 1), (q_dist, 0)] + scale_chunk(2) + [(q_dist, 1)],
+                [(widen_scalar, 2, 1), (ident_to_bf16,)] + steps(group_dist, 0, count=2) + [(pol_to_f32,)] + steps(group_dist, 1, count=2),
+            ),
+            (scale_chunk(3) + quarters(0, 1)[:3] + [(q_k2, 2, 2)], empty_planes(0, 0) + regroup(0, 0)[:1]),
+            (quarters(0, 1)[3:] + scale_chunk(4), steps(group_k1, count=2) + regroup(0, 0)[1:]),
+            ([(q_k1, 0, 2), (q_h, 0)] + scale_chunk(5), steps(group_k1, count=2, first=2) + empty_planes(1, 0)[:3]),
+            (
+                subs(0, 0) + [(q_k1, 2, 2)] + quarters(1, 1)[2:] + subs(1, 1) + [(q_k2, 4, 2)],
+                empty_planes(1, 0)[3:] + steps(group_k1, count=2, first=4) + regroup(1, 0)[:1] + empty_planes(1, 1, CHUNK),
+            ),
+            (subs(2, 2) + scale_chunk(6) + scale_chunk(7), regroup(1, 0)[1:] + steps(group_k1, count=2, first=6)),
+            ([(q_k1, 4, 4)], regroup(1, 1, CHUNK) + empty_planes(2, 0)[:1]),
+            ([(q_h, 1), (q_k2, 6, 2)], empty_planes(2, 0)[1:]),
+            (subs(3, 5), empty_planes(2, 1)[:1] + regroup(2, 0)[:1]),
+            (subs(6, 6) + weigh(5) + subs(7, 7), empty_planes(2, 1)[1:]),
+            (subs(8, 9) + weigh(7) + subs(10, 11) + weigh(9), regroup(2, 0)[1:] + regroup(2, 1)),
+            (weigh(11) + subs(12, 12) + [(q_h, 2)], empty_planes(3, 0)),
+            (subs(13, 15), empty_planes(3, 1)[:1] + regroup(3, 0)[:1]),
+            (subs(16, 18), empty_planes(3, 1)[1:]),
+            (
+                weigh(16) + subs(19, 20) + weigh(18) + subs(21, 21) + weigh(20) + subs(22, 23) + [(q_h, 3)],
+                regroup(3, 0)[1:] + regroup(3, 1),
+            ),
+            (
+                weigh(21, 22) + in_turn(24, 31) + by_halves(subtract, 31) + by_halves(weigh_vector, 30)[1:] + by_halves(weigh_vector, 31),
+                [],
+            ),
         ]
-        spread_after = {PL(2, 0, 0, 512)[1]: (spread_wt, (0, 1)), (W, 11): (spread_wt, (2,)), (W, 20): (spread_wt, (2, 3))}
-        behind = {(T1, 5): [(SG, 0)], (T1, 2): [(T2, 8, 2)], GP(0, 0, 0, 512)[2]: [(T2, 6, 2)], (T1, 6): [(T2, 14, 2)], GP(1, 1, 0, 256)[0]: [(SG, 1)], (SG, 6): GP(2, 1, 0, 512)[:1]}
-        behind.update({GP(3, 1, 0, 512)[k]: [(SG, 15 + k)] for k in (1, 2, 3)})
-        borrowing = GP(1, 0, 0, 512)[2:]
-        on_vector = [s[1] for v, a in phases for s in v if s[0] is W]
-        tiles = [(weigh_gpsimd, n) for n in range(len(UNITS)) if n not in on_vector] + [(weigh_gpsimd, 30, 0, 256)]
-        gpsimd = [(widen_gpsimd, 3, 1), (widen_gpsimd, 4, 2), (widen_gpsimd, 6, 1), (widen_gpsimd, 7, 1)] + [(widen_gpsimd, r, 2) for r in range(8, 16, 2)] + tiles
-        opening = [(warm_up, 4, 0), (T2, 0, 1), (T2, 1, 1), (warm_up, 1, 1), (T2, 2, 2), (TD, 0, 0), (TD, 0, 1), (warm_up, 1, 2), (T2, 4, 2), (TD, 1, 0), (TD, 1, 1)]
-        sync = [(load_k2, 0, 1), (load_k2, 1, 1), (load_k2, 2, 2), (load_scale,), (load_dist, 0, 0), (load_k2, 4, 2), (load_dist, 0, 1), (load_k2, 6, 2), (load_pol,), (load_dist, 1, 0), (load_dist, 1, 1)]
-        sync += [(load_k2, 8, 2), (load_k2, 10, 2), (load_k1, 0), (load_k1, 1), (load_k2, 12, 2), (load_k2, 14, 2)] + steps(load_k1, count=6, first=2) + [(load_data, 0, 0), (load_wt, 0), (load_data, 0, 1)]
-        for b in range(1, N2 // BANK):
-            sync += [(load_wt, b), (load_data, b, 0), (load_data, b, 1)]
-        sync += steps(store, count=30) + [(store, n, lo, lo + 256) for n in (30, 31) for lo in (0, 256)]
+        spread_after = {empty_planes(2, 0)[1]: (spread_wt, (0, 1)), weigh(11)[0]: (spread_wt, (2,)), weigh(20)[0]: (spread_wt, (2, 3))}
+        behind = {
+            fill_planes(0, 0)[2]: (turn_k2, 6, 2),
+            (turn_k1, 2): (turn_k2, 8, 2),
+            (turn_k1, 5): (signal, 0),
+            fill_planes(1, 1, CHUNK)[0]: (signal, 1),
+            (turn_k1, 6): (turn_k2, 14, 2),
+            (signal, 6): fill_planes(2, 1)[0],
+        }
+        behind.update(zip(fill_planes(3, 1)[1:], steps(signal, count=3, first=16)))
+        borrowing = fill_planes(1, 0)[2:]
+        turns = [(turn_k2, 0, 1), (turn_k2, 1, 1)] + [(turn_k2, r, 2) for r in range(2, 2 * CHUNKS, 2)]
+        reuse = {7: (q_dist, 0), 8: (q_dist, 1), 10: (q_dist, 1), 12: (q_k2, 2, 2), 14: (q_h, 0)}
+        on_vector = [s[1] for v, a in phases for s in v if s[0] is weigh_vector]
+        gpsimd = [(widen_gpsimd, 3, 1), (widen_gpsimd, 4, 2), (widen_gpsimd, 6, 1), (widen_gpsimd, 7, 1)]
+        gpsimd += [(widen_gpsimd, r, 2) for r in range(8, 2 * CHUNKS, 2)]
+        gpsimd += [(weigh_gpsimd, n) for n in range(TILES) if n not in on_vector] + by_halves(weigh_gpsimd, 30)[:1]
+        opening = [(warm_up, FIRST_WARM_UPS, 0)] + turns[:2] + [(warm_up, 1, 1), turns[2]] + steps(turn_dist, 0, count=2)
+        opening += [(warm_up, 1, 2), turns[3]] + steps(turn_dist, 1, count=2)
+        sync = [(load_k2, 0, 1), (load_k2, 1, 1), (load_k2, 2, 2), (load_scale,), (load_dist, 0, 0), (load_k2, 4, 2), (load_dist, 0, 1)]
+        sync += [(load_k2, 6, 2), (load_pol,)] + steps(load_dist, 1, count=2) + [(load_k2, 8, 2), (load_k2, 10, 2)]
+        sync += steps(load_k1, count=2) + [(load_k2, 12, 2), (load_k2, 14, 2)] + steps(load_k1, count=6, first=2)
+        sync += [(load_data, 0, 0), (load_wt, 0), (load_data, 0, 1)]
+        for b in range(1, BLOCKS):
+            sync += [(load_wt, b)] + steps(load_data, b, count=2)
+        sync += steps(store, count=TILES - 2) + by_halves(store, 30) + by_halves(store, 31)
 
         maker = {scale_k2: turn_k2, group_dist: turn_dist, group_k1: turn_k1, h_quarter: g_quarter, h_planes: g_planes, subtract: signal}
         vector, scalar = [s for v, a in phases for s in v], [s for v, a in phases for s in a]
         every = vector + scalar + gpsimd
 
         def made_by(step):
-            return covering(turns, step[1])[0] if step[0] is scale_k2 else (maker[step[0]],) + (step[1:2] if step[0] is subtract else step[1:])
+            if step[0] is scale_k2:
+                return covering(turns, step[1])[0]
+            return (maker[step[0]],) + (step[1:2] if step[0] is subtract else step[1:])
 
         def covering(among, k):
             return [s for s in among if s[1] <= k < s[1] + s[2]]
 
         def all_of(f, among):
             return [s for s in among if s[0] is f]
-
-        def units_of(b):
-            return [n for n in range(len(UNITS)) if UNITS[n][0] == b]
 
         widenings = [s for s in every if s[0] in (widen_vector, widen_scalar, widen_gpsimd)]
         weighings = {s[1:]: s for s in every if s[0] in (weigh_vector, weigh_gpsimd)}
@@ -391,7 +401,7 @@ def tile_nmr_relaxometry_residual_s7_kernel(tc, k1, dist, k2_bytes, k2_scale, po
         def needs(step):
             f, a = step[0], step[1:]
             if step in widenings:
-                earlier = [reuse[a[0]][0]] if a[0] in reuse else []
+                earlier = [reuse[a[0]]] if a[0] in reuse else []
                 return covering(all_of(load_k2, sync), a[0]) + earlier
             if f is turn_k2:
                 return [s for r in range(a[0], a[0] + a[1]) for s in covering(widenings, r)]
@@ -401,16 +411,16 @@ def tile_nmr_relaxometry_residual_s7_kernel(tc, k1, dist, k2_bytes, k2_scale, po
                 return [(load_k1,) + a]
             if f in (g_quarter, g_planes):
                 lo, w = (a[2] * P, P) if f is g_quarter else a[2:4]
-                first, last = (STARTS[a[0]] + lo) // CHUNK, (STARTS[a[0]] + lo + w - 1) // CHUNK
+                first, last = (a[0] * BANK + lo) // CHUNK, (a[0] * BANK + lo + w - 1) // CHUNK
                 return covering(all_of(q_k2, vector), first) + covering(all_of(q_k2, vector), last) + [(q_dist, a[1])]
             if f is signal:
-                b, i = UNITS[a[0]]
-                return [(q_h, b)] + covering(all_of(q_k1, vector), i) + covering(all_of(q_k1, vector), i + BANK // WIDTHS[b] - 1)
+                b, i = divmod(a[0], ROW_TILES)
+                return [(q_h, b)] + covering(all_of(q_k1, vector), i)
             if f is spread_wt:
                 return [(ident_to_bf16,)] + [(load_wt, b) for b in a[0]]
             h_free = []
             if f in (h_quarter, group_planes) and a[0] >= H_BUFS:
-                h_free = [(q_h, a[0] - H_BUFS)] + [covering(turns, c)[0] for c in reuse if reuse[c][0] == (q_h, a[0] - H_BUFS)]
+                h_free = [(q_h, a[0] - H_BUFS)] + [covering(turns, r)[0] for r in reuse if reuse[r] == (q_h, a[0] - H_BUFS)]
             if f is h_quarter:
                 return [made_by(step), (pol_to_f32,)] + h_free
             if f is h_planes:
@@ -420,8 +430,8 @@ def tile_nmr_relaxometry_residual_s7_kernel(tc, k1, dist, k2_bytes, k2_scale, po
             if f is group_planes:
                 return [s for s in scalar if s[0] is h_planes and s[1:4] == a[:3]] + h_free
             if f is subtract:
-                b, i = UNITS[a[0]]
-                return [made_by(step), (load_data, span(a[0]), i // 4)] + ([(store, a[0] - RESULT_BUFS)] if a[0] >= RESULT_BUFS else [])
+                b, i = divmod(a[0], ROW_TILES)
+                return [made_by(step), (load_data, b, i // 4)] + ([(store, a[0] - RESULT_BUFS)] if a[0] >= RESULT_BUFS else [])
             if f is scale_k2:
                 return [made_by(step), (load_scale,)]
             if f in maker:
@@ -436,11 +446,11 @@ def tile_nmr_relaxometry_residual_s7_kernel(tc, k1, dist, k2_bytes, k2_scale, po
                 return steps(group_k1, count=a[1], first=a[0])
             if f is q_h:
                 writers = [s for s in every if s[0] in (h_quarter, group_planes) and s[1] == a[0]]
-                return writers + ([(signal, n) for n in units_of(a[0] - CODE_BUFS)] if a[0] >= CODE_BUFS else [])
+                return writers + (steps(signal, count=ROW_TILES, first=(a[0] - H_BUFS) * ROW_TILES) if a[0] >= H_BUFS else [])
             if f is weigh_vector:
                 return subtractions(a) + [spread_for(step)]
             if f is weigh_gpsimd:
-                return subtractions(a) + [(load_wt, span(a[0]))]
+                return subtractions(a) + [(load_wt, a[0] // ROW_TILES)]
             if f is store:
                 return [weighings[a]]
             return []
@@ -457,7 +467,8 @@ def tile_nmr_relaxometry_residual_s7_kernel(tc, k1, dist, k2_bytes, k2_scale, po
             return [bank for bank in banks_for(step) if all(s in written for s in readers.get(last_fill.get(bank), []))]
 
         def ready(step):
-            return all(s in written for s in needs(step) + behind.get(step, [])) and (step[0] not in banks_of or free_banks(step))
+            ahead = needs(step) + ([behind[step]] if step in behind else [])
+            return all(s in written for s in ahead) and (step[0] not in banks_of or free_banks(step))
 
         def write(step):
             if step[0] in banks_of:
@@ -480,20 +491,17 @@ def tile_nmr_relaxometry_residual_s7_kernel(tc, k1, dist, k2_bytes, k2_scale, po
         def banks_worth(step):
             f = step[0]
             if f in (q_k2, q_k1):
-                return step[2] * 0.5
-            if f is q_h:
-                return WIDTHS[step[1]] // CHUNK
-            return 2 if f is group_planes else 1
+                return step[2] / 2
+            return 2 if f in (q_h, group_planes) else 1
 
         waiting = {"sync": list(sync), "opening": list(opening), "for vector": fills(vector), "for scalar": fills(scalar), "wt": [], "gpsimd": list(gpsimd)}
 
         def follow():
-            for name, queue in waiting.items():
-                held = name in ("for vector", "for scalar") and waiting["opening"]
+            for whose, queue in waiting.items():
+                held = whose in ("for vector", "for scalar") and waiting["opening"]
                 while queue and not held and ready(queue[0]):
                     write(queue.pop(0))
 
-        nc.vector.memset(zeros[:], 0.0)
         make_identity(nc, ident[:])
         for v, a in phases:
             v, a = list(v), list(a)

@@ -18,20 +18,19 @@ COPY = mybir.ActivationFunctionType.Copy
 
 P = 128
 BANK = 512
+HALF = BANK // 2
 CHUNK = 256
 CHUNKS = N2 // CHUNK
 BLOCKS = N2 // BANK
 ROW_TILES = N1 // P
-TILES = BLOCKS * ROW_TILES
+UPPER = ROW_TILES // 2
 GROUPS = J1 // 512
-RESULT_BUFS = 16
+RESULT_BUFS = 12
 PLANE_BUFS = 3
 H_BUFS = 2
-SCALAR_LEAD = 1
-FIRST_WARM_UPS = 3
+STRIP_BUFS = 4
 VECTOR_BANKS = (0, 1, 2, 3)
 SCALAR_BANKS = (4, 5, 6, 7)
-WT_BANK = 7
 
 
 def tile_nmr_relaxometry_residual_s7_kernel(tc, k1, dist, k2_bytes, k2_scale, pol, data, wt, out):
@@ -51,12 +50,14 @@ def tile_nmr_relaxometry_residual_s7_kernel(tc, k1, dist, k2_bytes, k2_scale, po
         k2_grouped = keep.tile([P, 2 * CHUNKS, P, 4], BF16, name="k2_grouped", align_bytes=64)
         k2_codes = keep.tile([P, N2], U32, name="k2_codes", align_bytes=64)
         k2_scales = keep.tile([P, N2], U8, name="k2_scales", align_bytes=64)
-        k1_grouped = keep.tile([P, GROUPS * ROW_TILES, P, 4], BF16, name="k1_grouped", align_bytes=64)
+        k1_upper = keep.tile([P, UPPER, GROUPS, 4 * P], BF16, name="k1_upper", align_bytes=64)
+        k1_lower = keep.tile([P, GROUPS, UPPER, 4 * P], BF16, name="k1_lower", align_bytes=64)
         k1_codes = keep.tile([P, GROUPS * N1], U32, name="k1_codes", align_bytes=64)
         k1_scales = keep.tile([P, GROUPS * N1], U8, name="k1_scales", align_bytes=64)
         k2_raw, k2_wide, dist_sb, k1_sb, data_sb, wt_sb = {}, {}, {}, {}, {}, {}
         dist_grouped, dist_codes, dist_scales = {}, {}, {}
         planes, h_grouped, h_codes, h_scales, result, filled, wt_bank = {}, {}, {}, {}, {}, {}, {}
+        negated, lower_result = {}, {}
 
         def load_k2(r, count):
             raw = keep.tile([P, count, J2], U8, name="k2_raw%d" % r)
@@ -80,7 +81,7 @@ def tile_nmr_relaxometry_residual_s7_kernel(tc, k1, dist, k2_bytes, k2_scale, po
             nc.sync.dma_start(out=k1_sb[i][:], in_=k1[i * P : (i + 1) * P, :])
 
         def load_data(b, h):
-            data_sb[b, h] = keep.tile([P, 4, BANK], BF16, name="data_sb%d_%d" % (b, h))
+            data_sb[b, h] = keep.tile([P, UPPER, BANK], BF16, name="data_sb%d_%d" % (b, h))
             rows = data[h * 512 : (h + 1) * 512, b * BANK : (b + 1) * BANK]
             nc.sync.dma_start(out=data_sb[b, h][:], in_=rows.rearrange("(i p) m -> p i m", p=P))
 
@@ -88,9 +89,14 @@ def tile_nmr_relaxometry_residual_s7_kernel(tc, k1, dist, k2_bytes, k2_scale, po
             wt_sb[b] = keep.tile([P, BANK], BF16, name="wt_sb%d" % b)
             nc.sync.dma_start(out=wt_sb[b][:], in_=wt[b * BANK : (b + 1) * BANK].partition_broadcast(P))
 
-        def store(n, lo=0, up=BANK):
+        def store(n, lo, up):
             b, i = divmod(n, ROW_TILES)
-            nc.sync.dma_start(out=out[i * P : (i + 1) * P, b * BANK + lo : b * BANK + up], in_=result[n][:, lo:up])
+            nc.sync.dma_start(out=out[i * P : (i + 1) * P, b * BANK + lo : b * BANK + up], in_=result[n, lo][:, 0 : up - lo])
+
+        def store_strips(b, first, count, a, rows):
+            m = slice(first * P, (first + count) * P)
+            dst = out[(UPPER + a) * P : (UPPER + a + rows) * P, b * BANK + m.start : b * BANK + m.stop]
+            nc.sync.dma_start(out=dst.rearrange("(i p) m -> p i m", p=P), in_=lower_result[b][:, a : a + rows, m])
 
         def new_bank(bank, shape, dtype):
             return psum.tile(shape, dtype, name="bank%d" % bank)
@@ -115,38 +121,63 @@ def tile_nmr_relaxometry_residual_s7_kernel(tc, k1, dist, k2_bytes, k2_scale, po
         def turn_k1(i, bank):
             turn_words(("k1", i), two_runs(k1_sb[i]), bank)
 
-        def mx(dst, lhs_codes, lhs_scales, rhs_codes, rhs_scales, start, stop):
+        def mx(dst, lhs, lhs_columns, rhs, rhs_columns, start, stop):
             nc.tensor.matmul_mx(
                 out=dst,
-                lhsT=lhs_codes.bitcast(FP8X4),
-                lhsT_scale=lhs_scales,
-                rhs=rhs_codes.bitcast(FP8X4),
-                rhs_scale=rhs_scales,
+                lhsT=lhs[0][:, lhs_columns].bitcast(FP8X4),
+                lhsT_scale=lhs[1][:, lhs_columns],
+                rhs=rhs[0][:, rhs_columns].bitcast(FP8X4),
+                rhs_scale=rhs[1][:, rhs_columns],
                 start=start,
                 stop=stop,
             )
 
+        def span(first, count):
+            return slice(first, first + count)
+
         def first_product(dst, g, t, m):
-            j = slice(t * P, (t + 1) * P)
-            mx(dst, dist_codes[g][:, j], dist_scales[g][:, j], k2_codes[:, m], k2_scales[:, m], True, True)
+            mx(dst, (dist_codes[g], dist_scales[g]), span(t * P, P), (k2_codes, k2_scales), m, True, True)
 
         def g_quarter(b, g, q, bank):
             filled["quarter", b, g, q] = new_bank(bank, [P, 4, P], F32)
             for t in range(4):
-                first_product(filled["quarter", b, g, q][:, t, :], g, t, slice(b * BANK + q * P, b * BANK + (q + 1) * P))
+                first_product(filled["quarter", b, g, q][:, t, :], g, t, span(b * BANK + q * P, P))
 
         def g_planes(b, g, lo, w, k, bank):
             count = BANK // w
             filled["planes", b, g, lo, k] = new_bank(bank, [P, count, w], F32)
             for e in range(count):
-                first_product(filled["planes", b, g, lo, k][:, e, :], g, count * k + e, slice(b * BANK + lo, b * BANK + lo + w))
+                first_product(filled["planes", b, g, lo, k][:, e, :], g, count * k + e, span(b * BANK + lo, w))
 
-        def signal(n, bank):
+        def k1_columns(i, g):
+            return span((GROUPS * i + g if i < UPPER else UPPER * (GROUPS + g) + i - UPPER) * P, P)
+
+        def signal(n, lo, up, bank):
             b, i = divmod(n, ROW_TILES)
-            filled["signal", n] = new_bank(bank, [P, BANK], F32)
+            filled["signal", n, lo] = new_bank(bank, [P, up - lo], F32)
             for g in range(GROUPS):
-                c, m = slice((GROUPS * i + g) * P, (GROUPS * i + g + 1) * P), slice(g * BANK, (g + 1) * BANK)
-                mx(filled["signal", n][:], k1_codes[:, c], k1_scales[:, c], h_codes[b][:, m], h_scales[b][:, m], g == 0, g == GROUPS - 1)
+                mx(filled["signal", n, lo][:], (k1_codes, k1_scales), k1_columns(i, g), (h_codes[b, g], h_scales[b, g]), slice(lo, up), g == 0, g == GROUPS - 1)
+
+        def turned_pass(b, c, g):
+            rows = span(k1_columns(UPPER, g).start, BANK)
+            mx(filled["turned", b, c][:], (h_codes[b, g], h_scales[b, g]), span(c * P, P), (k1_codes, k1_scales), rows, g == 0, g == GROUPS - 1)
+
+        def open_turned(b, c, bank):
+            filled["turned", b, c] = new_bank(bank, [P, BANK], F32)
+            turned_pass(b, c, 0)
+
+        def close_turned(b, c):
+            turned_pass(b, c, 1)
+
+        def lay_data(b, c, bank):
+            filled["strip", b, c] = new_bank(bank, [P, UPPER, P], F32)
+            nc.tensor.matmul(filled["strip", b, c][:], lhsT=ident_bf[:], rhs=data_sb[b, 1][:, :, span(c * P, P)], start=True, stop=False)
+
+        def turn_back(b, c):
+            for a in range(UPPER):
+                nc.tensor.matmul(
+                    filled["strip", b, c][:, a, :], lhsT=negated[b, c][:, span(a * P, P)], rhs=ident[:], is_transpose=True, start=False, stop=a == UPPER - 1
+                )
 
         def spread_wt(blocks, bank):
             both = new_bank(bank, [P, 2, BANK], BF16)
@@ -168,7 +199,7 @@ def tile_nmr_relaxometry_residual_s7_kernel(tc, k1, dist, k2_bytes, k2_scale, po
                 8: lambda: dist_grouped[1][:, 0:2],
                 10: lambda: dist_grouped[1][:, 2:4],
                 12: lambda: k2_grouped[:, 4:6],
-                14: lambda: h_grouped[0][:, 0:CHUNK].rearrange("p (a n) t -> p a n t", a=2),
+                14: lambda: h_grouped[0, 1][:, 0:HALF].rearrange("p (a n) t -> p a n t", a=2),
             }[r]()
 
         def widen(r, count, copy):
@@ -196,17 +227,17 @@ def tile_nmr_relaxometry_residual_s7_kernel(tc, k1, dist, k2_bytes, k2_scale, po
                 op=MULT,
             )
 
-        def group_words(name, grouped):
-            dst = flat(grouped).bitcast(F32).rearrange("p (a n u) -> p a n u", a=2, u=2)
+        def group_words(name, runs):
+            dst = runs.bitcast(F32).rearrange("p a (n u) -> p a n u", u=2)
             nc.scalar.copy(out=dst, in_=filled[name][:].rearrange("p a u n -> p a n u"))
 
         def group_dist(g, h):
             if h == 0:
                 dist_grouped[g] = keep.tile([P, 4, P, 4], BF16, name="dist_grouped%d" % g, align_bytes=64)
-            group_words(("dist", g, h), dist_grouped[g][:, 2 * h : 2 * h + 2])
+            group_words(("dist", g, h), dist_grouped[g][:, 2 * h : 2 * h + 2].rearrange("p a n t -> p a (n t)"))
 
         def group_k1(i):
-            group_words(("k1", i), k1_grouped[:, GROUPS * i : GROUPS * (i + 1)])
+            group_words(("k1", i), k1_upper[:, i] if i < UPPER else k1_lower[:, :, i - UPPER])
 
         def pol_to_f32():
             nc.scalar.activation(out=pol4[:], in_=pol_bf[:], func=COPY)
@@ -215,9 +246,9 @@ def tile_nmr_relaxometry_residual_s7_kernel(tc, k1, dist, k2_bytes, k2_scale, po
             nc.scalar.copy(out=ident_bf[:], in_=ident[:])
 
         def h_columns(b, g, lo, up):
-            if b not in h_grouped:
-                h_grouped[b] = turn.tile([P, GROUPS * BANK, 4], BF16, name="h_grouped", align_bytes=64, bufs=H_BUFS)
-            return h_grouped[b][:, g * BANK + lo : g * BANK + up, :]
+            if (b, g) not in h_grouped:
+                h_grouped[b, g] = turn.tile([P, BANK, 4], BF16, name="h_grouped%d" % g, align_bytes=64, bufs=H_BUFS)
+            return h_grouped[b, g][:, lo:up, :]
 
         def h_quarter(b, g, q):
             nc.vector.tensor_tensor(
@@ -236,15 +267,25 @@ def tile_nmr_relaxometry_residual_s7_kernel(tc, k1, dist, k2_bytes, k2_scale, po
                 dst = planes[b, g, lo][:, t, 0:w]
                 nc.scalar.activation(out=dst, in_=filled["planes", b, g, lo, k][:, e, :], func=COPY, scale=pol4[:, 4 * g + t : 4 * g + t + 1])
 
-        def group_planes(b, g, lo, h):
-            dst = h_columns(b, g, lo + h * CHUNK, lo + (h + 1) * CHUNK).rearrange("p (c i) t -> p c t i", i=4)
-            nc.scalar.copy(out=dst, in_=planes[b, g, lo][:, :, h * CHUNK : (h + 1) * CHUNK].rearrange("p t (c i) -> p c t i", i=4))
+        def group_planes(b, g, lo, h, copy):
+            dst = h_columns(b, g, lo + h * HALF, lo + (h + 1) * HALF).rearrange("p (c i) t -> p c t i", i=4)
+            copy(out=dst, in_=planes[b, g, lo][:, :, span(h * HALF, HALF)].rearrange("p t (c i) -> p c t i", i=4))
+
+        def group_scalar(b, g, lo, h):
+            group_planes(b, g, lo, h, nc.scalar.copy)
+
+        def group_gpsimd(b, g, lo, h):
+            group_planes(b, g, lo, h, nc.gpsimd.tensor_copy)
+
+        def negate(b, c):
+            negated[b, c] = turn.tile([P, BANK], F32, name="negated", bufs=STRIP_BUFS)
+            nc.scalar.activation(out=negated[b, c][:], in_=filled["turned", b, c][:], func=COPY, scale=-1.0)
 
         def quantise(codes, scales, grouped):
             nc.vector.quantize_mx(out=codes.bitcast(FP8X4), scales=scales, in_=grouped)
 
         def q_k2(c, count):
-            m = slice(c * CHUNK, (c + count) * CHUNK)
+            m = span(c * CHUNK, count * CHUNK)
             quantise(k2_codes[:, m], k2_scales[:, m], flat(k2_grouped[:, 2 * c : 2 * (c + count)]))
 
         def q_dist(g):
@@ -253,156 +294,185 @@ def tile_nmr_relaxometry_residual_s7_kernel(tc, k1, dist, k2_bytes, k2_scale, po
             quantise(dist_codes[g][:], dist_scales[g][:], flat(dist_grouped[g][:]))
 
         def q_k1(i, count):
-            c = slice(i * GROUPS * P, (i + count) * GROUPS * P)
-            quantise(k1_codes[:, c], k1_scales[:, c], flat(k1_grouped[:, GROUPS * i : GROUPS * (i + count)]))
+            c = span(i * GROUPS * P, count * GROUPS * P)
+            grouped = k1_upper[:, i : i + count] if i < UPPER else k1_lower[:]
+            quantise(k1_codes[:, c], k1_scales[:, c], grouped.rearrange("p a b x -> p (a b x)"))
 
-        def q_h(b):
-            h_codes[b] = turn.tile([P, GROUPS * BANK], U32, name="h_codes", align_bytes=64, bufs=H_BUFS)
-            h_scales[b] = turn.tile([P, GROUPS * BANK], U8, name="h_scales", align_bytes=64, bufs=H_BUFS)
-            quantise(h_codes[b][:], h_scales[b][:], h_grouped[b][:].rearrange("p n t -> p (n t)"))
+        def q_h(b, g):
+            h_codes[b, g] = turn.tile([P, BANK], U32, name="h_codes%d" % g, align_bytes=64, bufs=H_BUFS)
+            h_scales[b, g] = turn.tile([P, BANK], U8, name="h_scales%d" % g, align_bytes=64, bufs=H_BUFS)
+            quantise(h_codes[b, g][:], h_scales[b, g][:], h_grouped[b, g][:].rearrange("p n t -> p (n t)"))
 
-        def subtract(n, lo=0, up=BANK):
+        def subtract(n, lo, up):
             b, i = divmod(n, ROW_TILES)
-            if lo == 0:
-                result[n] = results.tile([P, BANK], F32, name="result")
-            nc.vector.tensor_tensor(out=result[n][:, lo:up], in0=filled["signal", n][:, lo:up], in1=data_sb[b, i // 4][:, i % 4, lo:up], op=SUB)
+            whole = [s for s in tensor if s[0] is signal and s[1] == n and s[2] <= lo < s[3]][0]
+            result[n, lo] = results.tile([P, BANK], F32, name="result")
+            sums = filled["signal", n, whole[2]][:, lo - whole[2] : up - whole[2]]
+            nc.vector.tensor_tensor(out=result[n, lo][:, 0 : up - lo], in0=sums, in1=data_sb[b, i // UPPER][:, i % UPPER, lo:up], op=SUB)
 
-        def weigh_vector(n, lo=0, up=BANK):
-            nc.vector.tensor_tensor(out=result[n][:, lo:up], in0=result[n][:, lo:up], in1=wt_bank[n // ROW_TILES][:, lo:up], op=MULT)
+        def part_of_result(n, lo, up):
+            first = max(s[2] for s in vector if s[0] is subtract and s[1] == n and s[2] <= lo)
+            result[n, lo] = result[n, first][:, lo - first :]
+            return result[n, lo][:, 0 : up - lo]
 
-        def weigh_gpsimd(n, lo=0, up=BANK):
-            nc.gpsimd.tensor_tensor(out=result[n][:, lo:up], in0=result[n][:, lo:up], in1=wt_sb[n // ROW_TILES][:, lo:up], op=MULT)
+        def weigh_vector(n, lo, up):
+            part = part_of_result(n, lo, up)
+            nc.vector.tensor_tensor(out=part, in0=part, in1=wt_bank[n // ROW_TILES][:, lo:up], op=MULT)
+
+        def weigh_gpsimd(n, lo, up):
+            part = part_of_result(n, lo, up)
+            nc.gpsimd.tensor_tensor(out=part, in0=part, in1=wt_sb[n // ROW_TILES][:, lo:up], op=MULT)
+
+        def weigh_strip(b, c):
+            if b not in lower_result:
+                lower_result[b] = keep.tile([P, UPPER, BANK], F32, name="lower_result%d" % b)
+            m = span(c * P, P)
+            nc.vector.scalar_tensor_tensor(
+                out=lower_result[b][:, :, m],
+                in0=filled["strip", b, c][:],
+                scalar=-1.0,
+                in1=wt_sb[b][:, m].rearrange("p (o m) -> p o m", o=1).to_broadcast([P, UPPER, P]),
+                op0=MULT,
+                op1=MULT,
+            )
 
         def steps(f, *heads, count, first=0):
             return [(f,) + heads + (k,) for k in range(first, first + count)]
 
+        def tiles(f, *numbers):
+            return [(f, n, 0, BANK) for n in numbers]
+
+        def halves(f, n):
+            return [(f, n, 0, HALF), (f, n, HALF, BANK)]
+
         def scale_chunk(c):
             return steps(scale_k2, count=2, first=2 * c)
 
-        def quarters(b, g):
-            return steps(h_quarter, b, g, count=4)
+        def quarters(f, b, g):
+            return steps(f, b, g, count=4)
 
-        def empty_planes(b, g, w=BANK):
-            return steps(h_planes, b, g, 0, w, count=4 * w // BANK)
+        def plane_set(f, b, g, w=BANK):
+            return steps(f, b, g, 0, w, count=4 * w // BANK)
 
-        def fill_planes(b, g, w=BANK):
-            return steps(g_planes, b, g, 0, w, count=4 * w // BANK)
+        def regroup(b, g, w=BANK, f=group_scalar):
+            return steps(f, b, g, 0, count=w // HALF)
 
-        def regroup(b, g, w=BANK):
-            return steps(group_planes, b, g, 0, count=w // CHUNK)
+        def q_block(b):
+            return steps(q_h, b, count=GROUPS)
 
-        def subs(first, last):
-            return steps(subtract, count=last - first + 1, first=first)
+        def weave(first, second):
+            order = [s for pair in zip(first, second) for s in pair]
+            return order + first[len(second) :] + second[len(first) :]
 
-        def weigh(*tiles):
-            return [(weigh_vector, n) for n in tiles]
+        reuse = {7: (q_dist, 0), 8: (q_dist, 1), 10: (q_dist, 1), 12: (q_k2, 2, 2), 14: (q_h, 0, 1)}
+        sub, wv, wg, sig = subtract, weigh_vector, weigh_gpsimd, signal
 
-        def in_turn(first, last):
-            order = subs(first, first)
-            for n in range(first + 1, last, 2):
-                order = order + subs(n, n + 1) + weigh(n)
-            return order
+        def right(f, *numbers):
+            return [(f, n, HALF, BANK) for n in numbers]
 
-        def by_halves(f, n):
-            return [(f, n, 0, CHUNK), (f, n, CHUNK, BANK)]
+        q11 = quarters(h_quarter, 1, 1)
+        vector = [(widen_vector, 0, 1), (widen_vector, 1, 1)] + scale_chunk(0) + scale_chunk(1)
+        vector += [(q_k2, 0, 1), (q_k2, 1, 1), (q_dist, 0)] + scale_chunk(2) + [(q_dist, 1)]
+        vector += scale_chunk(3) + quarters(h_quarter, 0, 1)[:3] + [(q_k2, 2, 2)] + quarters(h_quarter, 0, 1)[3:] + scale_chunk(4)
+        vector += [(q_k1, 0, 2)] + q_block(0) + scale_chunk(5)
+        vector += tiles(sub, 0) + [(q_k1, 2, 2), (q_k2, 4, 2)] + tiles(sub, 1) + q11[:3] + tiles(sub, 2) + [(q_k1, 4, 4)]
+        vector += q11[3:] + tiles(sub, 3) + scale_chunk(6) + tiles(sub, 4) + scale_chunk(7) + tiles(sub, 5) + q_block(1) + [(q_k2, 6, 2)]
+        vector += tiles(sub, 6, 7, 8, 9, 10) + q_block(2)
+        vector += tiles(sub, 11) + tiles(wv, 8) + tiles(sub, 12) + tiles(wv, 9) + tiles(sub, 13, 14) + tiles(wv, 11) + tiles(sub, 15, 16) + tiles(wv, 13)
+        vector += [(weigh_strip, 2, 0)] + tiles(sub, 17) + tiles(wv, 15) + tiles(sub, 18) + [(weigh_strip, 2, 1)] + tiles(sub, 19) + q_block(3)
+        vector += steps(weigh_strip, 2, count=2, first=2) + tiles(sub, 24, 25) + tiles(wv, 24) + tiles(sub, 26) + [(weigh_strip, 3, 0)] + tiles(sub, 27) + tiles(wv, 26) + [(weigh_strip, 3, 1)]
+        vector += right(sub, 28, 29, 30) + right(wv, 29) + right(sub, 31) + right(wv, 30, 31)
 
-        phases = [
-            (
-                [(widen_vector, 0, 1), (widen_vector, 1, 1)] + scale_chunk(0) + scale_chunk(1)
-                + [(q_k2, 0, 1), (q_k2, 1, 1), (q_dist, 0)] + scale_chunk(2) + [(q_dist, 1)],
-                [(widen_scalar, 2, 1), (ident_to_bf16,)] + steps(group_dist, 0, count=2) + [(pol_to_f32,)] + steps(group_dist, 1, count=2),
-            ),
-            (scale_chunk(3) + quarters(0, 1)[:3] + [(q_k2, 2, 2)], empty_planes(0, 0) + regroup(0, 0)[:1]),
-            (quarters(0, 1)[3:] + scale_chunk(4), steps(group_k1, count=2) + regroup(0, 0)[1:]),
-            ([(q_k1, 0, 2), (q_h, 0)] + scale_chunk(5), steps(group_k1, count=2, first=2) + empty_planes(1, 0)[:3]),
-            (
-                subs(0, 0) + [(q_k1, 2, 2)] + quarters(1, 1)[2:] + subs(1, 1) + [(q_k2, 4, 2)],
-                empty_planes(1, 0)[3:] + steps(group_k1, count=2, first=4) + regroup(1, 0)[:1] + empty_planes(1, 1, CHUNK),
-            ),
-            (subs(2, 2) + scale_chunk(6) + scale_chunk(7), regroup(1, 0)[1:] + steps(group_k1, count=2, first=6)),
-            ([(q_k1, 4, 4)], regroup(1, 1, CHUNK) + empty_planes(2, 0)[:1]),
-            ([(q_h, 1), (q_k2, 6, 2)], empty_planes(2, 0)[1:]),
-            (subs(3, 5), empty_planes(2, 1)[:1] + regroup(2, 0)[:1]),
-            (subs(6, 6) + weigh(5) + subs(7, 7), empty_planes(2, 1)[1:]),
-            (subs(8, 9) + weigh(7) + subs(10, 11) + weigh(9), regroup(2, 0)[1:] + regroup(2, 1)),
-            (weigh(11) + subs(12, 12) + [(q_h, 2)], empty_planes(3, 0)),
-            (subs(13, 15), empty_planes(3, 1)[:1] + regroup(3, 0)[:1]),
-            (subs(16, 18), empty_planes(3, 1)[1:]),
-            (
-                weigh(16) + subs(19, 20) + weigh(18) + subs(21, 21) + weigh(20) + subs(22, 23) + [(q_h, 3)],
-                regroup(3, 0)[1:] + regroup(3, 1),
-            ),
-            (
-                weigh(21, 22) + in_turn(24, 31) + by_halves(subtract, 31) + by_halves(weigh_vector, 30)[1:] + by_halves(weigh_vector, 31),
-                [],
-            ),
-        ]
-        spread_after = {empty_planes(2, 0)[1]: (spread_wt, (0, 1)), weigh(11)[0]: (spread_wt, (2,)), weigh(20)[0]: (spread_wt, (2, 3))}
-        behind = {
-            fill_planes(0, 0)[2]: (turn_k2, 6, 2),
-            (turn_k1, 2): (turn_k2, 8, 2),
-            (turn_k1, 5): (signal, 0),
-            fill_planes(1, 1, CHUNK)[0]: (signal, 1),
-            (turn_k1, 6): (turn_k2, 14, 2),
-            (signal, 6): fill_planes(2, 1)[0],
-        }
-        behind.update(zip(fill_planes(3, 1)[1:], steps(signal, count=3, first=16)))
-        borrowing = fill_planes(1, 0)[2:]
-        turns = [(turn_k2, 0, 1), (turn_k2, 1, 1)] + [(turn_k2, r, 2) for r in range(2, 2 * CHUNKS, 2)]
-        reuse = {7: (q_dist, 0), 8: (q_dist, 1), 10: (q_dist, 1), 12: (q_k2, 2, 2), 14: (q_h, 0)}
-        on_vector = [s[1] for v, a in phases for s in v if s[0] is weigh_vector]
+        scalar = [(widen_scalar, 2, 1), (ident_to_bf16,)] + steps(group_dist, 0, count=2) + [(pol_to_f32,)] + steps(group_dist, 1, count=2)
+        scalar += plane_set(h_planes, 0, 0) + regroup(0, 0)[:1] + steps(group_k1, count=2) + regroup(0, 0)[1:]
+        scalar += steps(group_k1, count=2, first=2) + plane_set(h_planes, 1, 0) + steps(group_k1, count=2, first=4) + regroup(1, 0)[:1]
+        scalar += steps(group_k1, count=2, first=6) + regroup(1, 0)[1:]
+        for b in (2, 3):
+            scalar += plane_set(h_planes, b, 0) + plane_set(h_planes, b, 1)[:1] + regroup(b, 0)[:1] + plane_set(h_planes, b, 1)[1:] + regroup(b, 0)[1:] + regroup(b, 1)
+        scalar = scalar[:-3] + weave(steps(negate, 2, count=3), scalar[-3:]) + [(negate, 2, 3)] + steps(negate, 3, count=2)
+
         gpsimd = [(widen_gpsimd, 3, 1), (widen_gpsimd, 4, 2), (widen_gpsimd, 6, 1), (widen_gpsimd, 7, 1)]
         gpsimd += [(widen_gpsimd, r, 2) for r in range(8, 2 * CHUNKS, 2)]
-        gpsimd += [(weigh_gpsimd, n) for n in range(TILES) if n not in on_vector] + by_halves(weigh_gpsimd, 30)[:1]
-        opening = [(warm_up, FIRST_WARM_UPS, 0)] + turns[:2] + [(warm_up, 1, 1), turns[2]] + steps(turn_dist, 0, count=2)
-        opening += [(warm_up, 1, 2), turns[3]] + steps(turn_dist, 1, count=2)
+        gpsimd += tiles(wg, 0, 1, 2, 3, 4, 5, 6, 10, 7, 12, 14, 16, 17, 19, 18, 25, 27) + right(wg, 28)
+
+        tensor = [(warm_up, 3, 0), (turn_k2, 0, 1), (turn_k2, 1, 1), (warm_up, 1, 1), (turn_k2, 2, 2)] + steps(turn_dist, 0, count=2)
+        tensor += [(warm_up, 1, 2), (turn_k2, 4, 2)] + steps(turn_dist, 1, count=2)
+        g01, g11 = quarters(g_quarter, 0, 1), quarters(g_quarter, 1, 1)
+        p00, p10, p20, p21, p30, p31 = [plane_set(g_planes, b, g) for b, g in ((0, 0), (1, 0), (2, 0), (2, 1), (3, 0), (3, 1))]
+        tensor += p00[:2] + [(turn_k2, 6, 2)] + p00[2:] + g01[:3] + steps(turn_k1, count=2)
+        tensor += g01[3:] + [(turn_k2, 8, 2), (turn_k1, 2)] + p10[:1] + [(turn_k1, 3), (turn_k2, 10, 2)] + p10[1:]
+        tensor += tiles(sig, 0) + [(turn_k1, 4), (turn_k1, 5)] + tiles(sig, 1) + g11[:3] + [(turn_k1, 6), (turn_k1, 7)] + tiles(sig, 2) + p20[:1] + g11[3:] + p20[1:2] + tiles(sig, 3)
+        tensor += p20[2:] + [(turn_k2, 12, 2), (turn_k2, 14, 2)] + p21[:1] + tiles(sig, 4) + p21[1:2] + tiles(sig, 5) + p21[2:3] + tiles(sig, 6) + p21[3:] + tiles(sig, 7)
+        tensor += [(spread_wt, (1,))] + tiles(sig, 8, 9) + weave(p30, tiles(sig, 10, 11, 12, 13))
+        turned = [[(open_turned, b, c), (close_turned, b, c)] for b in (2, 3) for c in range(4)]
+        tensor += p31[:2] + tiles(sig, 14) + p31[2:] + tiles(sig, 15, 16) + turned[0] + turned[1] + [(lay_data, 2, 0), (turn_back, 2, 0)] + tiles(sig, 17) + turned[2] + tiles(sig, 18)
+        tensor += [(lay_data, 2, 1), (turn_back, 2, 1)] + tiles(sig, 19) + turned[3] + [(spread_wt, (3,))]
+        tensor += steps(lay_data, 2, count=2, first=2) + [(lay_data, 3, 0), (turn_back, 2, 2), (turn_back, 2, 3), (open_turned, 3, 0), (open_turned, 3, 1)]
+        tensor += tiles(sig, 24) + [(close_turned, 3, 0)] + tiles(sig, 25) + [(close_turned, 3, 1)] + tiles(sig, 26) + [(turn_back, 3, 0)] + tiles(sig, 27) + [(lay_data, 3, 1), (turn_back, 3, 1)] + right(sig, 28, 29, 30, 31)
+        spread_for = {s: [t for t in tensor if t[0] is spread_wt and s[1] // ROW_TILES in t[1]][0] for s in vector if s[0] is weigh_vector}
+        borrowing = p10[:1] + p10[2:3] + steps(lay_data, 3, count=1)
+
         sync = [(load_k2, 0, 1), (load_k2, 1, 1), (load_k2, 2, 2), (load_scale,), (load_dist, 0, 0), (load_k2, 4, 2), (load_dist, 0, 1)]
         sync += [(load_k2, 6, 2), (load_pol,)] + steps(load_dist, 1, count=2) + [(load_k2, 8, 2), (load_k2, 10, 2)]
         sync += steps(load_k1, count=2) + [(load_k2, 12, 2), (load_k2, 14, 2)] + steps(load_k1, count=6, first=2)
         sync += [(load_data, 0, 0), (load_wt, 0), (load_data, 0, 1)]
         for b in range(1, BLOCKS):
             sync += [(load_wt, b)] + steps(load_data, b, count=2)
-        sync += steps(store, count=TILES - 2) + by_halves(store, 30) + by_halves(store, 31)
 
-        maker = {scale_k2: turn_k2, group_dist: turn_dist, group_k1: turn_k1, h_quarter: g_quarter, h_planes: g_planes, subtract: signal}
-        vector, scalar = [s for v, a in phases for s in v], [s for v, a in phases for s in a]
+        sync += tiles(store, 0, 1, 2, 3, 4, 5, 6, 8, 10, 9, 7, 11, 12, 13, 14, 15, 16) + [(store_strips, 2, 0, 2, 0, 4)] + tiles(store, 17, 19) + [(store_strips, 2, 2, 2, 0, 4)]
+        sync += tiles(store, 18, 24, 25, 26) + [(store_strips, 3, 0, 2, 0, 4)] + tiles(store, 27) + right(store, 29, 28, 30, 31)
+
+        vector_banks, scalar_banks, bank_of = list(VECTOR_BANKS), list(SCALAR_BANKS), {}
+        for step in tensor:
+            if step[0] in (warm_up, spread_wt):
+                bank_of[step] = SCALAR_BANKS[-1]
+                if step[0] is spread_wt and bank_of[step] in scalar_banks:
+                    scalar_banks.remove(bank_of[step])
+            elif step[0] not in (turn_back, close_turned):
+                for_vector = step[0] in (turn_k2, g_quarter, signal, lay_data)
+                ring = vector_banks if for_vector != (step in borrowing) else scalar_banks
+                bank_of[step] = ring.pop(0)
+                ring.append(bank_of[step])
+
         every = vector + scalar + gpsimd
+        maker = {group_dist: turn_dist, group_k1: turn_k1, h_quarter: g_quarter, h_planes: g_planes, negate: open_turned, weigh_strip: lay_data}
 
-        def made_by(step):
-            if step[0] is scale_k2:
-                return covering(turns, step[1])[0]
-            return (maker[step[0]],) + (step[1:2] if step[0] is subtract else step[1:])
+        def all_of(among, *functions):
+            return [s for s in among if s[0] in functions]
 
         def covering(among, k):
             return [s for s in among if s[1] <= k < s[1] + s[2]]
 
-        def all_of(f, among):
-            return [s for s in among if s[0] is f]
+        def over(among, n, lo):
+            return [s for s in among if s[1] == n and s[2] <= lo < s[3]]
 
-        widenings = [s for s in every if s[0] in (widen_vector, widen_scalar, widen_gpsimd)]
-        weighings = {s[1:]: s for s in every if s[0] in (weigh_vector, weigh_gpsimd)}
-        plane_sets = [s[1:4] for s in scalar if s[0] is h_planes and s[5] == 0]
+        def made_by(step):
+            f, a = step[0], step[1:]
+            if f is scale_k2:
+                return covering(all_of(tensor, turn_k2), a[0])[0]
+            if f is subtract:
+                return over(all_of(tensor, signal), a[0], a[1])[0]
+            if f is weigh_vector:
+                return spread_for[step]
+            return (maker[f],) + a
 
-        def spread_for(step):
-            asked = [s for s in merged[: merged.index(step)] if s in spread_after]
-            return spread_after[asked[-1]]
-
-        merged = [s for v, a in phases for s in a + v]
         readers = {}
         for step in every:
-            if step[0] in maker:
+            if step[0] in maker or step[0] in (scale_k2, subtract, weigh_vector):
                 readers.setdefault(made_by(step), []).append(step)
-            if step[0] is weigh_vector:
-                readers.setdefault(spread_for(step), []).append(step)
+        widenings = all_of(every, widen_vector, widen_scalar, widen_gpsimd)
+        groupings = all_of(every, group_scalar, group_gpsimd)
+        plane_sets = [s[1:4] for s in all_of(scalar, h_planes) if s[5] == 0]
+        subtractions = all_of(vector, subtract)
+        negations = all_of(scalar, negate)
 
-        def subtractions(a):
-            return [(subtract,) + a] if (subtract,) + a in vector else [(subtract, a[0])]
+        def readers_of_h(b, g):
+            return [s for s in all_of(tensor, signal) if s[1] // ROW_TILES == b] + [s for s in all_of(tensor, open_turned, close_turned) if s[1] == b]
 
         def needs(step):
             f, a = step[0], step[1:]
             if step in widenings:
-                earlier = [reuse[a[0]]] if a[0] in reuse else []
-                return covering(all_of(load_k2, sync), a[0]) + earlier
+                return covering(all_of(sync, load_k2), a[0]) + ([reuse[a[0]]] if a[0] in reuse else [])
             if f is turn_k2:
                 return [s for r in range(a[0], a[0] + a[1]) for s in covering(widenings, r)]
             if f is turn_dist:
@@ -412,26 +482,41 @@ def tile_nmr_relaxometry_residual_s7_kernel(tc, k1, dist, k2_bytes, k2_scale, po
             if f in (g_quarter, g_planes):
                 lo, w = (a[2] * P, P) if f is g_quarter else a[2:4]
                 first, last = (a[0] * BANK + lo) // CHUNK, (a[0] * BANK + lo + w - 1) // CHUNK
-                return covering(all_of(q_k2, vector), first) + covering(all_of(q_k2, vector), last) + [(q_dist, a[1])]
+                return covering(all_of(vector, q_k2), first) + covering(all_of(vector, q_k2), last) + [(q_dist, a[1])]
             if f is signal:
                 b, i = divmod(a[0], ROW_TILES)
-                return [(q_h, b)] + covering(all_of(q_k1, vector), i)
+                return q_block(b) + covering(all_of(vector, q_k1), i)
+            if f is open_turned:
+                return [(q_h, a[0], 0)] + covering(all_of(vector, q_k1), UPPER)
+            if f is close_turned:
+                return [(q_h, a[0], 1), (open_turned,) + a]
+            if f is lay_data:
+                return [(ident_to_bf16,), (load_data, a[0], 1)]
+            if f is turn_back:
+                return [(lay_data,) + a, (negate,) + a]
             if f is spread_wt:
                 return [(ident_to_bf16,)] + [(load_wt, b) for b in a[0]]
             h_free = []
-            if f in (h_quarter, group_planes) and a[0] >= H_BUFS:
-                h_free = [(q_h, a[0] - H_BUFS)] + [covering(turns, r)[0] for r in reuse if reuse[r] == (q_h, a[0] - H_BUFS)]
+            if (f is h_quarter or step in groupings) and a[0] >= H_BUFS:
+                before = (q_h, a[0] - H_BUFS, a[1])
+                h_free = [before] + [covering(all_of(tensor, turn_k2), r)[0] for r in reuse if reuse[r] == before]
             if f is h_quarter:
                 return [made_by(step), (pol_to_f32,)] + h_free
             if f is h_planes:
                 k = plane_sets.index(a[:3]) - PLANE_BUFS
-                earlier = [s for s in scalar if s[0] is group_planes and s[1:4] == plane_sets[k]] if k >= 0 else []
-                return [made_by(step), (pol_to_f32,)] + earlier
-            if f is group_planes:
-                return [s for s in scalar if s[0] is h_planes and s[1:4] == a[:3]] + h_free
+                return [made_by(step), (pol_to_f32,)] + [s for s in groupings if k >= 0 and s[1:4] == plane_sets[k]]
+            if step in groupings:
+                return [s for s in all_of(scalar, h_planes) if s[1:4] == a[:3]] + h_free
             if f is subtract:
                 b, i = divmod(a[0], ROW_TILES)
-                return [made_by(step), (load_data, b, i // 4)] + ([(store, a[0] - RESULT_BUFS)] if a[0] >= RESULT_BUFS else [])
+                k = subtractions.index(step) - RESULT_BUFS
+                earlier = [s for s in all_of(sync, store) if k >= 0 and subtractions[k] in over(subtractions, s[1], s[2])]
+                return [made_by(step), (load_data, b, i // UPPER)] + earlier
+            if f is negate:
+                k = negations.index(step) - STRIP_BUFS
+                return [(close_turned,) + a] + ([(turn_back,) + negations[k][1:]] if k >= 0 else [])
+            if f is weigh_strip:
+                return [(turn_back,) + a, (load_wt, a[0])]
             if f is scale_k2:
                 return [made_by(step), (load_scale,)]
             if f in maker:
@@ -445,81 +530,37 @@ def tile_nmr_relaxometry_residual_s7_kernel(tc, k1, dist, k2_bytes, k2_scale, po
             if f is q_k1:
                 return steps(group_k1, count=a[1], first=a[0])
             if f is q_h:
-                writers = [s for s in every if s[0] in (h_quarter, group_planes) and s[1] == a[0]]
-                return writers + (steps(signal, count=ROW_TILES, first=(a[0] - H_BUFS) * ROW_TILES) if a[0] >= H_BUFS else [])
+                writers = [s for s in groupings + all_of(vector, h_quarter) if s[1:3] == a]
+                return writers + (readers_of_h(a[0] - H_BUFS, a[1]) if a[0] >= H_BUFS else [])
             if f is weigh_vector:
-                return subtractions(a) + [spread_for(step)]
+                return over(subtractions, a[0], a[1]) + [made_by(step)]
             if f is weigh_gpsimd:
-                return subtractions(a) + [(load_wt, a[0] // ROW_TILES)]
+                return over(subtractions, a[0], a[1]) + [(load_wt, a[0] // ROW_TILES)]
             if f is store:
-                return [weighings[a]]
+                return over(all_of(every, weigh_vector, weigh_gpsimd), a[0], a[1])
+            if f is store_strips:
+                return steps(weigh_strip, a[0], count=a[2], first=a[1])
             return []
 
-        vector_banks, scalar_banks, wt_banks = list(VECTOR_BANKS), list(SCALAR_BANKS), [WT_BANK]
-        banks_of = {turn_k2: vector_banks, g_quarter: vector_banks, signal: vector_banks, spread_wt: wt_banks, warm_up: wt_banks}
-        banks_of.update({turn_dist: scalar_banks, turn_k1: scalar_banks, g_planes: scalar_banks})
         written, last_fill = set(), {}
 
-        def banks_for(step):
-            return vector_banks if step in borrowing else banks_of[step[0]]
-
-        def free_banks(step):
-            return [bank for bank in banks_for(step) if all(s in written for s in readers.get(last_fill.get(bank), []))]
-
         def ready(step):
-            ahead = needs(step) + ([behind[step]] if step in behind else [])
-            return all(s in written for s in ahead) and (step[0] not in banks_of or free_banks(step))
+            freed = readers.get(last_fill.get(bank_of.get(step)), [])
+            return all(s in written for s in needs(step) + freed)
 
         def write(step):
-            if step[0] in banks_of:
-                bank = free_banks(step)[0]
-                banks_for(step).remove(bank)
-                banks_for(step).append(bank)
-                last_fill[bank] = step
-                step[0](*step[1:], bank)
+            if step in bank_of:
+                last_fill[bank_of[step]] = step
+                step[0](*step[1:], bank_of[step])
             else:
                 step[0](*step[1:])
             written.add(step)
 
-        def fills(mine):
-            order = []
-            for step in mine:
-                if step[0] in maker and made_by(step) not in order + opening:
-                    order.append(made_by(step))
-            return order
-
-        def banks_worth(step):
-            f = step[0]
-            if f in (q_k2, q_k1):
-                return step[2] / 2
-            return 2 if f in (q_h, group_planes) else 1
-
-        waiting = {"sync": list(sync), "opening": list(opening), "for vector": fills(vector), "for scalar": fills(scalar), "wt": [], "gpsimd": list(gpsimd)}
-
-        def follow():
-            for whose, queue in waiting.items():
-                held = whose in ("for vector", "for scalar") and waiting["opening"]
-                while queue and not held and ready(queue[0]):
-                    write(queue.pop(0))
-
         make_identity(nc, ident[:])
-        for v, a in phases:
-            v, a = list(v), list(a)
-            v_all, a_all = sum(map(banks_worth, v)), sum(map(banks_worth, a))
-            v_done, a_done = SCALAR_LEAD, 0
-            while v or a:
-                follow()
-                if v and ready(v[0]) and (not a or not ready(a[0]) or v_done * a_all <= a_done * v_all):
-                    step = v.pop(0)
-                    v_done = v_done + banks_worth(step)
-                else:
-                    step = a.pop(0) if a else v.pop(0)
-                    assert ready(step)
-                    a_done = a_done + banks_worth(step)
-                write(step)
-                if step in spread_after:
-                    if WT_BANK in scalar_banks:
-                        scalar_banks.remove(WT_BANK)
-                    waiting["wt"].append(spread_after[step])
-        follow()
-        assert not any(waiting.values())
+        waiting = [list(sync), list(tensor), list(vector), list(scalar), list(gpsimd)]
+        while any(waiting):
+            left = sum(map(len, waiting))
+            for queue in waiting:
+                while queue and ready(queue[0]):
+                    write(queue.pop(0))
+            assert sum(map(len, waiting)) < left

@@ -195,11 +195,10 @@ def tile_nmr_relaxometry_residual_s7_kernel(tc, k1, dist, k2_bytes, k2_scale, po
 
         def spent(r):
             return {
-                7: lambda: dist_grouped[0][:, 0:1],
-                8: lambda: dist_grouped[1][:, 0:2],
-                10: lambda: dist_grouped[1][:, 2:4],
-                12: lambda: k2_grouped[:, 4:6],
-                14: lambda: h_grouped[0, 1][:, 0:HALF].rearrange("p (a n) t -> p a n t", a=2),
+                8: lambda: dist_grouped[0][:, 0:2],
+                10: lambda: dist_grouped[1][:, 0:2],
+                12: lambda: dist_grouped[1][:, 2:4],
+                14: lambda: k2_grouped[:, 4:6],
             }[r]()
 
         def widen(r, count, copy):
@@ -364,53 +363,61 @@ def tile_nmr_relaxometry_residual_s7_kernel(tc, k1, dist, k2_bytes, k2_scale, po
             order = [s for pair in zip(first, second) for s in pair]
             return order + first[len(second) :] + second[len(first) :]
 
-        reuse = {7: (q_dist, 0), 8: (q_dist, 1), 10: (q_dist, 1), 12: (q_k2, 2, 2), 14: (q_h, 0, 1)}
         sub, wv, wg, sig = subtract, weigh_vector, weigh_gpsimd, signal
 
         def right(f, *numbers):
             return [(f, n, HALF, BANK) for n in numbers]
 
-        q11 = quarters(h_quarter, 1, 1)
-        vector = [(widen_vector, 0, 1), (widen_vector, 1, 1)] + scale_chunk(0) + scale_chunk(1)
-        vector += [(q_k2, 0, 1), (q_k2, 1, 1), (q_dist, 0)] + scale_chunk(2) + [(q_dist, 1)]
-        vector += scale_chunk(3) + quarters(h_quarter, 0, 1)[:3] + [(q_k2, 2, 2)] + quarters(h_quarter, 0, 1)[3:] + scale_chunk(4)
-        vector += [(q_k1, 0, 2)] + q_block(0) + scale_chunk(5)
-        vector += tiles(sub, 0) + [(q_k1, 2, 2), (q_k2, 4, 2)] + tiles(sub, 1) + q11[:3] + tiles(sub, 2) + [(q_k1, 4, 4)]
-        vector += q11[3:] + tiles(sub, 3) + scale_chunk(6) + tiles(sub, 4) + scale_chunk(7) + tiles(sub, 5) + q_block(1) + [(q_k2, 6, 2)]
-        vector += tiles(sub, 6, 7, 8, 9, 10) + q_block(2)
-        vector += tiles(sub, 11) + tiles(wv, 8) + tiles(sub, 12) + tiles(wv, 9) + tiles(sub, 13, 14) + tiles(wv, 11) + tiles(sub, 15, 16) + tiles(wv, 13)
-        vector += [(weigh_strip, 2, 0)] + tiles(sub, 17) + tiles(wv, 15) + tiles(sub, 18) + [(weigh_strip, 2, 1)] + tiles(sub, 19) + q_block(3)
-        vector += steps(weigh_strip, 2, count=2, first=2) + tiles(sub, 24, 25) + tiles(wv, 24) + tiles(sub, 26) + [(weigh_strip, 3, 0)] + tiles(sub, 27) + tiles(wv, 26) + [(weigh_strip, 3, 1)]
-        vector += right(sub, 28, 29, 30) + right(wv, 29) + right(sub, 31) + right(wv, 30, 31)
+        def scales(*numbers):
+            return [(scale_k2, r) for r in numbers]
 
-        scalar = [(widen_scalar, 2, 1), (ident_to_bf16,)] + steps(group_dist, 0, count=2) + [(pol_to_f32,)] + steps(group_dist, 1, count=2)
-        scalar += plane_set(h_planes, 0, 0) + regroup(0, 0)[:1] + steps(group_k1, count=2) + regroup(0, 0)[1:]
-        scalar += steps(group_k1, count=2, first=2) + plane_set(h_planes, 1, 0) + steps(group_k1, count=2, first=4) + regroup(1, 0)[:1]
-        scalar += steps(group_k1, count=2, first=6) + regroup(1, 0)[1:]
-        for b in (2, 3):
-            scalar += plane_set(h_planes, b, 0) + plane_set(h_planes, b, 1)[:1] + regroup(b, 0)[:1] + plane_set(h_planes, b, 1)[1:] + regroup(b, 0)[1:] + regroup(b, 1)
-        scalar = scalar[:-3] + weave(steps(negate, 2, count=3), scalar[-3:]) + [(negate, 2, 3)] + steps(negate, 3, count=2)
-
-        gpsimd = [(widen_gpsimd, 3, 1), (widen_gpsimd, 4, 2), (widen_gpsimd, 6, 1), (widen_gpsimd, 7, 1)]
-        gpsimd += [(widen_gpsimd, r, 2) for r in range(8, 2 * CHUNKS, 2)]
-        gpsimd += tiles(wg, 0, 1, 2, 3, 4, 5, 6, 10, 7, 12, 14, 16, 17, 19, 18, 25, 27) + right(wg, 28)
-
-        tensor = [(warm_up, 3, 0), (turn_k2, 0, 1), (turn_k2, 1, 1), (warm_up, 1, 1), (turn_k2, 2, 2)] + steps(turn_dist, 0, count=2)
-        tensor += [(warm_up, 1, 2), (turn_k2, 4, 2)] + steps(turn_dist, 1, count=2)
+        q01, q11 = quarters(h_quarter, 0, 1), quarters(h_quarter, 1, 1)
         g01, g11 = quarters(g_quarter, 0, 1), quarters(g_quarter, 1, 1)
         p00, p10, p20, p21, p30, p31 = [plane_set(g_planes, b, g) for b, g in ((0, 0), (1, 0), (2, 0), (2, 1), (3, 0), (3, 1))]
-        tensor += p00[:2] + [(turn_k2, 6, 2)] + p00[2:] + g01[:3] + steps(turn_k1, count=2)
-        tensor += g01[3:] + [(turn_k2, 8, 2), (turn_k1, 2)] + p10[:1] + [(turn_k1, 3), (turn_k2, 10, 2)] + p10[1:]
-        tensor += tiles(sig, 0) + [(turn_k1, 4), (turn_k1, 5)] + tiles(sig, 1) + g11[:3] + [(turn_k1, 6), (turn_k1, 7)] + tiles(sig, 2) + p20[:1] + g11[3:] + p20[1:2] + tiles(sig, 3)
-        tensor += p20[2:] + [(turn_k2, 12, 2), (turn_k2, 14, 2)] + p21[:1] + tiles(sig, 4) + p21[1:2] + tiles(sig, 5) + p21[2:3] + tiles(sig, 6) + p21[3:] + tiles(sig, 7)
-        tensor += [(spread_wt, (1,))] + tiles(sig, 8, 9) + weave(p30, tiles(sig, 10, 11, 12, 13))
+        e00, e10, e20, e21, e30, e31 = [plane_set(h_planes, b, g) for b, g in ((0, 0), (1, 0), (2, 0), (2, 1), (3, 0), (3, 1))]
         turned = [[(open_turned, b, c), (close_turned, b, c)] for b in (2, 3) for c in range(4)]
-        tensor += p31[:2] + tiles(sig, 14) + p31[2:] + tiles(sig, 15, 16) + turned[0] + turned[1] + [(lay_data, 2, 0), (turn_back, 2, 0)] + tiles(sig, 17) + turned[2] + tiles(sig, 18)
-        tensor += [(lay_data, 2, 1), (turn_back, 2, 1)] + tiles(sig, 19) + turned[3] + [(spread_wt, (3,))]
-        tensor += steps(lay_data, 2, count=2, first=2) + [(lay_data, 3, 0), (turn_back, 2, 2), (turn_back, 2, 3), (open_turned, 3, 0), (open_turned, 3, 1)]
-        tensor += tiles(sig, 24) + [(close_turned, 3, 0)] + tiles(sig, 25) + [(close_turned, 3, 1)] + tiles(sig, 26) + [(turn_back, 3, 0)] + tiles(sig, 27) + [(lay_data, 3, 1), (turn_back, 3, 1)] + right(sig, 28, 29, 30, 31)
+
+        reuse = {8: (q_dist, 0), 10: (q_dist, 1), 12: (q_dist, 1), 14: (q_k2, 2, 2)}
+        vector = [(widen_vector, 0, 1), (widen_vector, 1, 1)] + scales(0, 1, 2, 3)
+        vector += [(q_k2, 0, 1), (q_k2, 1, 1), (q_dist, 0)] + scales(4, 5, 6) + [(q_dist, 1)] + scales(7, 8, 9)
+        vector += q01[:3] + [(q_k2, 2, 2)] + q01[3:] + scales(10, 11) + [(q_k1, 0, 2)] + q_block(0) + [(q_k1, 2, 2), (q_k2, 4, 2)]
+        vector += tiles(sub, 0) + q11[:1] + tiles(sub, 1) + q11[1:] + tiles(sub, 2) + [(q_k1, 4, 4)] + q_block(1)
+
+        f2, f3 = steps(weigh_strip, 2, count=4), steps(weigh_strip, 3, count=2)
+        vector += tiles(sub, 3) + scales(12, 13) + tiles(sub, 4) + scales(14, 15) + tiles(sub, 5, 6) + [(q_k2, 6, 2)]
+        vector += tiles(sub, 7, 8, 9) + tiles(wv, 8) + tiles(sub, 10) + q_block(2)
+        vector += tiles(sub, 11) + tiles(wv, 9) + tiles(sub, 12, 13) + tiles(wv, 11) + tiles(sub, 14, 15) + tiles(wv, 13) + tiles(sub, 16, 17)
+        vector += tiles(wv, 15) + tiles(sub, 18) + f2[:2] + tiles(sub, 19) + q_block(3)
+        vector += f2[2:] + tiles(sub, 24, 25, 26) + tiles(wv, 24) + tiles(sub, 27) + tiles(wv, 26) + f3[:1] + right(sub, 28, 29) + f3[1:]
+        vector += right(sub, 30, 31) + right(wv, 29, 31)
+
+        scalar = [(widen_scalar, 2, 1), (ident_to_bf16,)] + steps(group_dist, 0, count=2) + [(pol_to_f32,), (widen_scalar, 7, 1)] + steps(group_dist, 1, count=2)
+        scalar += e00 + [(group_k1, 0)] + regroup(0, 0) + steps(group_k1, count=3, first=1)
+        scalar += e10 + steps(group_k1, count=2, first=4) + regroup(1, 0)[:1] + steps(group_k1, count=2, first=6) + regroup(1, 0)[1:]
+
+        n2, n3 = steps(negate, 2, count=4), steps(negate, 3, count=2)
+        scalar += e20 + e21[:1] + regroup(2, 0)[:1] + e21[1:] + regroup(2, 0)[1:] + regroup(2, 1)
+        scalar += e30 + e31[:1] + regroup(3, 0)[:1] + e31[1:] + regroup(3, 0)[1:] + n2[:2] + regroup(3, 1) + n2[2:] + n3
+
+        gpsimd = [(widen_gpsimd, 3, 1), (widen_gpsimd, 4, 2), (widen_gpsimd, 6, 1)]
+        gpsimd += [(widen_gpsimd, r, 2) for r in range(8, 2 * CHUNKS, 2)]
+
+        gpsimd += tiles(wg, 0, 1, 2, 3, 4, 6, 5, 10, 7, 12, 14, 16, 17, 19, 18, 25, 27) + right(wg, 28, 30)
+
+        tensor = [(warm_up, 3, 0), (turn_k2, 0, 1), (turn_k2, 1, 1), (warm_up, 1, 1), (turn_k2, 2, 2)] + steps(turn_dist, 0, count=2)
+        tensor += [(warm_up, 1, 2), (turn_k2, 4, 2)] + steps(turn_dist, 1, count=2) + [(turn_k2, 6, 2)]
+        tensor += p00 + [(turn_k2, 8, 2), (turn_k1, 0)] + g01 + [(turn_k1, 1), (turn_k2, 10, 2), (turn_k1, 2), (turn_k1, 3)] + p10[:2] + g11[:1] + p10[2:] + g11[1:2]
+        tensor += [(turn_k1, 4), (turn_k1, 5)] + tiles(sig, 0, 1) + [(turn_k1, 6), (turn_k1, 7)] + g11[2:]
+
+        lay2, back2, lay3, back3 = steps(lay_data, 2, count=4), steps(turn_back, 2, count=4), steps(lay_data, 3, count=2), steps(turn_back, 3, count=2)
+        tensor += p20[:1] + tiles(sig, 2) + p20[1:3] + tiles(sig, 3) + p20[3:] + [(turn_k2, 12, 2), (turn_k2, 14, 2)] + p21[:1] + tiles(sig, 4) + p21[1:] + tiles(sig, 5, 6, 7)
+        tensor += [(spread_wt, (1, 3))] + tiles(sig, 8, 9) + p30[:1] + tiles(sig, 10) + p30[1:3] + tiles(sig, 11) + p30[3:] + tiles(sig, 12) + p31[:1] + tiles(sig, 13, 14)
+        tensor += p31[1:3] + tiles(sig, 15) + p31[3:] + tiles(sig, 16, 17) + turned[0] + turned[1] + tiles(sig, 18) + lay2[:2] + back2[:2]
+        tensor += tiles(sig, 19) + turned[2] + turned[3] + lay2[2:] + lay3[:1] + back2[2:]
+        tensor += tiles(sig, 24, 25, 26) + turned[4] + tiles(sig, 27) + turned[5] + lay3[1:] + back3[:1] + right(sig, 28, 29) + back3[1:] + right(sig, 30, 31)
+        borrowing = lay3[:1]
+
         spread_for = {s: [t for t in tensor if t[0] is spread_wt and s[1] // ROW_TILES in t[1]][0] for s in vector if s[0] is weigh_vector}
-        borrowing = p10[:1] + p10[2:3] + steps(lay_data, 3, count=1)
 
         sync = [(load_k2, 0, 1), (load_k2, 1, 1), (load_k2, 2, 2), (load_scale,), (load_dist, 0, 0), (load_k2, 4, 2), (load_dist, 0, 1)]
         sync += [(load_k2, 6, 2), (load_pol,)] + steps(load_dist, 1, count=2) + [(load_k2, 8, 2), (load_k2, 10, 2)]
@@ -419,20 +426,8 @@ def tile_nmr_relaxometry_residual_s7_kernel(tc, k1, dist, k2_bytes, k2_scale, po
         for b in range(1, BLOCKS):
             sync += [(load_wt, b)] + steps(load_data, b, count=2)
 
-        sync += tiles(store, 0, 1, 2, 3, 4, 5, 6, 8, 10, 9, 7, 11, 12, 13, 14, 15, 16) + [(store_strips, 2, 0, 2, 0, 4)] + tiles(store, 17, 19) + [(store_strips, 2, 2, 2, 0, 4)]
-        sync += tiles(store, 18, 24, 25, 26) + [(store_strips, 3, 0, 2, 0, 4)] + tiles(store, 27) + right(store, 29, 28, 30, 31)
-
-        vector_banks, scalar_banks, bank_of = list(VECTOR_BANKS), list(SCALAR_BANKS), {}
-        for step in tensor:
-            if step[0] in (warm_up, spread_wt):
-                bank_of[step] = SCALAR_BANKS[-1]
-                if step[0] is spread_wt and bank_of[step] in scalar_banks:
-                    scalar_banks.remove(bank_of[step])
-            elif step[0] not in (turn_back, close_turned):
-                for_vector = step[0] in (turn_k2, g_quarter, signal, lay_data)
-                ring = vector_banks if for_vector != (step in borrowing) else scalar_banks
-                bank_of[step] = ring.pop(0)
-                ring.append(bank_of[step])
+        sync += tiles(store, 0, 1, 2, 3, 4, 6, 8, 5, 9, 10, 7, 11, 12, 13, 14, 15, 16) + [(store_strips, 2, 0, 2, 0, 4)] + tiles(store, 17) + [(store_strips, 2, 2, 2, 0, 4)]
+        sync += tiles(store, 19, 18, 24, 25, 26, 27) + [(store_strips, 3, 0, 2, 0, 4)] + right(store, 28, 29, 31, 30)
 
         every = vector + scalar + gpsimd
         maker = {group_dist: turn_dist, group_k1: turn_k1, h_quarter: g_quarter, h_planes: g_planes, negate: open_turned, weigh_strip: lay_data}
@@ -541,6 +536,22 @@ def tile_nmr_relaxometry_residual_s7_kernel(tc, k1, dist, k2_bytes, k2_scale, po
             if f is store_strips:
                 return steps(weigh_strip, a[0], count=a[2], first=a[1])
             return []
+
+        vector_banks, scalar_banks, bank_of, held_by = list(VECTOR_BANKS), list(SCALAR_BANKS), {}, {}
+
+        def emptied(bank):
+            mine = vector if bank in VECTOR_BANKS else scalar
+            return max([-1] + [mine.index(s) if s in mine else len(mine) for s in readers.get(held_by.get(bank), [])])
+
+        for step in tensor:
+            if step[0] in (warm_up, spread_wt):
+                bank_of[step] = SCALAR_BANKS[-1]
+                if step[0] is spread_wt and bank_of[step] in scalar_banks:
+                    scalar_banks.remove(bank_of[step])
+            elif step[0] not in (turn_back, close_turned):
+                for_vector = step[0] in (turn_k2, g_quarter, signal, lay_data)
+                bank_of[step] = min(vector_banks if for_vector != (step in borrowing) else scalar_banks, key=emptied)
+                held_by[bank_of[step]] = step
 
         written, last_fill = set(), {}
 

@@ -156,11 +156,11 @@ def tile_nmr_relaxometry_residual_s7_kernel(tc, k1, dist, k2_bytes, k2_scale, po
             b, i = divmod(n, ROW_TILES)
             filled["signal", n, lo] = new_bank(bank, [P, up - lo], F32)
             for g in range(GROUPS):
-                mx(filled["signal", n, lo][:], (k1_codes, k1_scales), k1_columns(i, g), (h_codes[b, g], h_scales[b, g]), slice(lo, up), g == 0, g == GROUPS - 1)
+                mx(filled["signal", n, lo][:], (k1_codes, k1_scales), k1_columns(i, g), (h_codes[b], h_scales[b]), span(g * BANK + lo, up - lo), g == 0, g == GROUPS - 1)
 
         def turned_pass(b, c, g):
             rows = span(k1_columns(UPPER, g).start, BANK)
-            mx(filled["turned", b, c][:], (h_codes[b, g], h_scales[b, g]), span(c * P, P), (k1_codes, k1_scales), rows, g == 0, g == GROUPS - 1)
+            mx(filled["turned", b, c][:], (h_codes[b], h_scales[b]), span(g * BANK + c * P, P), (k1_codes, k1_scales), rows, g == 0, g == GROUPS - 1)
 
         def open_turned(b, c, bank):
             filled["turned", b, c] = new_bank(bank, [P, BANK], F32)
@@ -245,9 +245,9 @@ def tile_nmr_relaxometry_residual_s7_kernel(tc, k1, dist, k2_bytes, k2_scale, po
             nc.scalar.copy(out=ident_bf[:], in_=ident[:])
 
         def h_columns(b, g, lo, up):
-            if (b, g) not in h_grouped:
-                h_grouped[b, g] = turn.tile([P, BANK, 4], BF16, name="h_grouped%d" % g, align_bytes=64, bufs=H_BUFS)
-            return h_grouped[b, g][:, lo:up, :]
+            if b not in h_grouped:
+                h_grouped[b] = turn.tile([P, GROUPS * BANK, 4], BF16, name="h_grouped", align_bytes=64, bufs=H_BUFS)
+            return h_grouped[b][:, g * BANK + lo : g * BANK + up, :]
 
         def h_quarter(b, g, q):
             nc.vector.tensor_tensor(
@@ -297,10 +297,10 @@ def tile_nmr_relaxometry_residual_s7_kernel(tc, k1, dist, k2_bytes, k2_scale, po
             grouped = k1_upper[:, i : i + count] if i < UPPER else k1_lower[:]
             quantise(k1_codes[:, c], k1_scales[:, c], grouped.rearrange("p a b x -> p (a b x)"))
 
-        def q_h(b, g):
-            h_codes[b, g] = turn.tile([P, BANK], U32, name="h_codes%d" % g, align_bytes=64, bufs=H_BUFS)
-            h_scales[b, g] = turn.tile([P, BANK], U8, name="h_scales%d" % g, align_bytes=64, bufs=H_BUFS)
-            quantise(h_codes[b, g][:], h_scales[b, g][:], h_grouped[b, g][:].rearrange("p n t -> p (n t)"))
+        def q_h(b):
+            h_codes[b] = turn.tile([P, GROUPS * BANK], U32, name="h_codes", align_bytes=64, bufs=H_BUFS)
+            h_scales[b] = turn.tile([P, GROUPS * BANK], U8, name="h_scales", align_bytes=64, bufs=H_BUFS)
+            quantise(h_codes[b][:], h_scales[b][:], h_grouped[b][:].rearrange("p n t -> p (n t)"))
 
         def subtract(n, lo, up):
             b, i = divmod(n, ROW_TILES)
@@ -357,7 +357,7 @@ def tile_nmr_relaxometry_residual_s7_kernel(tc, k1, dist, k2_bytes, k2_scale, po
             return steps(f, b, g, 0, count=w // HALF)
 
         def q_block(b):
-            return steps(q_h, b, count=GROUPS)
+            return [(q_h, b)]
 
         def weave(first, second):
             order = [s for pair in zip(first, second) for s in pair]
@@ -381,10 +381,10 @@ def tile_nmr_relaxometry_residual_s7_kernel(tc, k1, dist, k2_bytes, k2_scale, po
         vector = [(widen_vector, 0, 1), (widen_vector, 1, 1)] + scales(0, 1, 2, 3)
         vector += [(q_k2, 0, 1), (q_k2, 1, 1), (q_dist, 0)] + scales(4, 5, 6) + [(q_dist, 1)] + scales(7, 8, 9)
         vector += q01[:3] + [(q_k2, 2, 2)] + q01[3:] + scales(10, 11) + [(q_k1, 0, 2)] + q_block(0) + [(q_k1, 2, 2), (q_k2, 4, 2)]
-        vector += tiles(sub, 0) + q11[:1] + tiles(sub, 1) + q11[1:] + tiles(sub, 2) + [(q_k1, 4, 4)] + q_block(1)
+        vector += tiles(sub, 0) + q11[:1] + tiles(sub, 1) + q11[1:] + tiles(sub, 2) + [(q_k1, 4, 4)]
 
         f2, f3 = steps(weigh_strip, 2, count=4), steps(weigh_strip, 3, count=2)
-        vector += tiles(sub, 3) + scales(12, 13) + tiles(sub, 4) + scales(14, 15) + tiles(sub, 5, 6) + [(q_k2, 6, 2)]
+        vector += scales(12, 13) + tiles(sub, 3) + q_block(1) + tiles(sub, 4) + scales(14, 15) + tiles(sub, 5, 6) + [(q_k2, 6, 2)]
         vector += tiles(sub, 7, 8, 9) + tiles(wv, 8) + tiles(sub, 10) + q_block(2)
         vector += tiles(sub, 11) + tiles(wv, 9) + tiles(sub, 12, 13) + tiles(wv, 11) + tiles(sub, 14, 15) + tiles(wv, 13) + tiles(sub, 16, 17)
         vector += tiles(wv, 15) + tiles(sub, 18) + f2[:2] + tiles(sub, 19) + q_block(3)
@@ -410,7 +410,7 @@ def tile_nmr_relaxometry_residual_s7_kernel(tc, k1, dist, k2_bytes, k2_scale, po
         tensor += [(turn_k1, 4), (turn_k1, 5)] + tiles(sig, 0, 1) + [(turn_k1, 6), (turn_k1, 7)] + g11[2:]
 
         lay2, back2, lay3, back3 = steps(lay_data, 2, count=4), steps(turn_back, 2, count=4), steps(lay_data, 3, count=2), steps(turn_back, 3, count=2)
-        tensor += p20[:1] + tiles(sig, 2) + p20[1:3] + tiles(sig, 3) + p20[3:] + [(turn_k2, 12, 2), (turn_k2, 14, 2)] + p21[:1] + tiles(sig, 4) + p21[1:] + tiles(sig, 5, 6, 7)
+        tensor += p20[:1] + tiles(sig, 2) + p20[1:3] + [(turn_k2, 12, 2)] + p20[3:] + tiles(sig, 3) + p21[:1] + [(turn_k2, 14, 2)] + tiles(sig, 4) + p21[1:] + tiles(sig, 5, 6, 7)
         tensor += [(spread_wt, (1, 3))] + tiles(sig, 8, 9) + p30[:1] + tiles(sig, 10) + p30[1:3] + tiles(sig, 11) + p30[3:] + tiles(sig, 12) + p31[:1] + tiles(sig, 13, 14)
         tensor += p31[1:3] + tiles(sig, 15) + p31[3:] + tiles(sig, 16, 17) + turned[0] + turned[1] + tiles(sig, 18) + lay2[:2] + back2[:2]
         tensor += tiles(sig, 19) + turned[2] + turned[3] + lay2[2:] + lay3[:1] + back2[2:]
@@ -461,7 +461,7 @@ def tile_nmr_relaxometry_residual_s7_kernel(tc, k1, dist, k2_bytes, k2_scale, po
         subtractions = all_of(vector, subtract)
         negations = all_of(scalar, negate)
 
-        def readers_of_h(b, g):
+        def readers_of_h(b):
             return [s for s in all_of(tensor, signal) if s[1] // ROW_TILES == b] + [s for s in all_of(tensor, open_turned, close_turned) if s[1] == b]
 
         def needs(step):
@@ -482,9 +482,9 @@ def tile_nmr_relaxometry_residual_s7_kernel(tc, k1, dist, k2_bytes, k2_scale, po
                 b, i = divmod(a[0], ROW_TILES)
                 return q_block(b) + covering(all_of(vector, q_k1), i)
             if f is open_turned:
-                return [(q_h, a[0], 0)] + covering(all_of(vector, q_k1), UPPER)
+                return [(q_h, a[0])] + covering(all_of(vector, q_k1), UPPER)
             if f is close_turned:
-                return [(q_h, a[0], 1), (open_turned,) + a]
+                return [(open_turned,) + a]
             if f is lay_data:
                 return [(ident_to_bf16,), (load_data, a[0], 1)]
             if f is turn_back:
@@ -493,7 +493,7 @@ def tile_nmr_relaxometry_residual_s7_kernel(tc, k1, dist, k2_bytes, k2_scale, po
                 return [(ident_to_bf16,)] + [(load_wt, b) for b in a[0]]
             h_free = []
             if (f is h_quarter or step in groupings) and a[0] >= H_BUFS:
-                before = (q_h, a[0] - H_BUFS, a[1])
+                before = (q_h, a[0] - H_BUFS)
                 h_free = [before] + [covering(all_of(tensor, turn_k2), r)[0] for r in reuse if reuse[r] == before]
             if f is h_quarter:
                 return [made_by(step), (pol_to_f32,)] + h_free
@@ -525,8 +525,8 @@ def tile_nmr_relaxometry_residual_s7_kernel(tc, k1, dist, k2_bytes, k2_scale, po
             if f is q_k1:
                 return steps(group_k1, count=a[1], first=a[0])
             if f is q_h:
-                writers = [s for s in groupings + all_of(vector, h_quarter) if s[1:3] == a]
-                return writers + (readers_of_h(a[0] - H_BUFS, a[1]) if a[0] >= H_BUFS else [])
+                writers = [s for s in groupings + all_of(vector, h_quarter) if s[1] == a[0]]
+                return writers + (readers_of_h(a[0] - H_BUFS) if a[0] >= H_BUFS else [])
             if f is weigh_vector:
                 return over(subtractions, a[0], a[1]) + [made_by(step)]
             if f is weigh_gpsimd:

@@ -383,13 +383,13 @@ def tile_nmr_relaxometry_residual_s7_kernel(tc, k1, dist, k2_bytes, k2_scale, po
         vector += q01[:3] + [(q_k2, 2, 2)] + q01[3:] + scales(10, 11) + [(q_k1, 0, 2)] + q_block(0) + [(q_k1, 2, 2), (q_k2, 4, 2)]
         vector += tiles(sub, 0) + q11[:1] + tiles(sub, 1) + q11[1:] + tiles(sub, 2) + [(q_k1, 4, 4)]
 
-        f2, f3 = steps(weigh_strip, 2, count=4), steps(weigh_strip, 3, count=2)
+        f2 = steps(weigh_strip, 2, count=4)
         vector += scales(12, 13) + tiles(sub, 3) + q_block(1) + tiles(sub, 4) + scales(14, 15) + tiles(sub, 5, 6) + [(q_k2, 6, 2)]
         vector += tiles(sub, 7, 8, 9) + tiles(wv, 8) + tiles(sub, 10) + q_block(2)
         vector += tiles(sub, 11) + tiles(wv, 9) + tiles(sub, 12, 13) + tiles(wv, 11) + tiles(sub, 14, 15) + tiles(wv, 13) + tiles(sub, 16, 17)
         vector += tiles(wv, 15) + tiles(sub, 18) + f2[:2] + tiles(sub, 19) + q_block(3)
-        vector += f2[2:] + tiles(sub, 24, 25, 26) + tiles(wv, 24) + tiles(sub, 27) + tiles(wv, 26) + f3[:1] + right(sub, 28, 29) + f3[1:]
-        vector += right(sub, 30, 31) + right(wv, 29, 31)
+        vector += f2[2:] + tiles(sub, 24, 25, 26) + tiles(wv, 24) + tiles(sub, 27) + tiles(wv, 26) + tiles(sub, 28, 29) + tiles(wv, 28) + tiles(sub, 30)
+        vector += halves(sub, 31) + halves(wv, 30)[1:] + halves(wv, 31)
 
         scalar = [(widen_scalar, 2, 1), (ident_to_bf16,)] + steps(group_dist, 0, count=2) + [(pol_to_f32,), (widen_scalar, 7, 1)] + steps(group_dist, 1, count=2)
         scalar += e00 + [(group_k1, 0)] + regroup(0, 0) + steps(group_k1, count=3, first=1)
@@ -397,25 +397,25 @@ def tile_nmr_relaxometry_residual_s7_kernel(tc, k1, dist, k2_bytes, k2_scale, po
 
         n2, n3 = steps(negate, 2, count=4), steps(negate, 3, count=2)
         scalar += e20 + e21[:1] + regroup(2, 0)[:1] + e21[1:] + regroup(2, 0)[1:] + regroup(2, 1)
-        scalar += e30 + e31[:1] + regroup(3, 0)[:1] + e31[1:] + regroup(3, 0)[1:] + n2[:2] + regroup(3, 1) + n2[2:] + n3
+        scalar += e30 + e31[:1] + regroup(3, 0)[:1] + e31[1:] + regroup(3, 0)[1:] + n2[:2] + regroup(3, 1) + n2[2:]
 
         gpsimd = [(widen_gpsimd, 3, 1), (widen_gpsimd, 4, 2), (widen_gpsimd, 6, 1)]
         gpsimd += [(widen_gpsimd, r, 2) for r in range(8, 2 * CHUNKS, 2)]
 
-        gpsimd += tiles(wg, 0, 1, 2, 3, 4, 6, 5, 10, 7, 12, 14, 16, 17, 19, 18, 25, 27) + right(wg, 28, 30)
+        gpsimd += tiles(wg, 0, 1, 2, 3, 4, 6, 5, 10, 7, 12, 14, 16, 17, 19, 18, 25, 27, 29) + halves(wg, 30)[:1]
 
         tensor = [(warm_up, 3, 0), (turn_k2, 0, 1), (turn_k2, 1, 1), (warm_up, 1, 1), (turn_k2, 2, 2)] + steps(turn_dist, 0, count=2)
         tensor += [(warm_up, 1, 2), (turn_k2, 4, 2)] + steps(turn_dist, 1, count=2) + [(turn_k2, 6, 2)]
-        tensor += p00 + [(turn_k2, 8, 2), (turn_k1, 0)] + g01 + [(turn_k1, 1), (turn_k2, 10, 2), (turn_k1, 2), (turn_k1, 3)] + p10[:2] + g11[:1] + p10[2:] + g11[1:2]
+        tensor += p00 + [(turn_k2, 8, 2), (turn_k1, 0)] + g01[:3] + [(turn_k1, 1), (turn_k2, 10, 2)] + g01[3:] + [(turn_k1, 2), (turn_k1, 3)] + p10[:2] + g11[:1] + p10[2:] + g11[1:2]
         tensor += [(turn_k1, 4), (turn_k1, 5)] + tiles(sig, 0, 1) + [(turn_k1, 6), (turn_k1, 7)] + g11[2:]
 
         lay2, back2, lay3, back3 = steps(lay_data, 2, count=4), steps(turn_back, 2, count=4), steps(lay_data, 3, count=2), steps(turn_back, 3, count=2)
         tensor += p20[:1] + tiles(sig, 2) + p20[1:3] + [(turn_k2, 12, 2)] + p20[3:] + tiles(sig, 3) + p21[:1] + [(turn_k2, 14, 2)] + tiles(sig, 4) + p21[1:] + tiles(sig, 5, 6, 7)
         tensor += [(spread_wt, (1, 3))] + tiles(sig, 8, 9) + p30[:1] + tiles(sig, 10) + p30[1:3] + tiles(sig, 11) + p30[3:] + tiles(sig, 12) + p31[:1] + tiles(sig, 13, 14)
         tensor += p31[1:3] + tiles(sig, 15) + p31[3:] + tiles(sig, 16, 17) + turned[0] + turned[1] + tiles(sig, 18) + lay2[:2] + back2[:2]
-        tensor += tiles(sig, 19) + turned[2] + turned[3] + lay2[2:] + lay3[:1] + back2[2:]
-        tensor += tiles(sig, 24, 25, 26) + turned[4] + tiles(sig, 27) + turned[5] + lay3[1:] + back3[:1] + right(sig, 28, 29) + back3[1:] + right(sig, 30, 31)
-        borrowing = lay3[:1]
+        tensor += tiles(sig, 19) + turned[2] + turned[3] + lay2[2:] + back2[2:]
+        tensor += tiles(sig, 24, 25, 26, 27, 28, 29, 30, 31)
+        borrowing = []
 
         spread_for = {s: [t for t in tensor if t[0] is spread_wt and s[1] // ROW_TILES in t[1]][0] for s in vector if s[0] is weigh_vector}
 
@@ -427,7 +427,7 @@ def tile_nmr_relaxometry_residual_s7_kernel(tc, k1, dist, k2_bytes, k2_scale, po
             sync += [(load_wt, b)] + steps(load_data, b, count=2)
 
         sync += tiles(store, 0, 1, 2, 3, 4, 6, 8, 5, 9, 10, 7, 11, 12, 13, 14, 15, 16) + [(store_strips, 2, 0, 2, 0, 4)] + tiles(store, 17) + [(store_strips, 2, 2, 2, 0, 4)]
-        sync += tiles(store, 19, 18, 24, 25, 26, 27) + [(store_strips, 3, 0, 2, 0, 4)] + right(store, 28, 29, 31, 30)
+        sync += tiles(store, 19, 18, 24, 25, 26, 27, 28, 29) + halves(store, 30)[::-1] + halves(store, 31)
 
         every = vector + scalar + gpsimd
         maker = {group_dist: turn_dist, group_k1: turn_k1, h_quarter: g_quarter, h_planes: g_planes, negate: open_turned, weigh_strip: lay_data}

from contextlib import ExitStack

import concourse.mybir as mybir
from concourse.masks import make_identity

N1, N2, J1, J2 = 1024, 2048, 1024, 512
FLOPS = 2 * J1 * N2 * J2 + 2 * N1 * N2 * J1

F32 = mybir.dt.float32
BF16 = mybir.dt.bfloat16
U32 = mybir.dt.uint32
U8 = mybir.dt.uint8
FP8 = mybir.dt.float8_e4m3fn
FP8X4 = mybir.dt.float8_e4m3fn_x4
MULT = mybir.AluOpType.mult
SUB = mybir.AluOpType.subtract
COPY = mybir.ActivationFunctionType.Copy

P = 128
BANK = 512
HALF = BANK // 2
CHUNK = 256
CHUNKS = N2 // CHUNK
BLOCKS = N2 // BANK
ROW_TILES = N1 // P
UPPER = ROW_TILES // 2
GROUPS = J1 // 512
RESULT_BUFS = 12
PLANE_BUFS = 3
H_BUFS = 2
STRIP_BUFS = 4
VECTOR_BANKS = (0, 1, 2, 3)
SCALAR_BANKS = (4, 5, 6, 7)


def tile_nmr_relaxometry_residual_s7_kernel(tc, k1, dist, k2_bytes, k2_scale, pol, data, wt, out):
    nc = tc.nc
    with ExitStack() as ctx:
        keep = ctx.enter_context(tc.tile_pool(name="keep", bufs=1))
        turn = ctx.enter_context(tc.tile_pool(name="turn", bufs=2))
        results = ctx.enter_context(tc.tile_pool(name="results", bufs=RESULT_BUFS))
        psum = ctx.enter_context(tc.psum_pool(name="psum", bufs=1))
        ctx.enter_context(tc.manual_schedule())

        ident = keep.tile([P, P], F32, name="ident")
        ident_bf = keep.tile([P, P], BF16, name="ident_bf")
        scale4 = keep.tile([P, 4], F32, name="scale4")
        pol_bf = keep.tile([P, 4 * GROUPS], BF16, name="pol_bf")
        pol4 = keep.tile([P, 4 * GROUPS], F32, name="pol4")
        k2_grouped = keep.tile([P, 2 * CHUNKS, P, 4], BF16, name="k2_grouped", align_bytes=64)
        k2_codes = keep.tile([P, N2], U32, name="k2_codes", align_bytes=64)
        k2_scales = keep.tile([P, N2], U8, name="k2_scales", align_bytes=64)
        k1_upper = keep.tile([P, UPPER, GROUPS, 4 * P], BF16, name="k1_upper", align_bytes=64)
        k1_lower = keep.tile([P, GROUPS, UPPER, 4 * P], BF16, name="k1_lower", align_bytes=64)
        k1_codes = keep.tile([P, GROUPS * N1], U32, name="k1_codes", align_bytes=64)
        k1_scales = keep.tile([P, GROUPS * N1], U8, name="k1_scales", align_bytes=64)
        k2_raw, k2_wide, dist_sb, k1_sb, data_sb, wt_sb = {}, {}, {}, {}, {}, {}
        dist_grouped, dist_codes, dist_scales = {}, {}, {}
        planes, h_grouped, h_codes, h_scales, result, filled, wt_bank = {}, {}, {}, {}, {}, {}, {}
        negated, lower_result = {}, {}

        def load_k2(r, count):
            raw = keep.tile([P, count, J2], U8, name="k2_raw%d" % r)
            nc.sync.dma_start(out=raw[:], in_=k2_bytes[r * P : (r + count) * P, :].rearrange("(r p) l -> p r l", p=P))
            for e in range(count):
                k2_raw[r + e] = (raw, e)

        def load_scale():
            nc.sync.dma_start(out=scale4[:], in_=k2_scale.rearrange("o (p t) -> p (o t)", t=4))

        def load_pol():
            nc.sync.dma_start(out=pol_bf[:].rearrange("p (g t) -> p g t", t=4), in_=pol.rearrange("(g p t) -> p g t", p=P, t=4))

        def load_dist(g, h):
            dist_sb[g, h] = keep.tile([P, 2 * J2], BF16, name="dist_sb%d_%d" % (g, h))
            rows = dist[g * 512 : (g + 1) * 512, :].rearrange("(p t) l -> p (t l)", t=4)
            nc.sync.dma_start(out=dist_sb[g, h][:], in_=rows[:, h * 2 * J2 : (h + 1) * 2 * J2])

        def load_k1(i):
            k1_sb[i] = keep.tile([P, J1], BF16, name="k1_sb%d" % i)
            nc.sync.dma_start(out=k1_sb[i][:], in_=k1[i * P : (i + 1) * P, :])

        def load_data(b, h):
            data_sb[b, h] = keep.tile([P, UPPER, BANK], BF16, name="data_sb%d_%d" % (b, h))
            rows = data[h * 512 : (h + 1) * 512, b * BANK : (b + 1) * BANK]
            nc.sync.dma_start(out=data_sb[b, h][:], in_=rows.rearrange("(i p) m -> p i m", p=P))

        def load_wt(b):
            wt_sb[b] = keep.tile([P, BANK], BF16, name="wt_sb%d" % b)
            nc.sync.dma_start(out=wt_sb[b][:], in_=wt[b * BANK : (b + 1) * BANK].partition_broadcast(P))

        def store(n, lo, up):
            b, i = divmod(n, ROW_TILES)
            nc.sync.dma_start(out=out[i * P : (i + 1) * P, b * BANK + lo : b * BANK + up], in_=result[n, lo][:, 0 : up - lo])

        def store_strips(b, first, count, a, rows):
            m = slice(first * P, (first + count) * P)
            dst = out[(UPPER + a) * P : (UPPER + a + rows) * P, b * BANK + m.start : b * BANK + m.stop]
            nc.sync.dma_start(out=dst.rearrange("(i p) m -> p i m", p=P), in_=lower_result[b][:, a : a + rows, m])

        def new_bank(bank, shape, dtype):
            return psum.tile(shape, dtype, name="bank%d" % bank)

        def turn_words(name, runs, bank):
            filled[name] = new_bank(bank, [P, len(runs), 2, P], F32)
            for a, run in enumerate(runs):
                for u in (0, 1):
                    nc.tensor.transpose(filled[name][:, a, u, :], run.bitcast(F32)[:, u : 256 : 2], ident[:])

        def two_runs(rows):
            return [rows[:, 0:512], rows[:, 512:1024]]

        def turn_k2(r, count, bank):
            turn_words(("k2", r), [k2_wide[r + e] for e in range(count)], bank)
            for e in range(count):
                filled["k2 tile", r + e] = filled["k2", r][:, e]

        def turn_dist(g, h, bank):
            turn_words(("dist", g, h), two_runs(dist_sb[g, h]), bank)

        def turn_k1(i, bank):
            turn_words(("k1", i), two_runs(k1_sb[i]), bank)

        def mx(dst, lhs, lhs_columns, rhs, rhs_columns, start, stop):
            nc.tensor.matmul_mx(
                out=dst,
                lhsT=lhs[0][:, lhs_columns].bitcast(FP8X4),
                lhsT_scale=lhs[1][:, lhs_columns],
                rhs=rhs[0][:, rhs_columns].bitcast(FP8X4),
                rhs_scale=rhs[1][:, rhs_columns],
                start=start,
                stop=stop,
            )

        def span(first, count):
            return slice(first, first + count)

        def first_product(dst, g, t, m):
            mx(dst, (dist_codes[g], dist_scales[g]), span(t * P, P), (k2_codes, k2_scales), m, True, True)

        def g_quarter(b, g, q, bank):
            filled["quarter", b, g, q] = new_bank(bank, [P, 4, P], F32)
            for t in range(4):
                first_product(filled["quarter", b, g, q][:, t, :], g, t, span(b * BANK + q * P, P))

        def g_planes(b, g, lo, w, k, bank):
            count = BANK // w
            filled["planes", b, g, lo, k] = new_bank(bank, [P, count, w], F32)
            for e in range(count):
                first_product(filled["planes", b, g, lo, k][:, e, :], g, count * k + e, span(b * BANK + lo, w))

        def k1_columns(i, g):
            return span((GROUPS * i + g if i < UPPER else UPPER * (GROUPS + g) + i - UPPER) * P, P)

        def signal(n, lo, up, bank):
            b, i = divmod(n, ROW_TILES)
            filled["signal", n, lo] = new_bank(bank, [P, up - lo], F32)
            for g in range(GROUPS):
                mx(filled["signal", n, lo][:], (k1_codes, k1_scales), k1_columns(i, g), (h_codes[b], h_scales[b]), span(g * BANK + lo, up - lo), g == 0, g == GROUPS - 1)

        def turned_pass(b, c, g):
            rows = span(k1_columns(UPPER, g).start, BANK)
            mx(filled["turned", b, c][:], (h_codes[b], h_scales[b]), span(g * BANK + c * P, P), (k1_codes, k1_scales), rows, g == 0, g == GROUPS - 1)

        def open_turned(b, c, bank):
            filled["turned", b, c] = new_bank(bank, [P, BANK], F32)
            turned_pass(b, c, 0)

        def close_turned(b, c):
            turned_pass(b, c, 1)

        def lay_data(b, c, bank):
            filled["strip", b, c] = new_bank(bank, [P, UPPER, P], F32)
            nc.tensor.matmul(filled["strip", b, c][:], lhsT=ident_bf[:], rhs=data_sb[b, 1][:, :, span(c * P, P)], start=True, stop=False)

        def turn_back(b, c):
            for a in range(UPPER):
                nc.tensor.matmul(
                    filled["strip", b, c][:, a, :], lhsT=negated[b, c][:, span(a * P, P)], rhs=ident[:], is_transpose=True, start=False, stop=a == UPPER - 1
                )

        def spread_wt(blocks, bank):
            both = new_bank(bank, [P, 2, BANK], BF16)
            for e, b in enumerate(blocks):
                wt_bank[b] = both[:, e, :]
                nc.tensor.matmul(wt_bank[b], lhsT=ident_bf[:], rhs=wt_sb[b][:], start=True, stop=True)

        def warm_up(count, k, bank):
            idle = new_bank(bank, [P, P], F32)
            for r in range(count):
                nc.tensor.matmul(idle[:], lhsT=ident[:], rhs=ident[:], start=True, stop=True)

        def flat(grouped):
            return grouped.rearrange("p a n t -> p (a n t)")

        def spent(r):
            return {
                8: lambda: dist_grouped[0][:, 0:2],
                10: lambda: dist_grouped[1][:, 0:2],
                12: lambda: dist_grouped[1][:, 2:4],
                14: lambda: k2_grouped[:, 4:6],
            }[r]()

        def widen(r, count, copy):
            wide = flat(spent(r)) if r in reuse else keep.tile([P, count * J2], BF16, name="wide%d" % r)[:]
            raw, e = k2_raw[r]
            copy(out=wide, in_=raw[:, e : e + count].rearrange("p r l -> p (r l)").bitcast(FP8))
            for e in range(count):
                k2_wide[r + e] = wide[:, e * J2 : (e + 1) * J2]

        def widen_vector(r, count):
            widen(r, count, nc.vector.tensor_copy)

        def widen_gpsimd(r, count):
            widen(r, count, nc.gpsimd.tensor_copy)

        def widen_scalar(r, count):
            widen(r, count, nc.scalar.copy)

        def scale_k2(r):
            words = filled["k2 tile", r].rearrange("p u n -> p (u n)")
            nc.vector.tensor_tensor(
                out=k2_grouped[:, r].rearrange("p n (u e) -> p n u e", u=2),
                in0=words.bitcast(BF16).rearrange("p (u n e) -> p n u e", u=2, e=2),
                in1=scale4[:].rearrange("p (o u e) -> p o u e", o=1, u=2).to_broadcast([P, P, 2, 2]),
                op=MULT,
            )

        def group_words(name, runs):
            dst = runs.bitcast(F32).rearrange("p a (n u) -> p a n u", u=2)
            nc.scalar.copy(out=dst, in_=filled[name][:].rearrange("p a u n -> p a n u"))

        def group_dist(g, h):
            if h == 0:
                dist_grouped[g] = keep.tile([P, 4, P, 4], BF16, name="dist_grouped%d" % g, align_bytes=64)
            group_words(("dist", g, h), dist_grouped[g][:, 2 * h : 2 * h + 2].rearrange("p a n t -> p a (n t)"))

        def group_k1(i):
            group_words(("k1", i), k1_upper[:, i] if i < UPPER else k1_lower[:, :, i - UPPER])

        def pol_to_f32():
            nc.scalar.activation(out=pol4[:], in_=pol_bf[:], func=COPY)

        def ident_to_bf16():
            nc.scalar.copy(out=ident_bf[:], in_=ident[:])

        def h_columns(b, g, lo, up):
            if b not in h_grouped:
                h_grouped[b] = turn.tile([P, GROUPS * BANK, 4], BF16, name="h_grouped", align_bytes=64, bufs=H_BUFS)
            return h_grouped[b][:, g * BANK + lo : g * BANK + up, :]

        def h_quarter(b, g, q):
            nc.vector.tensor_tensor(
                out=h_columns(b, g, q * P, (q + 1) * P),
                in0=filled["quarter", b, g, q][:].rearrange("p t n -> p n t"),
                in1=pol4[:, 4 * g : 4 * g + 4].rearrange("p (o t) -> p o t", o=1).to_broadcast([P, P, 4]),
                op=MULT,
            )

        def h_planes(b, g, lo, w, k):
            count = BANK // w
            if k == 0:
                planes[b, g, lo] = turn.tile([P, 4, BANK], BF16, name="planes", align_bytes=64, bufs=PLANE_BUFS)
            for e in range(count):
                t = count * k + e
                dst = planes[b, g, lo][:, t, 0:w]
                nc.scalar.activation(out=dst, in_=filled["planes", b, g, lo, k][:, e, :], func=COPY, scale=pol4[:, 4 * g + t : 4 * g + t + 1])

        def group_planes(b, g, lo, h, copy):
            dst = h_columns(b, g, lo + h * HALF, lo + (h + 1) * HALF).rearrange("p (c i) t -> p c t i", i=4)
            copy(out=dst, in_=planes[b, g, lo][:, :, span(h * HALF, HALF)].rearrange("p t (c i) -> p c t i", i=4))

        def group_scalar(b, g, lo, h):
            group_planes(b, g, lo, h, nc.scalar.copy)

        def group_gpsimd(b, g, lo, h):
            group_planes(b, g, lo, h, nc.gpsimd.tensor_copy)

        def negate(b, c):
            negated[b, c] = turn.tile([P, BANK], F32, name="negated", bufs=STRIP_BUFS)
            nc.scalar.activation(out=negated[b, c][:], in_=filled["turned", b, c][:], func=COPY, scale=-1.0)

        def quantise(codes, scales, grouped):
            nc.vector.quantize_mx(out=codes.bitcast(FP8X4), scales=scales, in_=grouped)

        def q_k2(c, count):
            m = span(c * CHUNK, count * CHUNK)
            quantise(k2_codes[:, m], k2_scales[:, m], flat(k2_grouped[:, 2 * c : 2 * (c + count)]))

        def q_dist(g):
            dist_codes[g] = keep.tile([P, 512], U32, name="dist_codes%d" % g, align_bytes=64)
            dist_scales[g] = keep.tile([P, 512], U8, name="dist_scales%d" % g, align_bytes=64)
            quantise(dist_codes[g][:], dist_scales[g][:], flat(dist_grouped[g][:]))

        def q_k1(i, count):
            c = span(i * GROUPS * P, count * GROUPS * P)
            grouped = k1_upper[:, i : i + count] if i < UPPER else k1_lower[:]
            quantise(k1_codes[:, c], k1_scales[:, c], grouped.rearrange("p a b x -> p (a b x)"))

        def q_h(b):
            h_codes[b] = turn.tile([P, GROUPS * BANK], U32, name="h_codes", align_bytes=64, bufs=H_BUFS)
            h_scales[b] = turn.tile([P, GROUPS * BANK], U8, name="h_scales", align_bytes=64, bufs=H_BUFS)
            quantise(h_codes[b][:], h_scales[b][:], h_grouped[b][:].rearrange("p n t -> p (n t)"))

        def subtract(n, lo, up):
            b, i = divmod(n, ROW_TILES)
            whole = [s for s in tensor if s[0] is signal and s[1] == n and s[2] <= lo < s[3]][0]
            result[n, lo] = results.tile([P, BANK], F32, name="result")
            sums = filled["signal", n, whole[2]][:, lo - whole[2] : up - whole[2]]
            nc.vector.tensor_tensor(out=result[n, lo][:, 0 : up - lo], in0=sums, in1=data_sb[b, i // UPPER][:, i % UPPER, lo:up], op=SUB)

        def part_of_result(n, lo, up):
            first = max(s[2] for s in vector if s[0] is subtract and s[1] == n and s[2] <= lo)
            result[n, lo] = result[n, first][:, lo - first :]
            return result[n, lo][:, 0 : up - lo]

        def weigh_vector(n, lo, up):
            part = part_of_result(n, lo, up)
            nc.vector.tensor_tensor(out=part, in0=part, in1=wt_bank[n // ROW_TILES][:, lo:up], op=MULT)

        def weigh_gpsimd(n, lo, up):
            part = part_of_result(n, lo, up)
            nc.gpsimd.tensor_tensor(out=part, in0=part, in1=wt_sb[n // ROW_TILES][:, lo:up], op=MULT)

        def weigh_strip(b, c):
            if b not in lower_result:
                lower_result[b] = keep.tile([P, UPPER, BANK], F32, name="lower_result%d" % b)
            m = span(c * P, P)
            nc.vector.scalar_tensor_tensor(
                out=lower_result[b][:, :, m],
                in0=filled["strip", b, c][:],
                scalar=-1.0,
                in1=wt_sb[b][:, m].rearrange("p (o m) -> p o m", o=1).to_broadcast([P, UPPER, P]),
                op0=MULT,
                op1=MULT,
            )

        def steps(f, *heads, count, first=0):
            return [(f,) + heads + (k,) for k in range(first, first + count)]

        def tiles(f, *numbers):
            return [(f, n, 0, BANK) for n in numbers]

        def halves(f, n):
            return [(f, n, 0, HALF), (f, n, HALF, BANK)]

        def scale_chunk(c):
            return steps(scale_k2, count=2, first=2 * c)

        def quarters(f, b, g):
            return steps(f, b, g, count=4)

        def plane_set(f, b, g, w=BANK):
            return steps(f, b, g, 0, w, count=4 * w // BANK)

        def regroup(b, g, w=BANK, f=group_scalar):
            return steps(f, b, g, 0, count=w // HALF)

        def q_block(b):
            return [(q_h, b)]

        def weave(first, second):
            order = [s for pair in zip(first, second) for s in pair]
            return order + first[len(second) :] + second[len(first) :]

        sub, wv, wg, sig = subtract, weigh_vector, weigh_gpsimd, signal

        def right(f, *numbers):
            return [(f, n, HALF, BANK) for n in numbers]

        def scales(*numbers):
            return [(scale_k2, r) for r in numbers]

        q01, q11 = quarters(h_quarter, 0, 1), quarters(h_quarter, 1, 1)
        g01, g11 = quarters(g_quarter, 0, 1), quarters(g_quarter, 1, 1)
        p00, p10, p20, p21, p30, p31 = [plane_set(g_planes, b, g) for b, g in ((0, 0), (1, 0), (2, 0), (2, 1), (3, 0), (3, 1))]
        e00, e10, e20, e21, e30, e31 = [plane_set(h_planes, b, g) for b, g in ((0, 0), (1, 0), (2, 0), (2, 1), (3, 0), (3, 1))]
        turned = [[(open_turned, b, c), (close_turned, b, c)] for b in (2, 3) for c in range(4)]

        reuse = {8: (q_dist, 0), 10: (q_dist, 1), 12: (q_dist, 1), 14: (q_k2, 2, 2)}
        vector = [(widen_vector, 0, 1), (widen_vector, 1, 1)] + scales(0, 1, 2, 3)
        vector += [(q_k2, 0, 1), (q_k2, 1, 1), (q_dist, 0)] + scales(4, 5, 6) + [(q_dist, 1)] + scales(7, 8, 9)
        vector += q01[:3] + [(q_k2, 2, 2)] + q01[3:] + scales(10, 11) + [(q_k1, 0, 2)] + q_block(0) + [(q_k1, 2, 2), (q_k2, 4, 2)]
        vector += tiles(sub, 0) + q11[:1] + tiles(sub, 1) + q11[1:] + tiles(sub, 2) + [(q_k1, 4, 4)]

        f2 = steps(weigh_strip, 2, count=4)
        vector += scales(12, 13) + tiles(sub, 3) + q_block(1) + tiles(sub, 4) + scales(14, 15) + tiles(sub, 5, 6) + [(q_k2, 6, 2)]
        vector += tiles(sub, 7, 8, 9) + tiles(wv, 8) + tiles(sub, 10) + q_block(2)
        vector += tiles(sub, 11) + tiles(wv, 9) + tiles(sub, 12, 13) + tiles(wv, 11) + tiles(sub, 14, 15) + tiles(wv, 13) + tiles(sub, 16, 17)
        vector += tiles(wv, 15) + tiles(sub, 18) + f2[:2] + tiles(sub, 19) + q_block(3)
        vector += f2[2:] + tiles(sub, 24, 25, 26) + tiles(wv, 24) + tiles(sub, 27) + tiles(wv, 26) + tiles(sub, 28, 29) + tiles(wv, 28) + tiles(sub, 30)
        vector += halves(sub, 31) + halves(wv, 30)[1:] + halves(wv, 31)

        scalar = [(widen_scalar, 2, 1), (ident_to_bf16,)] + steps(group_dist, 0, count=2) + [(pol_to_f32,), (widen_scalar, 7, 1)] + steps(group_dist, 1, count=2)
        scalar += e00 + [(group_k1, 0)] + regroup(0, 0) + steps(group_k1, count=3, first=1)
        scalar += e10 + steps(group_k1, count=2, first=4) + regroup(1, 0)[:1] + steps(group_k1, count=2, first=6) + regroup(1, 0)[1:]

        n2, n3 = steps(negate, 2, count=4), steps(negate, 3, count=2)
        scalar += e20 + e21[:1] + regroup(2, 0)[:1] + e21[1:] + regroup(2, 0)[1:] + regroup(2, 1)
        scalar += e30 + e31[:1] + regroup(3, 0)[:1] + e31[1:] + regroup(3, 0)[1:] + n2[:2] + regroup(3, 1) + n2[2:]

        gpsimd = [(widen_gpsimd, 3, 1), (widen_gpsimd, 4, 2), (widen_gpsimd, 6, 1)]
        gpsimd += [(widen_gpsimd, r, 2) for r in range(8, 2 * CHUNKS, 2)]

        gpsimd += tiles(wg, 0, 1, 2, 3, 4, 6, 5, 10, 7, 12, 14, 16, 17, 19, 18, 25, 27, 29) + halves(wg, 30)[:1]

        tensor = [(warm_up, 3, 0), (turn_k2, 0, 1), (turn_k2, 1, 1), (warm_up, 1, 1), (turn_k2, 2, 2)] + steps(turn_dist, 0, count=2)
        tensor += [(warm_up, 1, 2), (turn_k2, 4, 2)] + steps(turn_dist, 1, count=2) + [(turn_k2, 6, 2)]
        tensor += p00 + [(turn_k2, 8, 2), (turn_k1, 0)] + g01[:3] + [(turn_k1, 1), (turn_k2, 10, 2)] + g01[3:] + [(turn_k1, 2), (turn_k1, 3)] + p10[:2] + g11[:1] + p10[2:] + g11[1:2]
        tensor += [(turn_k1, 4), (turn_k1, 5)] + tiles(sig, 0, 1) + [(turn_k1, 6), (turn_k1, 7)] + g11[2:]

        lay2, back2, lay3, back3 = steps(lay_data, 2, count=4), steps(turn_back, 2, count=4), steps(lay_data, 3, count=2), steps(turn_back, 3, count=2)
        tensor += p20[:1] + tiles(sig, 2) + p20[1:3] + [(turn_k2, 12, 2)] + p20[3:] + tiles(sig, 3) + p21[:1] + [(turn_k2, 14, 2)] + tiles(sig, 4) + p21[1:] + tiles(sig, 5, 6, 7)
        tensor += [(spread_wt, (1, 3))] + tiles(sig, 8, 9) + p30[:1] + tiles(sig, 10) + p30[1:3] + tiles(sig, 11) + p30[3:] + tiles(sig, 12) + p31[:1] + tiles(sig, 13, 14)
        tensor += p31[1:3] + tiles(sig, 15) + p31[3:] + tiles(sig, 16, 17) + turned[0] + turned[1] + tiles(sig, 18) + lay2[:2] + back2[:2]
        tensor += tiles(sig, 19) + turned[2] + turned[3] + lay2[2:] + back2[2:]
        tensor += tiles(sig, 24, 25, 26, 27, 28, 29, 30, 31)
        borrowing = []

        spread_for = {s: [t for t in tensor if t[0] is spread_wt and s[1] // ROW_TILES in t[1]][0] for s in vector if s[0] is weigh_vector}

        sync = [(load_k2, 0, 1), (load_k2, 1, 1), (load_k2, 2, 2), (load_scale,), (load_dist, 0, 0), (load_k2, 4, 2), (load_dist, 0, 1)]
        sync += [(load_k2, 6, 2), (load_pol,)] + steps(load_dist, 1, count=2) + [(load_k2, 8, 2), (load_k2, 10, 2)]
        sync += steps(load_k1, count=2) + [(load_k2, 12, 2), (load_k2, 14, 2)] + steps(load_k1, count=6, first=2)
        sync += [(load_data, 0, 0), (load_wt, 0), (load_data, 0, 1)]
        for b in range(1, BLOCKS):
            sync += [(load_wt, b)] + steps(load_data, b, count=2)

        sync += tiles(store, 0, 1, 2, 3, 4, 6, 8, 5, 9, 10, 7, 11, 12, 13, 14, 15, 16) + [(store_strips, 2, 0, 2, 0, 4)] + tiles(store, 17) + [(store_strips, 2, 2, 2, 0, 4)]
        sync += tiles(store, 19, 18, 24, 25, 26, 27, 28, 29) + halves(store, 30)[::-1] + halves(store, 31)

        every = vector + scalar + gpsimd
        maker = {group_dist: turn_dist, group_k1: turn_k1, h_quarter: g_quarter, h_planes: g_planes, negate: open_turned, weigh_strip: lay_data}

        def all_of(among, *functions):
            return [s for s in among if s[0] in functions]

        def covering(among, k):
            return [s for s in among if s[1] <= k < s[1] + s[2]]

        def over(among, n, lo):
            return [s for s in among if s[1] == n and s[2] <= lo < s[3]]

        def made_by(step):
            f, a = step[0], step[1:]
            if f is scale_k2:
                return covering(all_of(tensor, turn_k2), a[0])[0]
            if f is subtract:
                return over(all_of(tensor, signal), a[0], a[1])[0]
            if f is weigh_vector:
                return spread_for[step]
            return (maker[f],) + a

        readers = {}
        for step in every:
            if step[0] in maker or step[0] in (scale_k2, subtract, weigh_vector):
                readers.setdefault(made_by(step), []).append(step)
        widenings = all_of(every, widen_vector, widen_scalar, widen_gpsimd)
        groupings = all_of(every, group_scalar, group_gpsimd)
        plane_sets = [s[1:4] for s in all_of(scalar, h_planes) if s[5] == 0]
        subtractions = all_of(vector, subtract)
        negations = all_of(scalar, negate)

        def readers_of_h(b):
            return [s for s in all_of(tensor, signal) if s[1] // ROW_TILES == b] + [s for s in all_of(tensor, open_turned, close_turned) if s[1] == b]

        def needs(step):
            f, a = step[0], step[1:]
            if step in widenings:
                return covering(all_of(sync, load_k2), a[0]) + ([reuse[a[0]]] if a[0] in reuse else [])
            if f is turn_k2:
                return [s for r in range(a[0], a[0] + a[1]) for s in covering(widenings, r)]
            if f is turn_dist:
                return [(load_dist,) + a]
            if f is turn_k1:
                return [(load_k1,) + a]
            if f in (g_quarter, g_planes):
                lo, w = (a[2] * P, P) if f is g_quarter else a[2:4]
                first, last = (a[0] * BANK + lo) // CHUNK, (a[0] * BANK + lo + w - 1) // CHUNK
                return covering(all_of(vector, q_k2), first) + covering(all_of(vector, q_k2), last) + [(q_dist, a[1])]
            if f is signal:
                b, i = divmod(a[0], ROW_TILES)
                return q_block(b) + covering(all_of(vector, q_k1), i)
            if f is open_turned:
                return [(q_h, a[0])] + covering(all_of(vector, q_k1), UPPER)
            if f is close_turned:
                return [(open_turned,) + a]
            if f is lay_data:
                return [(ident_to_bf16,), (load_data, a[0], 1)]
            if f is turn_back:
                return [(lay_data,) + a, (negate,) + a]
            if f is spread_wt:
                return [(ident_to_bf16,)] + [(load_wt, b) for b in a[0]]
            h_free = []
            if (f is h_quarter or step in groupings) and a[0] >= H_BUFS:
                before = (q_h, a[0] - H_BUFS)
                h_free = [before] + [covering(all_of(tensor, turn_k2), r)[0] for r in reuse if reuse[r] == before]
            if f is h_quarter:
                return [made_by(step), (pol_to_f32,)] + h_free
            if f is h_planes:
                k = plane_sets.index(a[:3]) - PLANE_BUFS
                return [made_by(step), (pol_to_f32,)] + [s for s in groupings if k >= 0 and s[1:4] == plane_sets[k]]
            if step in groupings:
                return [s for s in all_of(scalar, h_planes) if s[1:4] == a[:3]] + h_free
            if f is subtract:
                b, i = divmod(a[0], ROW_TILES)
                k = subtractions.index(step) - RESULT_BUFS
                earlier = [s for s in all_of(sync, store) if k >= 0 and subtractions[k] in over(subtractions, s[1], s[2])]
                return [made_by(step), (load_data, b, i // UPPER)] + earlier
            if f is negate:
                k = negations.index(step) - STRIP_BUFS
                return [(close_turned,) + a] + ([(turn_back,) + negations[k][1:]] if k >= 0 else [])
            if f is weigh_strip:
                return [(turn_back,) + a, (load_wt, a[0])]
            if f is scale_k2:
                return [made_by(step), (load_scale,)]
            if f in maker:
                return [made_by(step)]
            if f is pol_to_f32:
                return [(load_pol,)]
            if f is q_k2:
                return steps(scale_k2, count=2 * a[1], first=2 * a[0])
            if f is q_dist:
                return steps(group_dist, a[0], count=2)
            if f is q_k1:
                return steps(group_k1, count=a[1], first=a[0])
            if f is q_h:
                writers = [s for s in groupings + all_of(vector, h_quarter) if s[1] == a[0]]
                return writers + (readers_of_h(a[0] - H_BUFS) if a[0] >= H_BUFS else [])
            if f is weigh_vector:
                return over(subtractions, a[0], a[1]) + [made_by(step)]
            if f is weigh_gpsimd:
                return over(subtractions, a[0], a[1]) + [(load_wt, a[0] // ROW_TILES)]
            if f is store:
                return over(all_of(every, weigh_vector, weigh_gpsimd), a[0], a[1])
            if f is store_strips:
                return steps(weigh_strip, a[0], count=a[2], first=a[1])
            return []

        vector_banks, scalar_banks, bank_of, held_by = list(VECTOR_BANKS), list(SCALAR_BANKS), {}, {}

        def emptied(bank):
            mine = vector if bank in VECTOR_BANKS else scalar
            return max([-1] + [mine.index(s) if s in mine else len(mine) for s in readers.get(held_by.get(bank), [])])

        for step in tensor:
            if step[0] in (warm_up, spread_wt):
                bank_of[step] = SCALAR_BANKS[-1]
                if step[0] is spread_wt and bank_of[step] in scalar_banks:
                    scalar_banks.remove(bank_of[step])
            elif step[0] not in (turn_back, close_turned):
                for_vector = step[0] in (turn_k2, g_quarter, signal, lay_data)
                bank_of[step] = min(vector_banks if for_vector != (step in borrowing) else scalar_banks, key=emptied)
                held_by[bank_of[step]] = step

        written, last_fill = set(), {}

        def ready(step):
            freed = readers.get(last_fill.get(bank_of.get(step)), [])
            return all(s in written for s in needs(step) + freed)

        def write(step):
            if step in bank_of:
                last_fill[bank_of[step]] = step
                step[0](*step[1:], bank_of[step])
            else:
                step[0](*step[1:])
            written.add(step)

        make_identity(nc, ident[:])
        waiting = [list(sync), list(tensor), list(vector), list(scalar), list(gpsimd)]
        while any(waiting):
            left = sum(map(len, waiting))
            for queue in waiting:
                while queue and ready(queue[0]):
                    write(queue.pop(0))
            assert sum(map(len, waiting)) < left
